import numpy as np, ml_dtypes
CORES = [6,15,38,47]
N = 4
BF = ml_dtypes.bfloat16
def gentries(a):
    return np.ascontiguousarray(a.reshape(8, 16, -1).transpose(0, 2, 1)).reshape(8, -1)
def gtable(e):
    e = np.asarray(e); return np.ascontiguousarray(e.reshape(8, -1, 16).transpose(0, 2, 1)).reshape(128, -1).astype(np.int32)
P, H, S, ST, RO, CAP = 4096, 1536, 256, 3, 3, 64
def parts(rng):
    x = rng.integers(0, 256, (N, 8, 16, P)); l = rng.integers(0, P, (N, 8, 16, H)); w = rng.integers(0, H, (N, 8, P))
    hs = np.ascontiguousarray(np.argsort(rng.random((N, 8, RO, H)), axis=-1)[..., :S])
    a = rng.choice(np.array([0.5, 0.7, 0.9, 1.1]), (N, 8, 1, RO, 1)) + 0.4 * (rng.random((N, 8, 1, RO, S)) - 0.5)
    d = np.minimum((256 * rng.random((N, 8, 16, RO, S)) ** a).astype(np.int64), 255)
    return x, l, w, hs, d
def lanes(rng, l, w, hs):
    K = (P - 2) // ((ST + 1) * S); steps = np.zeros((N, 8, ST + 1, S, K), np.int64)
    for q in range(N):
        for g in range(8):
            o = (4 + rng.permutation(H - 8)[:(ST + 1) * S]).reshape(ST + 1, S)
            c = (1 + rng.permutation(P - 2)[:(ST + 1) * S * K]).reshape(ST + 1, S, K)
            u = rng.integers(0, K, (16, ST + 1, S))
            l[q, g][:, o] = c[np.arange(ST + 1)[:, None], np.arange(S), u]
            w[q, g][c[:ST]] = o[1:, :, None]
            hs[q, g, 0] = o[0]; steps[q, g] = c
    return steps
def levels(rng):
    x = rng.integers(0, 100, (N, 8, 16, P)); x[1::2] += 150
    x[:, 4:] = rng.integers(0, 30, (N, 4, 16, P)); x[1::2, 4:] += 225
    return x
def pack(x, l, w, hs, d):
    return {"xs": x.reshape(N, 128, P).astype(np.float32).astype(BF), "hl": np.ascontiguousarray(l.reshape(N, 128, H)).astype(np.int32), "wr": np.ascontiguousarray(w).astype(np.int32),
            "ho": np.stack([gtable(a.reshape(8, -1)) for a in hs]), "dm": d.reshape(N, 128, RO * S).astype(np.float32).astype(BF)}
def setup_inputs(rng):
    return pack(*parts(rng))
def setup_inputs_room(rng):
    x, l, w, hs, d = parts(rng); x = levels(rng); c = lanes(rng, l, w, hs)
    for q in range(N):
        for g in range(8):
            n = int(rng.choice(np.array([0, 1, CAP - 1, CAP, CAP + 1, S])))
            if q == 0: n = (CAP, CAP + 1, S, CAP - 1, 1, 0, CAP, CAP + 1)[g]
            v = d[q, g, :, 0]; v[:] = 0
            v[:, rng.permutation(S)[:n]] = rng.integers(100, 150, (16, n)) if q % 2 == 0 else 255
            if q == 2 and g < 4:
                i = 1 + rng.permutation(S) % ST; v[:] = rng.integers(100, 150, (16, S))
                x[q, g][:, c[q, g][i, np.arange(S)]] += 150
    return pack(x, l, w, hs, d)
def setup_inputs_trade(rng):
    x, l, w, hs, d = parts(rng); x = levels(rng); c = lanes(rng, l, w, hs); ends = np.array([0, 1, 2, 3, H - 4, H - 3, H - 2, H - 1])
    for q in range(N):
        for g in range(8):
            last = c[q, g, ST]; w[q, g][last] = rng.choice(ends, last.shape)
            m = rng.random(S) < 0.5; m[:3] = True
            if q % 2 == 1 and g >= 6: m[CAP // 2:] = False
            d[q, g, :, 0] = np.where(m, rng.integers(100, 150, (16, S)) if q % 2 == 0 else 255, 0)
            if g >= 4: w[q, g][last[:3]] = np.array([1, H - 1, 0])[:, None]
            if q % 2 == 1:
                own = l[q, g][0, hs[q, g, 0]][m]
                l[q, g][:, ends] = rng.permutation(np.concatenate([rng.choice(own, 64), rng.integers(0, P, 64)])).reshape(16, 8)
                if g >= 4:
                    l[q, g][:, np.array([1, H - 1, 0])] = np.array([own[0], P - 1, 0])
                    hs[q, g, 1] = hs[q, g, 0]
                    d[q, g, :, 1] = np.where(m, 255, 0) if q % 4 == 1 else 0
                    if q % 4 == 3: x[q, g][:, own[0]] = 255
    return pack(x, l, w, hs, d)
def setup_inputs_ties(rng):
    x, l, w, hs, d = parts(rng); pal = rng.integers(0, 255, (N, 8, 16, 7))
    x = np.take_along_axis(pal, rng.integers(0, 7, (N, 8, 1, P)), 3)
    for t in range(RO):
        e = np.take_along_axis(l[:, :, t], hs[:, :, t], 2); v = np.take_along_axis(x, e[:, :, None, :], 3)
        o = np.argsort(rng.random((N, 8, 16, S)), axis=2)
        d[:, :, :, t] = v + (o >= rng.integers(8, 11, (N, 8, 1, S)))
    if RO > 2:
        q = int(rng.integers(0, N)); d[q, :, :, :2] = 255; d[q, 0, :, 0, 0] = 0
        w[q, 0, l[q, 0, 0, hs[q, 0, 0, 0]]] = np.setdiff1d(np.arange(H), hs[q, 0, 0])[0]
    return pack(x, l, w, hs, d)
def setup_inputs_alike(rng):
    x, l, w, hs, d = parts(rng)
    w[:, 0] = rng.choice(rng.permutation(H)[:40], (N, P))
    l[:, 2] = rng.choice(np.concatenate([np.array([0, P - 1]), 1 + rng.permutation(P - 2)[:60]]), (N, 16, H))
    x[:, 3] = rng.integers(0, 16, (N, 16, P)); v = rng.integers(0, 256, x[1::2, 3].shape)
    x[1::2, 3] = np.where(np.argsort(rng.random(v.shape), axis=1) < 12, 255, v); d[::2, 3, :, 0] = 0
    w[:, 4] = np.take_along_axis(hs[:, 4, 0], rng.integers(0, S, (N, P)), 1)
    x[:, 5] = rng.choice(np.array([0, 1, 254, 255]), (N, 16, P))
    for q in range(N):
        e = l[q, 6][0, hs[q, 6, 0]]
        l[q, 6][rng.integers(1, 16, S), w[q, 6][e]] = e
    w[:, 7, ::2] = rng.choice(np.array([0, H - 1]), (N, (P + 1) // 2))
    return pack(x, l, w, hs, d)
def setup_inputs_spread(rng):
    x, l, w, hs, d = parts(rng)
    x = np.minimum(np.exp2(8 * rng.random((N, 8, 1, P))) * (0.25 + 1.5 * rng.random((N, 8, 16, P))), 255).astype(np.int64)
    d = np.minimum(np.exp2(8 * rng.random((N, 8, 1, RO, S))) * (0.25 + 1.5 * rng.random((N, 8, 16, RO, S))), 255).astype(np.int64)
    w = np.minimum((H * rng.random((N, 8, P)) ** 2).astype(np.int64), H - 1)
    q = rng.permutation(N); d[q[0]] = 0; d[q[1]] = 255
    return pack(x, l, w, hs, d)
def check_inputs(d):
    bad = []
    for k in ("xs", "dm"):
        v = np.asarray(d[k]).astype(np.float32)
        if not np.all((v >= 0) & (v <= 255) & (v == np.floor(v))): bad.append("whole numbers of " + k)
    for k, hi in (("hl", P - 1), ("wr", H - 1), ("ho", H - 1)):
        if np.min(d[k]) < 0 or np.max(d[k]) > hi: bad.append("range of " + k)
    e = np.sort(np.stack([gentries(a) for a in d["ho"]]).reshape(N, 8, RO, S), axis=-1)
    if np.any(e[..., 1:] == e[..., :-1]): bad.append("different holders of a round in ho")
    return bad
def nearest(x, lc, x0):
    dist = np.add.reduce(np.abs(x[:, lc] - x0[:, None, :]), axis=0)
    j = np.argmin(dist, axis=0)
    return j, lc[j, np.arange(lc.shape[1])]
def lowest(key, on, size):
    k = np.arange(key.shape[0]); first = np.full(size, key.shape[0]); np.minimum.at(first, key[on], k[on])
    return on & (first[key] == k)
def climb(x, l, w, h0, d, t, need):
    k = np.arange(S); e0 = l[t, h0]; x0 = x[:, e0]
    vouched = np.zeros(H, bool); vouched[h0] = True
    hv, jv, ev = [h0], [np.full(S, t)], [e0]
    up = np.ones(S, bool); m = np.zeros(S, np.int64); h = w[e0]
    for i in range(1, ST + 1):
        up = lowest(h, up, H) & ~vouched[h]
        vouched[h[up]] = True
        j, e = nearest(x, l[:, h], x0)
        able = up & (np.add.reduce((x[:, e] >= d).astype(np.int64), axis=0) >= need)
        m[able] = i; up = up & ~able
        hv.append(h); jv.append(j); ev.append(e); h = w[e]
    for i in range(ST + 1):
        c = (m > 0) & (m >= i)
        v = np.where(m > i, ev[min(i + 1, ST)], e0)
        l[jv[i][c], hv[i][c]] = v[c]
        if i > 0: w[ev[i][m > i]] = hv[i][m > i]
    c = m > 0
    w[e0[c]] = np.stack(hv)[m, k][c]
    u = np.flatnonzero(up)[:CAP]
    return int(np.count_nonzero(c)), (e0[u], x0[:, u], d[:, u], h[u])
def reference(xs, hl, wr, ho, dm):
    x = xs.astype(np.float32).astype(np.int64).reshape(N, 8, 16, P); l = hl.astype(np.int64).reshape(N, 8, 16, H); w = wr.astype(np.int64)
    hs = np.stack([gentries(a) for a in ho]).astype(np.int64).reshape(N, 8, RO, S); d = dm.astype(np.float32).astype(np.int64).reshape(N, 8, 16, RO, S)
    odd = [0] * N
    for t in range(RO):
        paid = [0] * N; sent = {}
        for a in range(N):
            for g in range(8):
                n, sent[a, g] = climb(x[a, g], l[a, g], w[a, g], hs[a, g, t], d[a, g, :, t], t, 9 + odd[a])
                paid[a] += n
        swaps = []
        for a in range(N):
            b = (a + 1 + t % (N - 1)) % N
            for g in range(8):
                e0, x0, dd, h = sent[a, g]
                j, e1 = nearest(x[b, g], l[b, g][:, h], x0)
                able = np.add.reduce((x[b, g][:, e1] >= dd).astype(np.int64), axis=0) >= 9 + odd[b]
                ok = lowest(e1, able & ~np.isin(e1, sent[b, g][0]), P)
                swaps.append((a, b, g, e0[ok], e1[ok]))
        for a, b, g, e0, e1 in swaps:
            va, vb = x[a, g][:, e0], x[b, g][:, e1]
            x[a, g][:, e0] = vb; x[b, g][:, e1] = va
        odd = [n & 1 for n in paid]
    return {"yx": x.reshape(N, 128, P).astype(np.float32).astype(BF), "yl": l.reshape(N, 128, H).astype(np.float32), "yw": w.astype(np.float32)}

@@ -1,0 +1,579 @@
+from concourse.mybir import AluOpType as A, AxisListType, ActivationFunctionType as F
+
+P, H, S, RO, CAP = 4096, 1536, 256, 3, 64
+F32, BF, F16, I32, U16 = "float32", "bfloat16", "float16", "int32", "uint16"
+SB = {
+    "X": (P + 64, BF), "HLi": (H, I32), "HL": (H + 1024, F32), "WT": (P + 768, F32), "wi": (256, I32), "w16": (256, F16),
+    "hoi": (48, I32), "hou": (48, U16), "hop": (48, F32), "DM": (816, BF), "VT": (H + 256, F32), "IO2": (8192, F32),
+    "ONE": (128, F32), "IDf": (128, F32), "BLf": (128, F32), "BLt": (128, F32), "I8": (128, BF), "I8n": (128, BF), "I16": (128, F16),
+    "BL16": (128, F16), "BL4": (128, BF), "POW": (128, BF), "ONEb": (128, BF), "G2": (8, BF), "Gm": (8, BF),
+    "Z": (144, F16), "Zb": (144, BF), "LT": (2048, BF), "THR": (256, F32), "THH": (256, F32), "TN": (256, F32), "THb": (256, BF),
+    "RST": (128, F32), "pi": (2, I32), "q16": (16, F32), "M16": (16, F32),
+    "tm16": (16, F32), "col": (8, F32), "lasti": (8, I32), "last": (8, U16), "SW": (64, F32), "DL1": (64, F32), "DW1": (48, F32),
+    "DX1": (4, F32), "KH": (4, F32), "CODE": (256, F32), "need": (4, F32), "ni": (2, I32),
+    "Aa": (2048, BF), "Ab": (2048, BF), "Ma": (2048, BF), "Mb": (2048, BF), "ma": (256, F32), "mb": (256, F32),
+    "Ua": (390, BF), "Ub": (390, BF), "VV": (768, F32), "hq": (64, F32), "eq": (64, F32),
+    "LSu": (256, U16), "LS16": (256, F16), "C": (256, F16), "C0": (256, F16),
+    "JB": (2048, F16), "X0": (272, BF), "H4": (264, F32), "LSF": (1032, F32), "PR": (1024, F32),
+    "eu": (64, U16), "ef": (64, F32), "hu": (64, U16), "hp": (64, F32), "nab": (64, F32), "up": (80, F32), "al": (64, F32),
+    "pd": (64, F32), "hm": (16, F32), "t1": (64, F32), "t2": (64, F32), "t3": (64, F32), "t4": (64, F32), "t5": (48, F32), "vo": (16, U16),
+    "EQ": (2176, BF), "VB": (256, BF), "DB": (256, BF), "NU": (256, F16), "FB": (256, BF), "PF": (256, BF), "junk": (1024, BF),
+    "sa": (8, F32), "ixf": (4, F32), "ixu": (4, U16), "du": (64, U16), "df": (64, F32), "nq": (64, F32), "lo": (64, U16), "wo": (48, U16),
+    "hmu": (16, U16), "HM": (256, F32), "ps": (2, F32), "psb": (2, BF),
+    "OUT1": (576, F16), "IN1": (576, F16), "OUT2": (192, BF), "IN2": (192, BF), "x0s": (64, BF), "c0s": (64, F16),
+    "e0s": (4, F32), "e0u": (4, U16), "xs4": (40, F32), "xu": (8, U16), "xg": (64, F16), "xd": (64, BF), "xp": (128, BF), "xq": (64, F16),
+    "xo": (4, U16), "xb": (64, BF),
+}
+SCRATCH = {k: ("sbuf", [128, w], d) for k, (w, d) in SB.items()}
+for _b in range(8):
+    SCRATCH["pb%d" % _b] = ("psum", [128, 512], F32)
+SCRATCH["pb6"] = ("psum", [128, 1024], BF)
+DMAS = ["dho", "dhl", "dwr", "ddm0", "ddm1", "ddm2", "dx0", "dx1", "dyl", "dyw", "dy0", "dy1"]
+SEMAPHORES = ["V", "S", "PE", "G", "sent"] + DMAS + ["a1_%d" % t for t in range(RO)] + ["a2_%d" % t for t in range(RO)]
+
+PAR = dict(GA=1.56, SC=3.8, HOP=150.0, PEC=0.5, NET=3000.0, DMAL=2400.0, MX=1.0,
+           SPL=24, GS=2, NQ=2, IT=6, MARG=300.0, FR=0.5, NE=8, LB=("ma", 0, 128))
+PLAN = {}
+
+
+def rank_program(g, core, T, topo):
+    rank = T.rank_of(core)
+    if rank is None:
+        return
+    N = len(T.cores)
+    ops = []
+    GA, SC, PEC = PAR["GA"], PAR["SC"], PAR["PEC"]
+
+    def R(name, lo=0, hi=None, step=1):
+        hi = T[name].shape[1] if hi is None else hi
+        ap = T[name][:, lo:hi:step] if step > 1 else T[name][:, lo:hi]
+        return dict(ap=ap, rg=[(name, lo, hi)], n=len(range(lo, hi, step)), ps=name.startswith("pb"),
+                    b2=SB.get(name, (0, F32))[1] in (BF, F16, U16), ind=False)
+
+    def IND(win, off):
+        return dict(ap=win["ap"].indirect(off["ap"]), rg=win["rg"], off=off["rg"], n=16 * off["n"], ps=False, b2=win["b2"], ind=True)
+
+    def add(eng, fn, outs, ins, cost, **kw):
+        rd, wr = [], []
+        for o in outs:
+            wr += o["rg"]
+            rd += o.get("off", [])
+        for i in ins:
+            if isinstance(i, dict):
+                rd += i["rg"] + i.get("off", [])
+        ops.append(dict(eng=eng, fn=fn, rd=rd, wr=wr, cost=cost, **kw))
+
+    def ap(x):
+        return x["ap"] if isinstance(x, dict) else x
+
+    def vcost(out, in0, base):
+        return 60 + SC * out["n"] if out["ind"] else 60 + GA * in0["n"] if in0["ind"] else max(64, base)
+
+    def tt(out, a, b, op, f=1.0):
+        add("V", lambda: g.vector.tensor_tensor(out["ap"], a["ap"], b["ap"], op), [out], [a, b],
+            vcost(out, a, f * b["n"] * (1 if a["ps"] or b["ps"] else 2)))
+
+    def ts(out, a, s1, s2, op0, op1=None):
+        c = vcost(out, a, a["n"] * (0.5 if a["b2"] and out["b2"] else 1))
+        if op1 is None:
+            add("V", lambda: g.vector.tensor_scalar(out["ap"], a["ap"], ap(s1), None, op0), [out], [a, s1], c)
+        else:
+            add("V", lambda: g.vector.tensor_scalar(out["ap"], a["ap"], ap(s1), ap(s2), op0, op1), [out], [a, s1, s2], c)
+
+    def cp(out, a):
+        add("V", lambda: g.vector.tensor_copy(out["ap"], a["ap"]), [out], [a], vcost(out, a, a["n"] * (0.5 if a["b2"] and out["b2"] else 1)))
+
+    def ms(out, v):
+        add("V", lambda: g.vector.memset(out["ap"], v), [out], [], max(64, out["n"] * (0.5 if out["b2"] else 1)))
+
+    def scan(out, d0, d1, init, op0, op1):
+        add("V", lambda: g.vector.tensor_tensor_scan(out["ap"], d0["ap"], d1["ap"], ap(init), op0, op1), [out], [d0, d1, init], max(64, out["n"]))
+
+    def red(out, a):
+        add("V", lambda: g.vector.tensor_reduce(out["ap"], a["ap"], AxisListType.X, A.add), [out], [a], max(64, a["n"]))
+
+    def act(out, a, f=F.Copy, bias=0.0, scale=1.0, acc=None):
+        c = 80 + SC * a["n"] if out["ind"] else 80 + GA * a["n"] if a["ind"] else max(64, a["n"]) + (24 if acc else 0)
+        if out["ind"]:
+            add("S", lambda: g.scalar.activation(out["ap"], a["ap"], f), [out], [a], c)
+        elif acc:
+            add("S", lambda: g.scalar.activation(out["ap"], a["ap"], f, ap(bias), scale, accum_out=acc["ap"]), [out, acc], [a, bias], c)
+        else:
+            add("S", lambda: g.scalar.activation(out["ap"], a["ap"], f, ap(bias), ap(scale)), [out], [a, bias, scale], c)
+
+    def mm(lst, each=False, st=True, sp=True):
+        def fn():
+            ins = None
+            for k, (o, l, r) in enumerate(lst):
+                ins = g.tensor.matmul(o["ap"], l["ap"], r["ap"], each or (st and k == 0), each or (sp and k == len(lst) - 1))
+            return ins
+        add("PE", fn, [o for o, l, r in lst], [x for o, l, r in lst for x in (l, r)],
+            sum(PEC * max(64, r["n"]) * (1 if r["b2"] else 4) for o, l, r in lst))
+
+    def b2w(out, name, lo, hi, Z="Z"):
+        mm([(out, R(Z, 15 - r, 143 - r), R(name, lo + r, hi, 16)) for r in range(16)])
+
+    def iota(out, pat, base, cm, flt=True):
+        if flt:
+            add("G", lambda: g.iota(out["ap"], pat, base, cm, allow_small_or_imprecise_dtypes=True), [out], [], 160 + 2 * out["n"])
+        else:
+            add("G", lambda: g.iota(out["ap"], pat, base, cm), [out], [], 160 + 2 * out["n"])
+
+    def asel(out, a, pat, op, base, cm):
+        add("G", lambda: g.affine_select(out["ap"], a["ap"], pat, op, 0.0, base, cm), [out], [a], 200 + 2 * out["n"])
+
+    def dma(q, sem, out, in_, outs, ins, kb):
+        e = g.sync if q == "Y" else g.scalar
+        add(q, lambda: e.dma_start(out, in_), outs, ins, 60, sem=sem, lat=PAR["DMAL"] + kb, pri=(1e9 - len(ops) if outs else 0))
+
+    def swap(land, out, dst, src, sem):
+        rid, pid, _ = topo.addr(dst)
+        eng = topo.engines(core, dst)[:PAR["NE"]]
+        m = sum(1 << e for e in eng)
+        add("G", lambda: g.remote_dma(land["ap"], out["ap"], T.sem[sem], T.sem.sent, pid, rid, m), [], [out], 300, remote=len(eng))
+        add("N", None, [land], [], 0, sem=sem, val=len(topo.engines(src, core)[:PAR["NE"]]), lat=PAR["NET"], after=len(ops) - 1)
+
+    pb = lambda b, lo=0, hi=512, st=1: R("pb%d" % b, lo, hi, st)
+    KB, ZB, DBK, ACC, XP, AB = (0, 1), (2, 3), 4, 5, 6, 7
+
+    dma("Y", "dho", T.hoi[:], T.ho[:], [R("hoi")], [], 0)
+    dma("S", "dwr", T.wi[:], T.wr[:], [R("wi")], [], 300)
+    dma("Y", "dhl", T.HLi[:], T.hl[:], [R("HLi")], [], 3300)
+    dma("Y", "dx0", T.X[:, 0:2048], T.xs[:, 0:2048], [R("X", 0, 2048)], [], 5500)
+    dma("Y", "dx1", T.X[:, 2048:P], T.xs[:, 2048:P], [R("X", 2048, P)], [], 7500)
+    for t in range(RO):
+        dma("Y", "ddm%d" % t, T.DM[:, 272 * t:272 * t + 256], T.dm[:, 256 * t:256 * t + 256], [R("DM", 272 * t, 272 * t + 256)], [], 8000)
+
+    ms(R("ONE"), 1.0)
+    iota(R("pi", 0, 1), [[0, 1]], 0, 1, False)
+    asel(R("BLt"), R("ONE"), [[-16, 8], [0, 16]], A.is_ge, 0, 1)
+    asel(R("BLf"), R("BLt"), [[16, 8], [0, 16]], A.is_ge, 15, -1)
+    iota(R("q16"), [[1, 16]], 0, 0)
+    asel(R("IDf"), R("ONE"), [[-1, 128]], A.is_equal, 0, 1)
+    iota(R("lasti"), [[16, 8]], 15, 0, False)
+    iota(R("SW"), [[16, 64]], 0, 0)
+    for k in range(4):
+        iota(R("IO2", 2048 * k, 2048 * k + 2048), [[1, 2048]], 2048 * k - 4096, 0)
+    ts(R("pi", 1, 2), R("pi", 0, 1), 15, None, A.bitwise_and)
+    QC, PW, SCL, SC2 = R("col", 0, 1), R("col", 1, 2), R("col", 2, 3), R("col", 3, 4)
+    cp(QC, R("pi", 1, 2))
+    ts(R("M16"), R("q16"), QC, None, A.is_equal)
+    for i in range(16):
+        o = R("LT", 128 * i, 128 * i + 128)
+        if i % 2:
+            act(o, R("BLf"), F.Identity, 0.0, R("M16", i, i + 1))
+        else:
+            ts(o, R("BLf"), R("M16", i, i + 1), None, A.mult)
+    cp(R("w16"), R("wi"))
+    for b in range(8):
+        k0 = (0, 1, 2, 3, 4, 5, 7, 0)[b]
+        mm([(pb(k0, 256 * k, 256 * k + 256), R("LT", 128 * (2 * b + k), 128 * (2 * b + k) + 128), R("w16")) for k in range(2)], each=True)
+        if b in (1, 4, 6):
+            cp(R("WT", 512 * b, 512 * b + 512), pb(k0))
+        else:
+            act(R("WT", 512 * b, 512 * b + 512), pb(k0))
+    cp(R("hou"), R("hoi"))
+    ts(R("hop"), R("hoi"), 1.0, None, A.add)
+    for k in range(4):
+        cp(R("HL", 384 * k, 384 * k + 384), R("HLi", 384 * k, 384 * k + 384))
+    for z in ("Z", "Zb"):
+        ms(R(z), 0.0)
+        cp(R(z, 15, 143, 16), R("BLf", 0, 128, 16))
+    for nm, v in (("G2", 2.0), ("Gm", -1.0)):
+        act(R(nm), R("BLf", 0, 128, 16), scale=v)
+    act(R("I8"), R("IDf"), scale=8192.0)
+    act(R("I8n"), R("IDf"), scale=-8192.0)
+    cp(R("I16"), R("IDf"))
+    cp(R("BL16"), R("BLf"))
+    act(R("BL4"), R("BLf"), scale=4.0)
+    act(R("ONEb"), R("ONE"))
+    for r in range(16):
+        ms(R("THR", r, 256, 16), 2.0 * 4.0 ** -r)
+    act(R("THH"), R("THR"), scale=0.5)
+    act(R("TN"), R("THR"), scale=-0.65)
+    act(R("THb"), R("THR"), scale=2.0 ** -13)
+    tt(R("tm16"), R("THH", 0, 16), R("M16"), A.mult)
+    red(PW, R("tm16"))
+    act(R("POW"), R("BLf"), F.Identity, 0.0, PW)
+    ts(SCL, QC, 0.5, -8192.0, A.is_gt, A.mult)
+    ts(SC2, SCL, -1.0, -6144.0, A.mult, A.add)
+    ms(R("RST"), 0.0)
+    ms(R("RST", 0, 128, 16), 1e6)
+    cp(R("last"), R("lasti"))
+    ts(R("SW"), R("SW"), QC, None, A.add)
+    ts(R("DL1"), R("SW"), H + 1.0, None, A.add)
+    ts(R("DW1"), R("SW", 0, 48), float(P), None, A.add)
+    ts(R("DX1"), R("SW", 0, 4), float(P), None, A.add)
+    ts(R("KH"), R("SW", 0, 4), 0.5, None, A.add)
+    for k in range(4):
+        ms(R("VT", 448 * k, 448 * k + 448), 0.0)
+    ms(R("Ua"), 1.0)
+    ms(R("Ub"), 1.0)
+    ms(R("need", 0, 1), 9.0)
+    ms(R("up", 16, 32), 1.0)
+    for t in range(RO):
+        ms(R("DM", 272 * t + 256, 272 * t + 272), 256.0)
+    ms(R("X0", 256, 272), 0.0)
+    ms(R("H4", 256, 264), 0.0)
+    ms(R("LSF", 1024, 1032), 4096.0)
+
+    XW, HW, WW = R("X", 0, P), R("HL", 0, H), R("WT", 0, P)
+    EOFF = 15 * 2050.0 + 2048.0
+
+    def nearest(a, lo, n, hoff, hw, split, lk=None, uo=0):
+        An, Mn, mn, Un = ("Aa", "Ma", "ma", "Ua") if a == 0 else ("Ab", "Mb", "mb", "Ub")
+        cp(R("LSu", lo, lo + n), IND(hw, hoff))
+        ts(R("LS16", lo, lo + n), R("LSu", lo, lo + n), -2048.0, None, A.add)
+        ns = n - split
+        gs = ns // PAR["GS"] if n == 128 else ns
+        for u in range(0, ns, gs):
+            act(R(An, 16 * u, 16 * (u + gs)), IND(XW, R("LSu", lo + u, lo + u + gs)))
+            if u == 0 and lk:
+                ops[-1]["rd"].append(lk)
+        if split:
+            cp(R(An, 16 * ns, 16 * n), IND(XW, R("LSu", lo + ns, lo + n)))
+        nq = n // PAR["NQ"] if n == 128 else n
+        for u in range(0, n, nq):
+            for j in range(16):
+                o = pb(KB[a], j, 128, 16)
+                tt(R(Mn, 128 * j + u, 128 * j + u + nq), R(An, 16 * u + j, 16 * (u + nq), 16), pb(XP, lo + u, lo + u + nq), A.max, PAR["MX"])
+                if u + nq == n:
+                    mm([(o, R(An, j, 2048, 16), R("Gm")), (o, R(Mn, 128 * j, 128 * j + 128), R("G2"))])
+        scan(R(mn, 0, 128), R("RST"), pb(KB[a], 0, 128), 0.0, A.add, A.min)
+        scan(R(mn, 128, 256), R("RST"), pb(KB[a], 0, 128), 0.0, A.add, A.min)
+        tt(R(Un, uo + 2, uo + 130), IND(R(mn, 0, 128), R("last")), R(mn, 128, 256), A.is_equal)
+        z = pb(ZB[a], 0, n)
+        mm([(z, R("I16"), R("LS16", lo, lo + n)), (z, R(Un, uo + 2, uo + 130), R("I8", 0, n)), (z, R(Un, uo + 1, uo + 129), R("I8n", 0, n))])
+        ts(R("C", lo, lo + n), z, SCL, -2050.0, A.add, A.max)
+
+    def pairs(nb, first, eqop, last=()):
+        lst, o = list(first), 0
+        for c in range(nb):
+            w = 16 * (nb - c)
+            eqop(R("EQ", o, o + w), c)
+            lst.append((pb(ACC, 16 * c, 16 * c + 16), R("POW"), R("EQ", o, o + 16)))
+            if w > 16:
+                lst.append((pb(ACC, 16 * c + 16, 16 * nb), R("BL4"), R("EQ", o + 16, o + w)))
+            o += w
+            if nb == 16 or c == nb - 1:
+                mm(lst, st=(c == 0 or nb < 16), sp=(c == nb - 1 and not last))
+                lst = []
+        if last:
+            mm(last, st=False)
+
+    W16 = lambda name, i: R(name, 16 * i, 16 * i + 16)
+    POS = {1: 0, 2: 1, 3: 2, 0: 3}
+    U = lambda a, i, k: R("Ub" if a else "Ua", 130 * (i - 1) + k, 130 * (i - 1) + k + 128)
+
+    def comes(a, k):
+        lo = 256 * POS[k] + 128 * a
+        o = pb(AB, 256 + 128 * a, 384 + 128 * a)
+        mm([(o, R("IDf"), R("VV", lo, lo + 128)), (o, U(a, k, 2), R("I8")), (o, U(a, k, 1), R("I8n"))])
+        act(R("PR", lo, lo + 128), o, F.Relu, SCL)
+
+    for t in range(RO):
+        need = R("need", t, t + 1)
+        MT = R("M16", t, t + 1)
+        h0 = W16("hou", t)
+        hw1 = R("HLi") if t == 0 else HW
+        dmt = lambda lo, hi: R("DM", 272 * t + lo, 272 * t + hi)
+        ts(R("C0"), IND(hw1, h0), -2048.0, MT, A.add, A.mult)
+        act(R("LSF", 768, 1024), IND(HW, h0))
+        b2w(pb(ZB[0], 256, 272), "C0", 0, 256)
+        ts(W16("eu", 0), pb(ZB[0], 256, 272), 2048.0, None, A.add)
+        act(W16("ef", 0), pb(ZB[0], 256, 272), F.Identity, 2048.0)
+        cp(R("JB", 128, 384), IND(WW, W16("eu", 0)))
+        b2w(pb(ZB[1], 256, 272), "JB", 128, 384)
+        ts(W16("hu", 1), pb(ZB[1], 256, 272), 1.0 / 16, None, A.mult)
+        act(W16("hp", 1), pb(ZB[1], 256, 272), F.Identity, 1.0, 1.0 / 16)
+        cp(R("X0", 0, 256), IND(XW, W16("eu", 0)))
+        cp(pb(XP, 0, 256), R("X0", 0, 256))
+        for a in range(2):
+            act(R("CODE", 128 * a, 128 * a + 128), R("ONE"), scale=2.0 ** (40 * t))
+            act(R("hq", 32 * a + 24, 32 * a + 32), R("hop", 16 * t + 8 * a, 16 * t + 8 * a + 8))
+            act(R("eq", 32 * a + 24, 32 * a + 32), R("ef", 8 * a, 8 * a + 8))
+        ts(W16("du", 3), W16("ef", 0), 4096.0, None, A.add)
+        act(R("VV", 512, 768), IND(R("IO2"), W16("du", 3)))
+        act(IND(R("VT"), h0), R("CODE"), F.Silu)
+        for i in range(1, 4):
+            jb, jn = 512 * (i - 1), 512 * i
+            act(R("VB"), IND(R("VT", 0, H), W16("hu", i)), scale=2.0 ** (-40 * t - 11))
+            tt(R("hm"), W16("hp", i), W16("up", i), A.mult)
+            pairs(16, [(pb(ACC, 0, 256), R("I8n"), R("THb"))],
+                  lambda o, c, jb=jb: ts(o, R("JB", jb + 128 + 16 * c, jb + 384), 1.0, R("hm", c, c + 1), A.add, A.is_equal),
+                  [(pb(ACC, 0, 256), R("I8"), R("VB"))])
+            act(R("DB"), pb(ACC, 0, 256), F.Relu, 0.0, 2.0 ** 31)
+            if i == 3:
+                tt(R("NU"), pb(ACC, 0, 256), R("TN"), A.is_lt)
+            b2w(pb(DBK, 0, 16), "DB", 0, 256, "Zb")
+            tt(W16("al", i), W16("up", i), pb(DBK, 0, 16), A.is_gt)
+            if i < 3:
+                tt(W16("t1", 0), W16("up", i), pb(DBK, 0, 16), A.is_le)
+                tt(W16("t1", 1), W16("t1", 0), W16("DL1", 0), A.mult)
+                tt(W16("t1", 2), W16("t1", 1), W16("hp", i), A.max)
+                ts(R("vo"), W16("t1", 2), -1.0, None, A.add)
+                act(IND(R("VT"), R("vo")), R("CODE"), F.Silu)
+            for a in range(2):
+                lo = 128 * a
+                w8 = lambda name, k: R(name, 16 * k + 8 * a, 16 * k + 8 * a + 8)
+                nearest(a, lo, 128, w8("hu", i), hw1 if i == 1 else HW, 0, PAR["LB"] if a else None, 130 * (i - 1))
+                o = pb(AB, lo, lo + 128)
+                mm([(o, R("I16"), R("LS16", lo, lo + 128)), (o, U(a, i, 2), R("I8n")), (o, U(a, i, 1), R("I8"))])
+                act(R("LSF", 256 * POS[i] + lo, 256 * POS[i] + lo + 128), o, F.Relu, SC2)
+                b2w(pb(ZB[a], 256, 264), "C", lo, lo + 128)
+                ts(w8("eu", i), pb(ZB[a], 256, 264), EOFF, None, A.add)
+                ts(w8("ef", i), pb(ZB[a], 256, 264), EOFF, None, A.add)
+                act(R("hq", 32 * a + 8 * i - 8, 32 * a + 8 * i), w8("hp", i))
+                ge = R("JB", jn + 384 * a, jn + 384 * a + 128)
+                if i < 3:
+                    act(R("eq", 32 * a + 8 * i, 32 * a + 8 * i + 8), w8("ef", i))
+                    cp(R("JB", jn + 128 + lo, jn + 256 + lo), IND(WW, w8("eu", i)))
+                    tt(ge, IND(XW, w8("eu", i)), dmt(lo, lo + 128), A.is_ge)
+                    b2w(pb(ZB[a], 272, 288), "JB", jn + 256 * a, jn + 256 * a + 256)
+                    hc, gc = pb(ZB[a], 280 - 8 * a, 288 - 8 * a), pb(ZB[a], 272 + 8 * a, 280 + 8 * a)
+                    ts(w8("hu", i + 1), hc, 1.0 / 16, None, A.mult)
+                    ts(w8("nab", i), gc, need, None, A.is_lt)
+                    act(w8("hp", i + 1), hc, F.Identity, 1.0, 1.0 / 16)
+                    continue
+                comes(a, 3)
+                tt(w8("t2", 0), w8("ef", 0), w8("ef", 3), A.subtract)
+                tt(w8("t2", 1), w8("t2", 0), w8("pd", 2), A.mult)
+                tt(w8("t2", 2), w8("t2", 1), w8("ef", 3), A.add)
+                ts(w8("du", 2), w8("t2", 2), 4096.0, None, A.add)
+                act(R("VV", 256 + lo, 384 + lo), IND(R("IO2"), w8("du", 2)))
+                comes(a, 2)
+                tt(ge, IND(XW, w8("eu", i)), dmt(lo, lo + 128), A.is_ge)
+                act(R("H4", lo, lo + 128), IND(WW, w8("eu", i)))
+                sc = pb(DBK, 256 + lo, 384 + lo)
+                mm([(sc, R("BL4"), R("DB", lo, lo + 128)), (sc, R("BL16"), R("NU", lo, lo + 128)), (sc, R("BL16"), ge)])
+                ts(R("FB", lo, lo + 128), sc, need, None, A.is_lt)
+                scan(R("PF", lo, lo + 128), R("ONE"), R("FB", lo, lo + 128), R("PF", 127, 128) if a else 0.0, A.mult, A.add)
+                for c in range(4):
+                    act(R("junk", 512 * a + 128 * c, 512 * a + 128 * c + 128), R("PF", lo, lo + 128), F.Sign,
+                        R("KH", c, c + 1), -1.0, R("sa", 4 * a + c, 4 * a + c + 1))
+                b2w(pb(ZB[a], 272, 280), "JB", jn + 384 * a, jn + 384 * a + 128)
+                ts(w8("nab", i), pb(ZB[a], 272, 280), need, None, A.is_ge)
+            if i == 3:
+                break
+            tt(W16("up", i + 1), W16("al", i), W16("nab", i), A.mult)
+            tt(W16("pd", i), W16("al", i), W16("up", i + 1), A.subtract)
+            if i == 1:
+                tt(W16("df", 0), W16("ef", 1), W16("ef", 0), A.subtract)
+                ts(W16("du", 0), W16("df", 0), 4096.0, None, A.add)
+                act(R("PR", 768, 1024), IND(R("IO2"), W16("du", 0)), F.Identity, 0.0, MT)
+            else:
+                tt(W16("t2", 0), W16("ef", 0), W16("ef", 2), A.subtract)
+                tt(W16("t2", 1), W16("t2", 0), W16("pd", 1), A.mult)
+                tt(W16("t2", 2), W16("t2", 1), W16("ef", 2), A.add)
+                ts(W16("du", 1), W16("t2", 2), 4096.0, None, A.add)
+                act(R("VV", 0, 256), IND(R("IO2"), W16("du", 1)))
+                comes(0, 1)
+                comes(1, 1)
+                ts(W16("df", 3), W16("pd", 2), -1.0, 1.0, A.mult, A.add)
+                tt(W16("up", 4), W16("df", 3), W16("pd", 1), A.subtract)
+                tt(R("t5", 0, 32), R("pd", 16, 48), R("hp", 16, 48), A.mult)
+                tt(W16("t5", 2), W16("t5", 0), W16("t5", 1), A.add)
+        for a in range(2):
+            lo = 128 * a
+            w8 = lambda name, k: R(name, 16 * k + 8 * a, 16 * k + 8 * a + 8)
+            q8 = lambda name, k, m=1: R(name, 32 * a + 8 * k, 32 * a + 8 * (k + m))
+            tt(w8("pd", 3), w8("al", 3), w8("nab", 3), A.mult)
+            tt(q8("nq", 0), w8("up", 4), w8("pd", 3), A.subtract)
+            tt(q8("nq", 1), w8("df", 3), w8("pd", 3), A.subtract)
+            ts(q8("nq", 2), w8("pd", 3), -1.0, 1.0, A.mult, A.add)
+            tt(q8("nq", 3), w8("up", 4), w8("pd", 3), A.subtract)
+            tt(q8("t3", 0, 4), q8("nq", 0, 4), q8("DL1", 0, 4), A.mult)
+            tt(q8("t4", 0, 4), q8("t3", 0, 4), q8("hq", 0, 4), A.max)
+            ts(q8("lo", 0, 4), q8("t4", 0, 4), -1.0, None, A.add)
+            for k in range(4):
+                tt(IND(R("HL"), q8("lo", k)), R("LSF", 256 * k + lo, 256 * k + lo + 128), R("PR", 256 * k + lo, 256 * k + lo + 128), A.add)
+            tt(q8("t3", 1, 3), q8("nq", 1, 3), R("DW1", 24 * a, 24 * a + 24), A.mult)
+            tt(q8("t4", 1, 3), q8("t3", 1, 3), q8("eq", 1, 3), A.max)
+            cp(R("wo", 24 * a, 24 * a + 24), q8("t4", 1, 3))
+        dst, src = T.cores[(rank + 1 + t % (N - 1)) % N], T.cores[(rank - 1 - t % (N - 1)) % N]
+        o1 = 192 * t
+        tt(R("ixf"), R("sa", 0, 4), R("sa", 4, 8), A.add)
+        ts(R("ixu"), R("ixf"), 256.0, 0.5, A.add, A.mult)
+        ix = R("ixu")
+        cp(R("OUT1", o1, o1 + 64), IND(R("H4", 0, 257), ix))
+        cp(R("OUT1", o1 + 64, o1 + 128), IND(R("X0", 0, 257), ix))
+        cp(R("OUT1", o1 + 128, o1 + 192), IND(dmt(0, 257), ix))
+        swap(R("IN1", o1, o1 + 192), R("OUT1", o1, o1 + 192), dst, src, "a1_%d" % t)
+        if t == RO - 1:
+            dma("Y", "dyl", T.yl[:], T.HL[:, 0:H], [], [HW], 3000)
+        act(R("x0s"), IND(R("X0", 0, 257), ix))
+        ts(R("c0s"), IND(R("LSF", 768, 1025), ix), -2048.0, MT, A.add, A.mult)
+        b2w(pb(DBK, 16, 20), "c0s", 0, 64)
+        x4 = lambda k: R("xs4", 4 * k, 4 * k + 4)
+        ts(R("e0s"), pb(DBK, 16, 20), 2048.0 - EOFF, None, A.add)
+        ts(x4(0), R("ixf"), 255.5, None, A.is_ge)
+        tt(x4(1), x4(0), R("SW", 0, 4), A.mult)
+        tt(x4(2), x4(1), pb(DBK, 16, 20), A.add)
+        ts(R("e0u"), x4(2), 2048.0, None, A.add)
+        tt(W16("t5", 0), W16("pd", 3), W16("hp", 3), A.mult)
+        tt(W16("t5", 1), W16("t5", 0), W16("t5", 2), A.add)
+        ts(R("hmu"), W16("t5", 1), 4095.0, None, A.add)
+        act(R("HM"), IND(R("IO2"), R("hmu")))
+        for k in range(3):
+            for u in range(0, 16, 8):
+                cp(IND(R("WT"), R("wo", 3 * u + 8 * k, 3 * u + 8 * k + 8)),
+                   R("JB", 512 * k + 128 + 16 * u, 512 * k + 256 + 16 * u) if k < 2 else R("HM", 16 * u, 16 * u + 128))
+        if t == RO - 1:
+            dma("S", "dyw", T.yw[:], T.WT[0:128:16, 0:P], [], [WW], 500)
+        else:
+            red(R("ps", 0, 1), R("nq", 0, 8))
+            red(R("ps", 1, 2), R("nq", 32, 40))
+            cp(R("psb"), R("ps"))
+            mm([(pb(DBK, 24, 25), R("ONEb"), R("psb", k, k + 1)) for k in range(2)])
+            cp(R("ni", 0, 1), pb(DBK, 24, 25))
+            ts(R("ni", 1, 2), R("ni", 0, 1), 1, None, A.bitwise_and)
+            ts(R("need", t + 1, t + 2), R("ni", 1, 2), 9.0, None, A.add)
+        b2w(pb(ZB[0], 256, 260), "IN1", o1, o1 + 64)
+        ts(R("xu", 0, 4), pb(ZB[0], 256, 260), 1.0 / 16, None, A.mult)
+        cp(R("xb"), R("IN1", o1 + 64, o1 + 128))
+        cp(pb(XP, 0, 64), R("IN1", o1 + 64, o1 + 128))
+        nearest(0, 0, 64, R("xu", 0, 4), HW, PAR["SPL"])
+        fw, fb = pb(ZB[0], 256, 260), pb(DBK, 256, 320)
+        b2w(fw, "C", 0, 64)
+        mm([(fb, R("BL16"), R("C", 0, 64))])
+        fu = R("xu", 4, 8)
+        ts(fu, fw, EOFF, None, A.add)
+        cp(x4(3), fw)
+        tt(R("xg"), IND(XW, fu), R("IN1", o1 + 128, o1 + 192), A.is_ge)
+        tt(R("xd"), IND(XW, fu), R("xb"), A.subtract)
+        b2w(pb(ZB[1], 256, 260), "xg", 0, 64)
+        for c in range(4):
+            ts(R("EQ", 256 + 64 * c, 320 + 64 * c), fb, R("e0s", c, c + 1), None, A.is_equal)
+        ts(x4(4), pb(ZB[1], 256, 260), need, None, A.is_ge)
+        tt(x4(5), x4(4), x4(3), A.mult)
+        pairs(4, [(pb(ACC, 0, 64), R("BL4"), R("EQ", 256 + 64 * c, 320 + 64 * c)) for c in range(4)],
+              lambda o, c: ts(o, pb(DBK, 256 + 16 * c, 320), R("xs4", 20 + c, 21 + c), None, A.is_equal))
+        tt(R("xp", 0, 64), pb(ACC, 0, 64), R("THH", 0, 64), A.is_ge)
+        tt(R("xp", 64, 128), pb(ACC, 0, 64), R("THR", 0, 64), A.is_lt)
+        tt(R("xq"), R("xp", 0, 64), R("xp", 64, 128), A.mult)
+        o2 = 64 * t
+        tt(R("OUT2", o2, o2 + 64), R("xq"), R("xd"), A.mult)
+        swap(R("IN2", o2, o2 + 64), R("OUT2", o2, o2 + 64), src, dst, "a2_%d" % t)
+        b2w(pb(ZB[1], 264, 268), "xq", 0, 64)
+        ts(x4(6), pb(ZB[1], 264, 268), 1.0, None, A.is_lt)
+        tt(x4(7), x4(6), R("DX1"), A.mult)
+        act(x4(8), x4(3), F.Identity, EOFF)
+        tt(x4(9), x4(7), x4(8), A.max)
+        cp(R("xo"), x4(9))
+        cp(IND(R("X"), R("xo")), R("xb"))
+        tt(IND(R("X"), R("e0u")), R("x0s"), R("IN2", o2, o2 + 64), A.add)
+    dma("Y", "dy0", T.yx[:, 0:2048], T.X[:, 0:2048], [], [XW], 4000)
+    dma("S", "dy1", T.yx[:, 2048:P], T.X[:, 2048:P], [], [XW], 4000)
+
+    emit(g, T, ops)
+
+
+def plan(ops, deps, succ, pr, delay, marg, fr):
+    n = len(ops)
+    left = [len(d) for d in deps]
+    pool = {}
+    for k in range(n):
+        if left[k] == 0:
+            pool.setdefault(ops[k]["eng"], []).append(k)
+    rt, fin, free, order, end = [0.0] * n, [0.0] * n, {}, [], 0.0
+    while len(order) < n:
+        t0, e = min((max(free.get(e, 0.0), min(rt[k] for k in p)), e) for e, p in pool.items() if p)
+        p = pool[e]
+        pick = None
+        for k in sorted((k for k in p if rt[k] <= t0), key=lambda k: -pr[k]):
+            if not any(rt[j] > t0 and pr[j] > pr[k] + marg and rt[j] - t0 < fr * ops[k]["cost"] for j in p):
+                pick = k
+                break
+        if pick is None:
+            free[e] = min(rt[j] for j in p if rt[j] > t0)
+            continue
+        p.remove(pick)
+        order.append(pick)
+        fin[pick] = free[e] = t0 + ops[pick]["cost"]
+        end = max(end, free[e] + ops[pick].get("lat", 0))
+        for j in succ[pick]:
+            rt[j] = max(rt[j], free[e] + delay(pick, j))
+            left[j] -= 1
+            if left[j] == 0:
+                pool.setdefault(ops[j]["eng"], []).append(j)
+    return end, order, fin
+
+
+def emit(g, T, ops):
+    n = len(ops)
+    if "order" not in PLAN:
+        seen, deps = {}, []
+        for k, o in enumerate(ops):
+            d = set()
+            for w, rgs in ((0, o["rd"]), (1, o["wr"])):
+                for name, lo, hi in rgs:
+                    ps = name.startswith("pb")
+                    for k2, w2, lo2, hi2 in seen.get(name, []):
+                        if (ps and ops[k2]["eng"] != o["eng"]) or ((w or w2) and lo < hi2 and lo2 < hi):
+                            d.add(k2)
+            if "after" in o:
+                d.add(o["after"])
+            for w, rgs in ((0, o["rd"]), (1, o["wr"])):
+                for name, lo, hi in set(rgs):
+                    seen.setdefault(name, []).append((k, w, lo, hi))
+            deps.append(sorted(d))
+        anc, red = [], []
+        for k in range(n):
+            m, keep = 0, []
+            for j in reversed(deps[k]):
+                if not m >> j & 1:
+                    keep.append(j)
+                m |= anc[j] | 1 << j
+            anc.append(m)
+            red.append(keep)
+        succ = [[] for _ in ops]
+        for k in range(n):
+            for j in red[k]:
+                succ[j].append(k)
+        fwd = lambda k, j: ops[k].get("lat", 0) + (0 if ops[k]["eng"] == ops[j]["eng"] == "PE" else PAR["HOP"])
+        bwd = lambda k, j: fwd(j, k)
+        pr0 = [0.0] * n
+        for k in range(n - 1, -1, -1):
+            pr0[k] = ops[k]["cost"] + max([pr0[j] + fwd(k, j) for j in succ[k]] + [ops[k].get("lat", 0)])
+        best = None
+        for fr in (PAR["FR"], 2 * PAR["FR"]):
+            pr = pr0
+            for it in range(PAR["IT"]):
+                res = plan(ops, red, succ, [max(pr[k], ops[k].get("pri", 0)) for k in range(n)], fwd, PAR["MARG"], fr)
+                if best is None or res[0] < best[0]:
+                    best = res
+                pr = plan(ops, succ, red, res[2], bwd, PAR["MARG"], fr)[2]
+        PLAN["order"], PLAN["deps"], PLAN["end"] = best[1], deps, best[0]
+    Q = {"V": g.vector, "S": g.scalar, "PE": g.tensor, "G": g, "Y": g.sync}
+    cnt, mark, known, sent = {}, {}, {}, 0
+    for k in PLAN["order"]:
+        o = ops[k]
+        e = o["eng"]
+        if e == "N":
+            mark[k] = (o["sem"], o["val"])
+            continue
+        want = {}
+        for j in PLAN["deps"][k]:
+            if j not in mark or (e == "PE" and ops[j]["eng"] == "PE"):
+                continue
+            s, v = mark[j]
+            want[s] = max(want.get(s, 0), v)
+        for s, v in want.items():
+            if known.get((e, s), 0) < v:
+                Q[e].wait_ge(T.sem[s], v)
+                known[(e, s)] = v
+        ins = o["fn"]()
+        if "remote" in o:
+            sent += o["remote"]
+        elif "sem" in o:
+            ins.then_inc(T.sem[o["sem"]], 16)
+            mark[k] = (o["sem"], 16)
+        else:
+            cnt[e] = cnt.get(e, 0) + 1
+            ins.then_inc(T.sem[e], 1)
+            mark[k] = (e, cnt[e])
+    for e in ("V", "S", "PE", "G"):
+        g.sync.wait_ge(T.sem[e], cnt[e])
+    g.sync.wait_ge(T.sem.sent, sent)
+    for s in DMAS:
+        g.sync.wait_ge(T.sem[s], 16)

@@ -3,36 +3,37 @@ from concourse.mybir import AluOpType as A, AxisListType, ActivationFunctionType
 P, H, S, RO, CAP = 4096, 1536, 256, 3, 64
 F32, BF, F16, I32, U16 = "float32", "bfloat16", "float16", "int32", "uint16"
 SB = {
-    "X": (P + 64, BF), "HLi": (H, I32), "HL": (H + 1024, F32), "WT": (P + 768, F32), "wi": (256, I32), "w16": (256, F16),
-    "hoi": (48, I32), "hou": (48, U16), "hop": (48, F32), "DM": (816, BF), "VT": (H + 256, F32), "IO2": (8192, F32),
-    "ONE": (128, F32), "IDf": (128, F32), "BLf": (128, F32), "BLt": (128, F32), "I8": (128, BF), "I8n": (128, BF), "I16": (128, F16),
-    "BL16": (128, F16), "BL4": (128, BF), "POW": (128, BF), "ONEb": (128, BF), "G2": (8, BF), "Gm": (8, BF),
-    "Z": (144, F16), "Zb": (144, BF), "LT": (2048, BF), "THR": (256, F32), "THH": (256, F32), "TN": (256, F32), "THb": (256, BF),
-    "RST": (128, F32), "pi": (2, I32), "q16": (16, F32), "M16": (16, F32),
-    "tm16": (16, F32), "col": (8, F32), "lasti": (8, I32), "last": (8, U16), "SW": (64, F32), "DL1": (64, F32), "DW1": (48, F32),
-    "DX1": (4, F32), "KH": (4, F32), "CODE": (256, F32), "need": (4, F32), "ni": (2, I32),
-    "Aa": (2048, BF), "Ab": (2048, BF), "Ma": (2048, BF), "Mb": (2048, BF), "ma": (256, F32), "mb": (256, F32),
-    "Ua": (390, BF), "Ub": (390, BF), "VV": (768, F32), "hq": (64, F32), "eq": (64, F32),
-    "LSu": (256, U16), "LS16": (256, F16), "C": (256, F16), "C0": (256, F16),
-    "JB": (2048, F16), "X0": (272, BF), "H4": (264, F32), "LSF": (1032, F32), "PR": (1024, F32),
-    "eu": (64, U16), "ef": (64, F32), "hu": (64, U16), "hp": (64, F32), "nab": (64, F32), "up": (80, F32), "al": (64, F32),
-    "pd": (64, F32), "hm": (16, F32), "t1": (64, F32), "t2": (64, F32), "t3": (64, F32), "t4": (64, F32), "t5": (48, F32), "vo": (16, U16),
-    "EQ": (2176, BF), "VB": (256, BF), "DB": (256, BF), "NU": (256, F16), "FB": (256, BF), "PF": (256, BF), "junk": (1024, BF),
-    "sa": (8, F32), "ixf": (4, F32), "ixu": (4, U16), "du": (64, U16), "df": (64, F32), "nq": (64, F32), "lo": (64, U16), "wo": (48, U16),
-    "hmu": (16, U16), "HM": (256, F32), "ps": (2, F32), "psb": (2, BF),
-    "OUT1": (576, F16), "IN1": (576, F16), "OUT2": (192, BF), "IN2": (192, BF), "x0s": (64, BF), "c0s": (64, F16),
-    "e0s": (4, F32), "e0u": (4, U16), "xs4": (40, F32), "xu": (8, U16), "xg": (64, F16), "xd": (64, BF), "xp": (128, BF), "xq": (64, F16),
-    "xo": (4, U16), "xb": (64, BF),
+    "X": (P + 64, BF), "HLi": (H, I32), "HL": (2 * H + 1024, F32), "DV": (16, F32), "HLo": (H, F32), "WT": (P + 768, F32), "wi": (256, I32), "w16": (256, F16),
+    "hoi": (48, I32), "hou": (48, U16), "DM": (816, BF), "VT": (H + 256, F32),
+    "ONE": (128, F32), "IDf": (128, F32), "BLf": (128, F32), "Ib": (128, BF), "In": (128, BF), "I8": (128, BF), "I8n": (128, BF),
+    "BLb": (128, BF), "BL4": (128, BF), "POW": (128, BF), "ONEb": (128, BF), "G2": (16, BF),
+    "Z": (144, BF), "Zn": (144, BF), "Zt": (432, BF), "Dt": (384, BF), "BT": (384, BF), "LT": (2048, BF), "THn": (256, BF), "th": (512, BF),
+    "RST": (128, F32), "RSn": (128, F32), "R01": (64, F32), "PW": (128, F16), "PX": (64, F32), "PP": (128, BF), "NP": (64, BF), "NN": (16, BF),
+    "pi": (2, I32), "q16": (128, F32), "dq": (384, F32), "M16": (16, F32), "col": (16, F32), "lasti": (8, I32), "last": (8, U16),
+    "SW": (64, F32), "DL": (64, F32), "DW": (48, F32), "DX": (12, F32), "CODE": (256, F32), "need": (4, F32), "ni": (2, I32),
+    "Aa": (2048, BF), "Ab": (2048, BF), "Ma": (2048, BF), "Mb": (2048, BF), "ma": (128, F32), "mb": (128, F32),
+    "Ua": (520, BF), "Ub": (390, BF), "LSu": (320, U16), "LS": (1088, F16), "C": (832, F16), "PR": (256, F16), "PRf": (256, F32),
+    "ES": (256, F32), "NEW": (1024, F32),
+    "JB": (768, F16), "GE": (768, BF), "SCN": (256, F16), "X0": (272, BF), "H4": (264, F32), "E0": (264, F32),
+    "eu": (64, U16), "hu": (64, U16), "hp": (64, F32), "ef": (48, F32), "hs": (16, F32), "nup": (32, BF), "dB": (48, F32), "pB": (32, F32),
+    "t1": (128, F32), "t2": (160, F32), "hD": (64, F32), "bs": (64, F32), "lof": (64, F32), "lo": (64, U16),
+    "val": (48, F16), "t3": (144, F32), "wo": (48, U16), "vo": (16, U16), "HM": (768, F32),
+    "EQ": (2176, BF), "EX": (416, BF), "VB": (256, BF), "DB": (256, BF), "FB": (256, BF), "PF": (256, BF), "junk": (1040, BF),
+    "sa": (12, F32), "ixu": (4, U16), "h4c": (64, F16), "e0c": (128, F32), "FS": (128, F32),
+    "OUT1": (576, F16), "IN1": (576, F16), "OUT2": (192, BF), "IN2": (192, BF), "x0s": (64, BF),
+    "e0u": (4, U16), "xs4": (24, F32), "xu": (8, U16), "xg": (64, BF), "xd": (64, BF), "nb": (64, BF), "xq": (64, BF), "xo": (4, U16),
 }
 SCRATCH = {k: ("sbuf", [128, w], d) for k, (w, d) in SB.items()}
 for _b in range(8):
     SCRATCH["pb%d" % _b] = ("psum", [128, 512], F32)
 SCRATCH["pb6"] = ("psum", [128, 1024], BF)
-DMAS = ["dho", "dhl", "dwr", "ddm0", "ddm1", "ddm2", "dx0", "dx1", "dyl", "dyw", "dy0", "dy1"]
+DMAS = ["dho", "dhl", "dwr", "ddm0", "ddm1", "ddm2", "dx0", "dx1", "dyl", "dyw", "dw2", "dy0", "dy1"]
 SEMAPHORES = ["V", "S", "PE", "G", "sent"] + DMAS + ["a1_%d" % t for t in range(RO)] + ["a2_%d" % t for t in range(RO)]
 
-PAR = dict(GA=1.56, SC=3.8, HOP=150.0, PEC=0.5, NET=3000.0, DMAL=2400.0, MX=1.0,
-           SPL=24, GS=2, NQ=2, IT=6, MARG=300.0, FR=0.5, NE=8, LB=("ma", 0, 128))
+PAR = dict(GA=1.56, SC=3.8, HOP=100.0, PEC=0.5, NET=3000.0, DMAL=2400.0,
+           SPL=24, SPS=(40, 0, 0, 0, 0, 0), GS=(0, 64), NQ=2, IT=3, MIX=0.3, LAM=(0.2, 0.4, 0.6), NE=8, WQ=0, UM="R",
+           HLE="SS", HG=((0, 2, 4), (0, 4)), WTE="SSSSSS", WG=(0, 2, 4, 6), HV=300.0, PRE="VVVV", FBE="V", EB="PPPPSS",
+           URG={})
 PLAN = {}
 
 
@@ -41,14 +42,18 @@ def rank_program(g, core, T, topo):
     if rank is None:
         return
     N = len(T.cores)
-    ops = []
+    ops, tag = [], ["set"]
     GA, SC, PEC = PAR["GA"], PAR["SC"], PAR["PEC"]
 
     def R(name, lo=0, hi=None, step=1):
         hi = T[name].shape[1] if hi is None else hi
         ap = T[name][:, lo:hi:step] if step > 1 else T[name][:, lo:hi]
         return dict(ap=ap, rg=[(name, lo, hi)], n=len(range(lo, hi, step)), ps=name.startswith("pb"),
-                    b2=SB.get(name, (0, F32))[1] in (BF, F16, U16), ind=False)
+                    b2=name == "pb6" or SB.get(name, (0, F32))[1] in (BF, F16, U16), ind=False)
+
+    def REV(x):
+        name, lo, hi = x["rg"][0]
+        return dict(x, ap=T[name][:, hi - 1:(lo - 1 if lo else None):-1])
 
     def IND(win, off):
         return dict(ap=win["ap"].indirect(off["ap"]), rg=win["rg"], off=off["rg"], n=16 * off["n"], ps=False, b2=win["b2"], ind=True)
@@ -61,7 +66,7 @@ def rank_program(g, core, T, topo):
         for i in ins:
             if isinstance(i, dict):
                 rd += i["rg"] + i.get("off", [])
-        ops.append(dict(eng=eng, fn=fn, rd=rd, wr=wr, cost=cost, **kw))
+        ops.append(dict(eng=eng, fn=fn, rd=rd, wr=wr, cost=cost, tag=tag[0], **kw))
 
     def ap(x):
         return x["ap"] if isinstance(x, dict) else x
@@ -69,9 +74,9 @@ def rank_program(g, core, T, topo):
     def vcost(out, in0, base):
         return 60 + SC * out["n"] if out["ind"] else 60 + GA * in0["n"] if in0["ind"] else max(64, base)
 
-    def tt(out, a, b, op, f=1.0):
+    def tt(out, a, b, op):
         add("V", lambda: g.vector.tensor_tensor(out["ap"], a["ap"], b["ap"], op), [out], [a, b],
-            vcost(out, a, f * b["n"] * (1 if a["ps"] or b["ps"] else 2)))
+            vcost(out, a, b["n"] * (1 if a["ps"] or b["ps"] else 2)))
 
     def ts(out, a, s1, s2, op0, op1=None):
         c = vcost(out, a, a["n"] * (0.5 if a["b2"] and out["b2"] else 1))
@@ -87,7 +92,8 @@ def rank_program(g, core, T, topo):
         add("V", lambda: g.vector.memset(out["ap"], v), [out], [], max(64, out["n"] * (0.5 if out["b2"] else 1)))
 
     def scan(out, d0, d1, init, op0, op1):
-        add("V", lambda: g.vector.tensor_tensor_scan(out["ap"], d0["ap"], d1["ap"], ap(init), op0, op1), [out], [d0, d1, init], max(64, out["n"]))
+        add("V", lambda: g.vector.tensor_tensor_scan(out["ap"], d0["ap"], d1["ap"], ap(init), op0, op1), [out], [d0, d1, init],
+            max(64, out["n"] * (0.5 if out["b2"] and d0["b2"] and d1["b2"] else 1)))
 
     def red(out, a):
         add("V", lambda: g.vector.tensor_reduce(out["ap"], a["ap"], AxisListType.X, A.add), [out], [a], max(64, a["n"]))
@@ -110,8 +116,11 @@ def rank_program(g, core, T, topo):
         add("PE", fn, [o for o, l, r in lst], [x for o, l, r in lst for x in (l, r)],
             sum(PEC * max(64, r["n"]) * (1 if r["b2"] else 4) for o, l, r in lst))
 
-    def b2w(out, name, lo, hi, Z="Z"):
-        mm([(out, R(Z, 15 - r, 143 - r), R(name, lo + r, hi, 16)) for r in range(16)])
+    def b2w(out, name, lo, hi, Z="Z", z0=0):
+        return [(out, R(Z, z0 + 15 - r, z0 + 143 - r), R(name, lo + r, hi, 16)) for r in range(16)]
+
+    def w2b(b, lo, hi, w):
+        return [(pb(b, lo + r, hi, 16), R("LT", 128 * r, 128 * r + 128), w) for r in range(16)]
 
     def iota(out, pat, base, cm, flt=True):
         if flt:
@@ -122,42 +131,44 @@ def rank_program(g, core, T, topo):
     def asel(out, a, pat, op, base, cm):
         add("G", lambda: g.affine_select(out["ap"], a["ap"], pat, op, 0.0, base, cm), [out], [a], 200 + 2 * out["n"])
 
-    def dma(q, sem, out, in_, outs, ins, kb):
+    def dma(q, sem, out, in_, outs, ins, kb, first=False):
         e = g.sync if q == "Y" else g.scalar
-        add(q, lambda: e.dma_start(out, in_), outs, ins, 60, sem=sem, lat=PAR["DMAL"] + kb, pri=(1e9 - len(ops) if outs else 0))
+        add(q, lambda: e.dma_start(out, in_), outs, ins, 60, sem=sem, lat=PAR["DMAL"] + kb, pri=(1e9 - len(ops) if first else 0))
 
     def swap(land, out, dst, src, sem):
         rid, pid, _ = topo.addr(dst)
         eng = topo.engines(core, dst)[:PAR["NE"]]
         m = sum(1 << e for e in eng)
         add("G", lambda: g.remote_dma(land["ap"], out["ap"], T.sem[sem], T.sem.sent, pid, rid, m), [], [out], 300, remote=len(eng))
-        add("N", None, [land], [], 0, sem=sem, val=len(topo.engines(src, core)[:PAR["NE"]]), lat=PAR["NET"], after=len(ops) - 1)
+        add("N", None, [land], [], 0, sem=sem, val=len(topo.engines(src, core)[:PAR["NE"]]), lat=PAR["NET"] - PAR["HOP"], after=len(ops) - 1)
 
     pb = lambda b, lo=0, hi=512, st=1: R("pb%d" % b, lo, hi, st)
-    KB, ZB, DBK, ACC, XP, AB = (0, 1), (2, 3), 4, 5, 6, 7
+    KZ, ACC, DK, GK, P0, XP, P1 = (0, 1), 2, 3, 4, 5, 6, 7
 
-    dma("Y", "dho", T.hoi[:], T.ho[:], [R("hoi")], [], 0)
-    dma("S", "dwr", T.wi[:], T.wr[:], [R("wi")], [], 300)
-    dma("Y", "dhl", T.HLi[:], T.hl[:], [R("HLi")], [], 3300)
-    dma("Y", "dx0", T.X[:, 0:2048], T.xs[:, 0:2048], [R("X", 0, 2048)], [], 5500)
-    dma("Y", "dx1", T.X[:, 2048:P], T.xs[:, 2048:P], [R("X", 2048, P)], [], 7500)
+    dma("Y", "dho", T.hoi[:], T.ho[:], [R("hoi")], [], 140, True)
+    dma("S", "dwr", T.wi[:], T.wr[:], [R("wi")], [], 860, True)
+    dma("Y", "dhl", T.HLi[:], T.hl[:], [R("HLi")], [], 5170, True)
+    dma("Y", "dx0", T.X[:, 0:2048], T.xs[:, 0:2048], [R("X", 0, 2048)], [], 8000, True)
+    dma("Y", "dx1", T.X[:, 2048:P], T.xs[:, 2048:P], [R("X", 2048, P)], [], 10880, True)
     for t in range(RO):
-        dma("Y", "ddm%d" % t, T.DM[:, 272 * t:272 * t + 256], T.dm[:, 256 * t:256 * t + 256], [R("DM", 272 * t, 272 * t + 256)], [], 8000)
+        dma("Y", "ddm%d" % t, T.DM[:, 272 * t:272 * t + 256], T.dm[:, 256 * t:256 * t + 256], [R("DM", 272 * t, 272 * t + 256)], [],
+            11200 + 300 * t, True)
 
+    col = lambda k: R("col", k, k + 1)
+    QC, PWc, SCL, FW, FX = col(0), col(1), col(2), col(3), col(4)
     ms(R("ONE"), 1.0)
     iota(R("pi", 0, 1), [[0, 1]], 0, 1, False)
-    asel(R("BLt"), R("ONE"), [[-16, 8], [0, 16]], A.is_ge, 0, 1)
-    asel(R("BLf"), R("BLt"), [[16, 8], [0, 16]], A.is_ge, 15, -1)
-    iota(R("q16"), [[1, 16]], 0, 0)
+    asel(R("dq", 0, 128), R("ONE"), [[-16, 8], [0, 16]], A.is_ge, 0, 1)
+    asel(R("BLf"), R("dq", 0, 128), [[16, 8], [0, 16]], A.is_ge, 15, -1)
+    iota(R("q16"), [[0, 8], [1, 16]], 0, 0)
     asel(R("IDf"), R("ONE"), [[-1, 128]], A.is_equal, 0, 1)
     iota(R("lasti"), [[16, 8]], 15, 0, False)
     iota(R("SW"), [[16, 64]], 0, 0)
-    for k in range(4):
-        iota(R("IO2", 2048 * k, 2048 * k + 2048), [[1, 2048]], 2048 * k - 4096, 0)
+    iota(R("CODE"), [[0, 256]], 1, 0)
+    iota(R("VT"), [[0, H + 256]], 0, 0)
     ts(R("pi", 1, 2), R("pi", 0, 1), 15, None, A.bitwise_and)
-    QC, PW, SCL, SC2 = R("col", 0, 1), R("col", 1, 2), R("col", 2, 3), R("col", 3, 4)
     cp(QC, R("pi", 1, 2))
-    ts(R("M16"), R("q16"), QC, None, A.is_equal)
+    ts(R("M16"), R("q16", 0, 16), QC, None, A.is_equal)
     for i in range(16):
         o = R("LT", 128 * i, 128 * i + 128)
         if i % 2:
@@ -169,358 +180,486 @@ def rank_program(g, core, T, topo):
         k0 = (0, 1, 2, 3, 4, 5, 7, 0)[b]
         mm([(pb(k0, 256 * k, 256 * k + 256), R("LT", 128 * (2 * b + k), 128 * (2 * b + k) + 128), R("w16")) for k in range(2)], each=True)
         if b in (1, 4, 6):
-            cp(R("WT", 512 * b, 512 * b + 512), pb(k0))
+            ts(R("WT", 512 * b, 512 * b + 512), pb(k0), 4096.0, None, A.add)
         else:
-            act(R("WT", 512 * b, 512 * b + 512), pb(k0))
+            act(R("WT", 512 * b, 512 * b + 512), pb(k0), F.Identity, 4096.0)
     cp(R("hou"), R("hoi"))
-    ts(R("hop"), R("hoi"), 1.0, None, A.add)
     for k in range(4):
-        cp(R("HL", 384 * k, 384 * k + 384), R("HLi", 384 * k, 384 * k + 384))
-    for z in ("Z", "Zb"):
-        ms(R(z), 0.0)
-        cp(R(z, 15, 143, 16), R("BLf", 0, 128, 16))
-    for nm, v in (("G2", 2.0), ("Gm", -1.0)):
-        act(R(nm), R("BLf", 0, 128, 16), scale=v)
-    act(R("I8"), R("IDf"), scale=8192.0)
-    act(R("I8n"), R("IDf"), scale=-8192.0)
-    cp(R("I16"), R("IDf"))
-    cp(R("BL16"), R("BLf"))
+        ts(R("HL", 384 * k, 384 * k + 384), R("HLi", 384 * k, 384 * k + 384), 4096.0, None, A.add)
+    ms(R("Z"), 0.0)
+    cp(R("Z", 15, 143, 16), R("BLf", 0, 128, 16))
+    act(R("Zn"), R("Z"), scale=-4096.0)
+    ms(R("BT"), 0.0)
+    for t in range(RO):
+        MT = R("M16", t, t + 1)
+        act(R("Zt", 144 * t, 144 * t + 144), R("Z"), F.Identity, 0.0, MT)
+        ts(col(8 + t), MT, -1.0, 1.0, A.mult, A.add)
+        act(R("Dt", 128 * t, 128 * t + 128), R("IDf"), F.Identity, 0.0, col(8 + t))
+        act(R("BT", 128 * t + t, 128 * t + 128, 16), R("BLf", 0, 128, 16))
+        ts(col(12 + t), MT, 30720.0, 6144.0, A.mult, A.add)
+    for k, v in ((0, 2.0), (8, -1.0)):
+        act(R("G2", k, k + 8), R("BLf", 0, 128, 16), scale=v)
+    for nm, v in (("I8", 8192.0), ("I8n", -8192.0), ("Ib", 1.0), ("In", -1.0)):
+        act(R(nm), R("IDf"), scale=v)
+    act(R("BLb"), R("BLf"))
     act(R("BL4"), R("BLf"), scale=4.0)
     act(R("ONEb"), R("ONE"))
-    for r in range(16):
-        ms(R("THR", r, 256, 16), 2.0 * 4.0 ** -r)
-    act(R("THH"), R("THR"), scale=0.5)
-    act(R("TN"), R("THR"), scale=-0.65)
-    act(R("THb"), R("THR"), scale=2.0 ** -13)
-    tt(R("tm16"), R("THH", 0, 16), R("M16"), A.mult)
-    red(PW, R("tm16"))
-    act(R("POW"), R("BLf"), F.Identity, 0.0, PW)
+    ms(R("th", 0, 256), 0.25)
+    ms(R("th", 256, 512), 0.0)
+    ms(R("th", 256, 512, 16), -2.0)
+    scan(R("THn"), R("th", 0, 256), R("th", 256, 512), 0.0, A.mult, A.min)
+    ms(R("th", 0, 256), 0.0)
+    tt(R("t1", 0, 16), R("THn", 0, 16), R("M16"), A.mult)
+    red(col(5), R("t1", 0, 16))
+    ts(PWc, col(5), -0.5, None, A.mult)
+    act(R("POW"), R("BLf"), F.Identity, 0.0, PWc)
     ts(SCL, QC, 0.5, -8192.0, A.is_gt, A.mult)
-    ts(SC2, SCL, -1.0, -6144.0, A.mult, A.add)
+    ts(FW, QC, 14.5, 1536.0, A.is_lt, A.mult)
+    ts(FX, QC, 14.5, 16384.0, A.is_lt, A.mult)
     ms(R("RST"), 0.0)
     ms(R("RST", 0, 128, 16), 1e6)
+    act(R("RSn"), R("RST"), scale=-1.0)
+    act(R("R01"), R("RST", 0, 64), F.Relu, 1.0, -1.0)
+    ts(R("dq", 0, 128), R("q16"), QC, None, A.subtract)
+    ts(R("dq", 128, 256), R("dq", 0, 128), 0.5, 4096.0, A.is_lt, A.mult)
+    ts(R("dq", 256, 384), R("dq", 0, 128), 1.0, -1536.0, A.is_equal, A.mult)
+    tt(R("PW"), R("dq", 128, 256), R("dq", 256, 384), A.add)
+    ts(R("PP"), R("dq", 0, 128), 0.0, -65536.0, A.not_equal, A.mult)
+    ts(R("dq", 128, 192), R("dq", 0, 64), 0.5, 32768.0, A.is_lt, A.mult)
+    ts(R("dq", 256, 320), R("dq", 0, 64), 1.0, -16384.0, A.is_equal, A.mult)
+    tt(R("PX"), R("dq", 128, 192), R("dq", 256, 320), A.add)
     cp(R("last"), R("lasti"))
     ts(R("SW"), R("SW"), QC, None, A.add)
-    ts(R("DL1"), R("SW"), H + 1.0, None, A.add)
-    ts(R("DW1"), R("SW", 0, 48), float(P), None, A.add)
-    ts(R("DX1"), R("SW", 0, 4), float(P), None, A.add)
-    ts(R("KH"), R("SW", 0, 4), 0.5, None, A.add)
-    for k in range(4):
-        ms(R("VT", 448 * k, 448 * k + 448), 0.0)
+    act(R("DL"), R("SW"), F.Identity, 2.0 * H)
+    act(R("DV"), R("SW", 0, 16), F.Identity, float(H))
+    ts(col(6), SCL, 2048.0, None, A.add)
+    act(R("DW"), R("SW", 0, 48), F.Identity, P - 2048.0)
+    act(R("DX", 0, 4), R("SW", 0, 4), F.Identity, float(P))
+    ts(R("DX", 4, 8), R("DX", 0, 4), FX, None, A.subtract)
+    act(R("DX", 8, 12), R("SW", 0, 4), F.Identity, 1.0, 2.0)
     ms(R("Ua"), 1.0)
     ms(R("Ub"), 1.0)
     ms(R("need", 0, 1), 9.0)
-    ms(R("up", 16, 32), 1.0)
     for t in range(RO):
         ms(R("DM", 272 * t + 256, 272 * t + 272), 256.0)
     ms(R("X0", 256, 272), 0.0)
     ms(R("H4", 256, 264), 0.0)
-    ms(R("LSF", 1024, 1032), 4096.0)
+    ms(R("E0", 256, 264), 8192.0)
 
     XW, HW, WW = R("X", 0, P), R("HL", 0, H), R("WT", 0, P)
-    EOFF = 15 * 2050.0 + 2048.0
+    EOFF, RND = 32768.0, 2.0 ** 23 - 4096
+    gat = []
 
-    def nearest(a, lo, n, hoff, hw, split, lk=None, uo=0):
+    def nearest(a, n, hoff, hw, sub, lu, ls, cc, xp, split, uo):
         An, Mn, mn, Un = ("Aa", "Ma", "ma", "Ua") if a == 0 else ("Ab", "Mb", "mb", "Ub")
-        cp(R("LSu", lo, lo + n), IND(hw, hoff))
-        ts(R("LS16", lo, lo + n), R("LSu", lo, lo + n), -2048.0, None, A.add)
+        ts(R("LSu", lu, lu + n), IND(hw, hoff), -sub, None, A.add)
+        ts(R("LS", ls, ls + n), R("LSu", lu, lu + n), -2048.0, None, A.add)
         ns = n - split
-        gs = ns // PAR["GS"] if n == 128 else ns
-        for u in range(0, ns, gs):
-            act(R(An, 16 * u, 16 * (u + gs)), IND(XW, R("LSu", lo + u, lo + u + gs)))
-            if u == 0 and lk:
-                ops[-1]["rd"].append(lk)
+        cuts = [u for u in PAR["GS"] if u < ns] + [ns] if n == 128 else [0, ns]
+        for u, v in zip(cuts, cuts[1:]):
+            act(R(An, 16 * u, 16 * v), IND(XW, R("LSu", lu + u, lu + v)))
+            ops[-1]["soft"] = gat[-1:]
+            gat.append(len(ops) - 1)
         if split:
-            cp(R(An, 16 * ns, 16 * n), IND(XW, R("LSu", lo + ns, lo + n)))
+            cp(R(An, 16 * ns, 16 * n), IND(XW, R("LSu", lu + ns, lu + n)))
         nq = n // PAR["NQ"] if n == 128 else n
         for u in range(0, n, nq):
             for j in range(16):
-                o = pb(KB[a], j, 128, 16)
-                tt(R(Mn, 128 * j + u, 128 * j + u + nq), R(An, 16 * u + j, 16 * (u + nq), 16), pb(XP, lo + u, lo + u + nq), A.max, PAR["MX"])
+                o = pb(KZ[a], j, 128, 16)
+                tt(R(Mn, 128 * j + u, 128 * j + u + nq), R(An, 16 * u + j, 16 * (u + nq), 16), pb(XP, xp + u, xp + u + nq), A.max)
                 if u + nq == n:
-                    mm([(o, R(An, j, 2048, 16), R("Gm")), (o, R(Mn, 128 * j, 128 * j + 128), R("G2"))])
-        scan(R(mn, 0, 128), R("RST"), pb(KB[a], 0, 128), 0.0, A.add, A.min)
-        scan(R(mn, 128, 256), R("RST"), pb(KB[a], 0, 128), 0.0, A.add, A.min)
-        tt(R(Un, uo + 2, uo + 130), IND(R(mn, 0, 128), R("last")), R(mn, 128, 256), A.is_equal)
-        z = pb(ZB[a], 0, n)
-        mm([(z, R("I16"), R("LS16", lo, lo + n)), (z, R(Un, uo + 2, uo + 130), R("I8", 0, n)), (z, R(Un, uo + 1, uo + 129), R("I8n", 0, n))])
-        ts(R("C", lo, lo + n), z, SCL, -2050.0, A.add, A.max)
+                    mm([(o, R(An, j, 2048, 16), R("G2", 8, 16)), (o, R(Mn, 128 * j, 128 * j + 128), R("G2", 0, 8))])
+        scan(R(mn), R("RST"), pb(KZ[a], 0, 128), 0.0, A.add, A.min)
+        if PAR["UM"] == "R":
+            scan(REV(pb(KZ[a], 128, 256)), R("RST"), REV(pb(KZ[a], 0, 128)), 0.0, A.add, A.min)
+            tt(R(Un, uo + 2, uo + 130), R(mn), pb(KZ[a], 128, 256), A.is_le)
+        else:
+            scan(R(mn + "2"), R("RST"), pb(KZ[a], 0, 128), 0.0, A.add, A.min)
+            tt(R(Un, uo + 2, uo + 130), IND(R(mn), R("last")), R(mn + "2"), A.is_equal)
+        z = pb(KZ[a], 128, 128 + n)
+        mm([(z, R("Ib"), R("LS", ls, ls + n)), (z, R(Un, uo + 2, uo + 130), R("I8", 0, n)), (z, R(Un, uo + 1, uo + 129), R("I8n", 0, n))])
+        ts(R("C", cc, cc + n), z, SCL, -2048.0, A.add, A.max)
 
-    def pairs(nb, first, eqop, last=()):
-        lst, o = list(first), 0
+    def pairs(nb, bank, EQ, eqop):
+        res, o = [], 0
         for c in range(nb):
             w = 16 * (nb - c)
-            eqop(R("EQ", o, o + w), c)
-            lst.append((pb(ACC, 16 * c, 16 * c + 16), R("POW"), R("EQ", o, o + 16)))
+            eqop(R(EQ, o, o + w), c)
+            lst = [(pb(bank, 16 * c, 16 * c + 16), R("POW"), R(EQ, o, o + 16))]
             if w > 16:
-                lst.append((pb(ACC, 16 * c + 16, 16 * nb), R("BL4"), R("EQ", o + 16, o + w)))
+                lst.append((pb(bank, 16 * c + 16, 16 * nb), R("BL4"), R(EQ, o + 16, o + w)))
             o += w
-            if nb == 16 or c == nb - 1:
-                mm(lst, st=(c == 0 or nb < 16), sp=(c == nb - 1 and not last))
-                lst = []
-        if last:
-            mm(last, st=False)
+            if nb == 16:
+                mm(lst, st=False, sp=False)
+            else:
+                res += lst
+        return res
 
-    W16 = lambda name, i: R(name, 16 * i, 16 * i + 16)
-    POS = {1: 0, 2: 1, 3: 2, 0: 3}
+    W16 = lambda name, i, m=1: R(name, 16 * i, 16 * (i + m))
+    N8 = lambda name, i, a: R(name, 16 * i + 8 * a, 16 * i + 8 * a + 8)
+    EP = {1: 0, 2: 1, 0: 2}
+    LP = {0: 0, 1: 1, 3: 2, 2: 3}
+    NEW = lambda i, a: R("NEW", 512 * a + 128 * LP[i], 512 * a + 128 * LP[i] + 128)
     U = lambda a, i, k: R("Ub" if a else "Ua", 130 * (i - 1) + k, 130 * (i - 1) + k + 128)
+    W256 = lambda name, i: R(name, 256 * i, 256 * i + 256)
+    HB = lambda name, i, a: R(name, 256 * i + 128 * a, 256 * i + 128 * a + 128)
 
-    def comes(a, k):
-        lo = 256 * POS[k] + 128 * a
-        o = pb(AB, 256 + 128 * a, 384 + 128 * a)
-        mm([(o, R("IDf"), R("VV", lo, lo + 128)), (o, U(a, k, 2), R("I8")), (o, U(a, k, 1), R("I8n"))])
-        act(R("PR", lo, lo + 128), o, F.Relu, SCL)
+    def unwrap(i, a):
+        sc = HB("SCN", 0, a)
+        scan(sc, R("PW"), HB("JB", i - 1, a), 0.0, A.add, A.min)
+        e = R("SCN", 128 * a + 15, 128 * a + 128, 16)
+        ts(N8("hu", i, a), e, FW, None, A.add)
+        if a:
+            ts(W16("hp", i), R("SCN", 15, 256, 16), FW, None, A.add)
 
+    def relist(q, o, i, lo, hi):
+        if PAR["PRE"][i] == "V":
+            ts(R("PR", lo, hi), q, SCL, -2048.0, A.add, A.max)
+            pr, bias = (o, R("Ib"), R("PR", lo, hi)), 6144.0
+        else:
+            act(R("PRf", lo, hi), q, F.Relu, col(6))
+            pr, bias = (o, R("IDf"), R("PRf", lo, hi)), 4096.0
+        mm([(o, R("Ib"), R("LS", 256 * i + lo, 256 * i + hi)), (o, R("In"), R("C", 256 * i - 256 + lo, 256 * i - 256 + hi)), pr])
+        o0 = o["rg"][0][1]
+        for u in range(lo, hi, 128):
+            act(NEW(i, u // 128), pb(P1, o0 + u - lo, o0 + u - lo + 128), F.Identity, bias)
+
+    def newlist(t, i, a):
+        o = pb(P1, 128 * a, 128 * a + 128)
+        if i == 0:
+            mm([(o, R("Dt", 128 * t, 128 * t + 128), HB("LS", 0, a)), (o, R("BT", 128 * t, 128 * t + 128), HB("C", 0, a))])
+            act(NEW(0, a), o, F.Identity, col(12 + t))
+            return
+        q = pb(P0, 128 * a, 128 * a + 128)
+        lst = [(q, U(a, i, 2), R("I8")), (q, U(a, i, 1), R("I8n"))]
+        if i == 3:
+            lst.append((q, R("LT", 128 * t, 128 * t + 128), HB("LS", 0, a)))
+        else:
+            lst += w2b(P0, 128 * a, 128 * a + 128, N8("val", 1, a))
+        mm(lst)
+        relist(q, o, i, 128 * a, 128 * a + 128)
+
+    sent = []
     for t in range(RO):
         need = R("need", t, t + 1)
-        MT = R("M16", t, t + 1)
         h0 = W16("hou", t)
-        hw1 = R("HLi") if t == 0 else HW
+        hw1, sub1 = (R("HLi"), 0.0) if t == 0 else (HW, 4096.0)
         dmt = lambda lo, hi: R("DM", 272 * t + lo, 272 * t + hi)
-        ts(R("C0"), IND(hw1, h0), -2048.0, MT, A.add, A.mult)
-        act(R("LSF", 768, 1024), IND(HW, h0))
-        b2w(pb(ZB[0], 256, 272), "C0", 0, 256)
-        ts(W16("eu", 0), pb(ZB[0], 256, 272), 2048.0, None, A.add)
-        act(W16("ef", 0), pb(ZB[0], 256, 272), F.Identity, 2048.0)
-        cp(R("JB", 128, 384), IND(WW, W16("eu", 0)))
-        b2w(pb(ZB[1], 256, 272), "JB", 128, 384)
-        ts(W16("hu", 1), pb(ZB[1], 256, 272), 1.0 / 16, None, A.mult)
-        act(W16("hp", 1), pb(ZB[1], 256, 272), F.Identity, 1.0, 1.0 / 16)
-        cp(R("X0", 0, 256), IND(XW, W16("eu", 0)))
-        cp(pb(XP, 0, 256), R("X0", 0, 256))
+        T1, T2 = (lambda k: W16("t1", k)), (lambda k: W16("t2", k))
+        p1, p2 = W16("pB", 0), W16("pB", 1)
+        tag[0] = "first"
+        ts(R("LS", 0, 256), IND(hw1, h0), -2048.0 - sub1, None, A.add)
+        mm(b2w(pb(GK, 32, 48), "LS", 0, 256, "Zt", 144 * t))
+        ts(W16("eu", 0), pb(GK, 32, 48), 2048.0, None, A.add)
         for a in range(2):
-            act(R("CODE", 128 * a, 128 * a + 128), R("ONE"), scale=2.0 ** (40 * t))
-            act(R("hq", 32 * a + 24, 32 * a + 32), R("hop", 16 * t + 8 * a, 16 * t + 8 * a + 8))
-            act(R("eq", 32 * a + 24, 32 * a + 32), R("ef", 8 * a, 8 * a + 8))
-        ts(W16("du", 3), W16("ef", 0), 4096.0, None, A.add)
-        act(R("VV", 512, 768), IND(R("IO2"), W16("du", 3)))
+            ts(HB("JB", 0, a), IND(WW, N8("eu", 0, a)), RND, -2.0 ** 23, A.add, A.add)
+            unwrap(1, a)
+        for a in range(2):
+            cp(HB("X0", 0, a), IND(XW, N8("eu", 0, a)))
+            cp(pb(XP, 128 * a, 128 * a + 128), HB("X0", 0, a))
+        tag[0] = "misc"
+        ts(W16("ef", EP[0]), W16("eu", 0), -2048.0, None, A.add)
+        cp(W16("hp", 0), W16("hoi", t))
+        mm([(pb(P1, 256, 512), R("LT", 128 * t, 128 * t + 128), R("LS", 0, 256))])
+        act(R("E0", 0, 256), pb(P1, 256, 512), F.Identity, 2048.0)
+        ts(R("NP"), R("PP", 0, 64), need, 1.0, A.subtract, A.add)
+        ts(col(7), need, 4096.0, None, A.mult)
+        if PAR["FBE"] == "S":
+            ts(col(11), need, -0.5, None, A.add)
+        tag[0] = "mark0"
+        if t:
+            act(R("CODE"), R("CODE"), scale=2.0 ** 40)
+            ops[-1]["soft"] = sent[-1:]
         act(IND(R("VT"), h0), R("CODE"), F.Silu)
+        ops[-1]["cost"] += 0 if t else 1560
         for i in range(1, 4):
-            jb, jn = 512 * (i - 1), 512 * i
+            tag[0] = "die%d" % i
             act(R("VB"), IND(R("VT", 0, H), W16("hu", i)), scale=2.0 ** (-40 * t - 11))
-            tt(R("hm"), W16("hp", i), W16("up", i), A.mult)
-            pairs(16, [(pb(ACC, 0, 256), R("I8n"), R("THb"))],
-                  lambda o, c, jb=jb: ts(o, R("JB", jb + 128 + 16 * c, jb + 384), 1.0, R("hm", c, c + 1), A.add, A.is_equal),
-                  [(pb(ACC, 0, 256), R("I8"), R("VB"))])
-            act(R("DB"), pb(ACC, 0, 256), F.Relu, 0.0, 2.0 ** 31)
-            if i == 3:
-                tt(R("NU"), pb(ACC, 0, 256), R("TN"), A.is_lt)
-            b2w(pb(DBK, 0, 16), "DB", 0, 256, "Zb")
-            tt(W16("al", i), W16("up", i), pb(DBK, 0, 16), A.is_gt)
+            hs, hc = ("hp", 16) if i == 1 else ("hs", 0)
+            if i > 1:
+                tt(R("hs"), W16("hp", i), W16("nup", i - 2), A.add)
+            mm([(pb(ACC, 0, 256), R("Ib"), R("THn"))] + (w2b(ACC, 0, 256, W16("nup", 1)) if i == 3 else []), sp=False)
+            pairs(16, ACC, "EQ", lambda o, c, i=i, hs=hs, hc=hc: ts(
+                o, R("JB", 256 * i - 256 + 16 * c, 256 * i), R(hs, hc + c, hc + c + 1), None, A.is_equal))
+            mm([(pb(ACC, 0, 256), R("I8"), R("VB"))], st=False)
+            act(R("DB"), pb(ACC, 0, 256), F.Relu, 0.0, 2.0 ** 38)
+            dW = pb(DK, 0, 16)
+            mm(b2w(dW, "DB", 0, 256))
             if i < 3:
-                tt(W16("t1", 0), W16("up", i), pb(DBK, 0, 16), A.is_le)
-                tt(W16("t1", 1), W16("t1", 0), W16("DL1", 0), A.mult)
-                tt(W16("t1", 2), W16("t1", 1), W16("hp", i), A.max)
-                ts(R("vo"), W16("t1", 2), -1.0, None, A.add)
+                tt(T1(0), R(hs, hc, hc + 16), dW, A.add)
+                tag[0] = "mark%d" % i
+                tt(T1(1), T1(0), R("DV"), A.min)
+                cp(R("vo"), T1(1))
                 act(IND(R("VT"), R("vo")), R("CODE"), F.Silu)
+                tag[0] = "up%d" % i
+                ts(W16("dB", i - 1), T1(0), 2000.0, 8192.0, A.is_ge, A.mult)
+            else:
+                d3 = W16("dB", 2)
+                ts(d3, dW, 1.0, 8192.0, A.is_ge, A.mult)
+                ts(R("NN"), d3, -8.0, col(7), A.mult, A.add)
+                tag[0] = "where"
+                tt(T2(3), d3, p2, A.subtract)
+                tt(T2(4), T2(3), p1, A.subtract)
+                for k, nq in ((0, T2(4)), (1, T2(4)), (2, T2(3)), (3, d3)):
+                    tt(W16("bs", k), W16("hp", k), nq, A.add)
+                tt(R("hD"), R("bs"), R("DL"), A.min)
             for a in range(2):
                 lo = 128 * a
-                w8 = lambda name, k: R(name, 16 * k + 8 * a, 16 * k + 8 * a + 8)
-                nearest(a, lo, 128, w8("hu", i), hw1 if i == 1 else HW, 0, PAR["LB"] if a else None, 130 * (i - 1))
-                o = pb(AB, lo, lo + 128)
-                mm([(o, R("I16"), R("LS16", lo, lo + 128)), (o, U(a, i, 2), R("I8n")), (o, U(a, i, 1), R("I8"))])
-                act(R("LSF", 256 * POS[i] + lo, 256 * POS[i] + lo + 128), o, F.Relu, SC2)
-                b2w(pb(ZB[a], 256, 264), "C", lo, lo + 128)
-                ts(w8("eu", i), pb(ZB[a], 256, 264), EOFF, None, A.add)
-                ts(w8("ef", i), pb(ZB[a], 256, 264), EOFF, None, A.add)
-                act(R("hq", 32 * a + 8 * i - 8, 32 * a + 8 * i), w8("hp", i))
-                ge = R("JB", jn + 384 * a, jn + 384 * a + 128)
+                tag[0] = "climb%d%s" % (i, "ab"[a])
+                nearest(a, 128, N8("hu", i, a), hw1 if i == 1 else HW, sub1 if i == 1 else 4096.0, lo, 256 * i + lo, 256 * i - 256 + lo, lo,
+                        PAR["SPS"][2 * i - 2 + a], 130 * (i - 1))
+                eu = N8("eu", i, a)
+                if PAR["EB"][2 * i - 2 + a] == "P":
+                    ew = pb(KZ[a], 256, 264)
+                    mm(b2w(ew, "C", 256 * i - 256 + lo, 256 * i - 128 + lo))
+                else:
+                    y = pb(KZ[a], 256, 384)
+                    mm([(y, R("Ib"), R("PP")), (y, R("BLb"), HB("C", i - 1, a))])
+                    scan(HB("ES", 0, a), R("RSn"), y, 0.0, A.add, A.max)
+                    ew = R("ES", lo + 15, lo + 128, 16)
+                ts(eu, ew, EOFF, None, A.add)
+                ge = HB("GE", i - 1, a)
                 if i < 3:
-                    act(R("eq", 32 * a + 8 * i, 32 * a + 8 * i + 8), w8("ef", i))
-                    cp(R("JB", jn + 128 + lo, jn + 256 + lo), IND(WW, w8("eu", i)))
-                    tt(ge, IND(XW, w8("eu", i)), dmt(lo, lo + 128), A.is_ge)
-                    b2w(pb(ZB[a], 272, 288), "JB", jn + 256 * a, jn + 256 * a + 256)
-                    hc, gc = pb(ZB[a], 280 - 8 * a, 288 - 8 * a), pb(ZB[a], 272 + 8 * a, 280 + 8 * a)
-                    ts(w8("hu", i + 1), hc, 1.0 / 16, None, A.mult)
-                    ts(w8("nab", i), gc, need, None, A.is_lt)
-                    act(w8("hp", i + 1), hc, F.Identity, 1.0, 1.0 / 16)
+                    ts(HB("JB", i, a), IND(WW, eu), RND, -2.0 ** 23, A.add, A.add)
+                    unwrap(i + 1, a)
+                    if i == 1:
+                        tag[0] = "new0"
+                        newlist(t, 0, a)
                     continue
-                comes(a, 3)
-                tt(w8("t2", 0), w8("ef", 0), w8("ef", 3), A.subtract)
-                tt(w8("t2", 1), w8("t2", 0), w8("pd", 2), A.mult)
-                tt(w8("t2", 2), w8("t2", 1), w8("ef", 3), A.add)
-                ts(w8("du", 2), w8("t2", 2), 4096.0, None, A.add)
-                act(R("VV", 256 + lo, 384 + lo), IND(R("IO2"), w8("du", 2)))
-                comes(a, 2)
-                tt(ge, IND(XW, w8("eu", i)), dmt(lo, lo + 128), A.is_ge)
-                act(R("H4", lo, lo + 128), IND(WW, w8("eu", i)))
-                sc = pb(DBK, 256 + lo, 384 + lo)
-                mm([(sc, R("BL4"), R("DB", lo, lo + 128)), (sc, R("BL16"), R("NU", lo, lo + 128)), (sc, R("BL16"), ge)])
-                ts(R("FB", lo, lo + 128), sc, need, None, A.is_lt)
-                scan(R("PF", lo, lo + 128), R("ONE"), R("FB", lo, lo + 128), R("PF", 127, 128) if a else 0.0, A.mult, A.add)
+                tag[0] = "fail" + "ab"[a]
+                tt(ge, IND(XW, eu), dmt(lo, lo + 128), A.is_ge)
+                act(HB("H4", 0, a), IND(WW, eu), F.Identity, -4096.0)
+                sc = pb(DK, 256 + lo, 384 + lo)
+                mm([(sc, R("BL4"), HB("DB", 0, a)), (sc, R("BLb"), ge)])
+                if PAR["FBE"] == "S":
+                    act(HB("FB", 0, a), sc, F.Sign, col(11), -1.0)
+                    scan(HB("PF", 0, a), R("ONEb"), HB("FB", 0, a), R("PF", 127, 128) if a else 0.0, A.add, A.add)
+                else:
+                    ts(HB("FB", 0, a), sc, need, 2.0, A.is_lt, A.mult)
+                    scan(HB("PF", 0, a), R("ONEb"), HB("FB", 0, a), R("PF", 127, 128) if a else 0.0, A.mult, A.add)
                 for c in range(4):
-                    act(R("junk", 512 * a + 128 * c, 512 * a + 128 * c + 128), R("PF", lo, lo + 128), F.Sign,
-                        R("KH", c, c + 1), -1.0, R("sa", 4 * a + c, 4 * a + c + 1))
-                b2w(pb(ZB[a], 272, 280), "JB", jn + 384 * a, jn + 384 * a + 128)
-                ts(w8("nab", i), pb(ZB[a], 272, 280), need, None, A.is_ge)
+                    act(R("junk", 512 * a + 128 * c, 512 * a + 128 * c + 128), HB("PF", 0, a), F.Sign,
+                        R("DX", 8 + c, 9 + c), -1.0, R("sa", 4 * a + c, 4 * a + c + 1))
+                    if a:
+                        ts(R("ixu", c, c + 1), R("sa", 4 + c, 5 + c), R("sa", 8 + c, 9 + c), 0.5, A.add, A.mult)
+                if a == 0:
+                    ts(R("sa", 8, 12), R("sa", 0, 4), 256.0, None, A.add)
+                tag[0] = "pay" + "ab"[a]
+                cn = pb(GK, 16 + 8 * a, 24 + 8 * a)
+                mm([(cn, R("Ib"), N8("NN", 0, a))] + b2w(cn, "GE", 512 + lo, 640 + lo, "Zn"))
+                q8 = lambda name, k, m=1: R(name, 32 * a + 8 * k, 32 * a + 8 * (k + m))
+                tt(N8("t2", 8, a), ew, N8("t2", 6, a), A.subtract)
+                tt(N8("val", 1, a), N8("t2", 8, a), N8("t2", 5, a), A.max)
+                newlist(t, 3, a)
+                newlist(t, 2, a)
+                ts(N8("t2", 7, a), cn, 0.0, float(H), A.max, A.min)
+                for k in range(4):
+                    tt(q8("lof", LP[k]), N8("t2", 7, a), N8("hD", k, a), A.add)
+                cp(q8("lo", 0, 4), q8("lof", 0, 4))
             if i == 3:
+                for a in range(2):
+                    tag[0] = "list" + "ab"[a]
+                    for u, v in zip(PAR["HG"][a], PAR["HG"][a][1:]):
+                        off, new = R("lo", 32 * a + 8 * u, 32 * a + 8 * v), R("NEW", 512 * a + 128 * u, 512 * a + 128 * v)
+                        if PAR["HLE"][a] == "S":
+                            act(IND(R("HL"), off), new, F.Silu)
+                        else:
+                            cp(IND(R("HL"), off), new)
                 break
-            tt(W16("up", i + 1), W16("al", i), W16("nab", i), A.mult)
-            tt(W16("pd", i), W16("al", i), W16("up", i + 1), A.subtract)
-            if i == 1:
-                tt(W16("df", 0), W16("ef", 1), W16("ef", 0), A.subtract)
-                ts(W16("du", 0), W16("df", 0), 4096.0, None, A.add)
-                act(R("PR", 768, 1024), IND(R("IO2"), W16("du", 0)), F.Identity, 0.0, MT)
-            else:
-                tt(W16("t2", 0), W16("ef", 0), W16("ef", 2), A.subtract)
-                tt(W16("t2", 1), W16("t2", 0), W16("pd", 1), A.mult)
-                tt(W16("t2", 2), W16("t2", 1), W16("ef", 2), A.add)
-                ts(W16("du", 1), W16("t2", 2), 4096.0, None, A.add)
-                act(R("VV", 0, 256), IND(R("IO2"), W16("du", 1)))
-                comes(0, 1)
-                comes(1, 1)
-                ts(W16("df", 3), W16("pd", 2), -1.0, 1.0, A.mult, A.add)
-                tt(W16("up", 4), W16("df", 3), W16("pd", 1), A.subtract)
-                tt(R("t5", 0, 32), R("pd", 16, 48), R("hp", 16, 48), A.mult)
-                tt(W16("t5", 2), W16("t5", 0), W16("t5", 1), A.add)
-        for a in range(2):
-            lo = 128 * a
-            w8 = lambda name, k: R(name, 16 * k + 8 * a, 16 * k + 8 * a + 8)
-            q8 = lambda name, k, m=1: R(name, 32 * a + 8 * k, 32 * a + 8 * (k + m))
-            tt(w8("pd", 3), w8("al", 3), w8("nab", 3), A.mult)
-            tt(q8("nq", 0), w8("up", 4), w8("pd", 3), A.subtract)
-            tt(q8("nq", 1), w8("df", 3), w8("pd", 3), A.subtract)
-            ts(q8("nq", 2), w8("pd", 3), -1.0, 1.0, A.mult, A.add)
-            tt(q8("nq", 3), w8("up", 4), w8("pd", 3), A.subtract)
-            tt(q8("t3", 0, 4), q8("nq", 0, 4), q8("DL1", 0, 4), A.mult)
-            tt(q8("t4", 0, 4), q8("t3", 0, 4), q8("hq", 0, 4), A.max)
-            ts(q8("lo", 0, 4), q8("t4", 0, 4), -1.0, None, A.add)
-            for k in range(4):
-                tt(IND(R("HL"), q8("lo", k)), R("LSF", 256 * k + lo, 256 * k + lo + 128), R("PR", 256 * k + lo, 256 * k + lo + 128), A.add)
-            tt(q8("t3", 1, 3), q8("nq", 1, 3), R("DW1", 24 * a, 24 * a + 24), A.mult)
-            tt(q8("t4", 1, 3), q8("t3", 1, 3), q8("eq", 1, 3), A.max)
-            cp(R("wo", 24 * a, 24 * a + 24), q8("t4", 1, 3))
+            tag[0] = "up%d" % i
+            tt(W256("GE", i - 1), IND(XW, W16("eu", i)), dmt(0, 256), A.is_ge)
+            mm(b2w(pb(GK, 0, 16), "GE", 256 * i - 256, 256 * i))
+            ts(T1(2), pb(GK, 0, 16), need, 8192.0, A.is_ge, A.mult)
+            tt(W16("nup", i - 1), T1(2), W16("dB", i - 1), A.max)
+            tt(W16("pB", i - 1), W16("nup", i - 1), W16("dB", i - 1), A.subtract)
+            tag[0] = "new1"
+            ts(W16("ef", EP[i]), W16("eu", i), -2048.0, None, A.add)
+            if i == 2:
+                ts(T2(0), W16("ef", EP[0]), -8192.0, None, A.add)
+                tt(T2(1), T2(0), p1, A.add)
+                tt(T2(2), W16("ef", EP[2]), p1, A.subtract)
+                tt(W16("val", 0), T2(1), T2(2), A.max)
+                q, o = pb(P0, 256, 512), pb(P1, 256, 512)
+                mm([(q, R("Ib"), R("th", 0, 256))] + w2b(P0, 256, 512, W16("val", 0)) +
+                   [(pb(P0, 256 + 128 * a, 384 + 128 * a), U(a, 1, k), R(w)) for a in range(2) for k, w in ((2, "I8"), (1, "I8n"))])
+                relist(q, o, 1, 0, 256)
+                tt(T2(5), T2(0), p2, A.add)
+                ts(T2(6), p2, 2048.0 - EOFF, None, A.add)
+        tag[0] = "send"
         dst, src = T.cores[(rank + 1 + t % (N - 1)) % N], T.cores[(rank - 1 - t % (N - 1)) % N]
         o1 = 192 * t
-        tt(R("ixf"), R("sa", 0, 4), R("sa", 4, 8), A.add)
-        ts(R("ixu"), R("ixf"), 256.0, 0.5, A.add, A.mult)
         ix = R("ixu")
-        cp(R("OUT1", o1, o1 + 64), IND(R("H4", 0, 257), ix))
+        cp(R("h4c"), IND(R("H4", 0, 257), ix))
         cp(R("OUT1", o1 + 64, o1 + 128), IND(R("X0", 0, 257), ix))
+        scan(R("OUT1", o1, o1 + 64), R("PW", 0, 64), R("h4c"), 0.0, A.add, A.min)
         cp(R("OUT1", o1 + 128, o1 + 192), IND(dmt(0, 257), ix))
         swap(R("IN1", o1, o1 + 192), R("OUT1", o1, o1 + 192), dst, src, "a1_%d" % t)
+        sent.append(len(ops) - 2)
+        tag[0] = "yl"
         if t == RO - 1:
-            dma("Y", "dyl", T.yl[:], T.HL[:, 0:H], [], [HW], 3000)
-        act(R("x0s"), IND(R("X0", 0, 257), ix))
-        ts(R("c0s"), IND(R("LSF", 768, 1025), ix), -2048.0, MT, A.add, A.mult)
-        b2w(pb(DBK, 16, 20), "c0s", 0, 64)
+            for k in range(4):
+                ts(R("HLo", 384 * k, 384 * k + 384), R("HL", 384 * k, 384 * k + 384), RND, -2.0 ** 23, A.add, A.add)
+            dma("Y", "dyl", T.yl[:], T.HLo[:], [], [R("HLo")], 4400)
+        tag[0] = "own"
         x4 = lambda k: R("xs4", 4 * k, 4 * k + 4)
-        ts(R("e0s"), pb(DBK, 16, 20), 2048.0 - EOFF, None, A.add)
-        ts(x4(0), R("ixf"), 255.5, None, A.is_ge)
-        tt(x4(1), x4(0), R("SW", 0, 4), A.mult)
-        tt(x4(2), x4(1), pb(DBK, 16, 20), A.add)
-        ts(R("e0u"), x4(2), 2048.0, None, A.add)
-        tt(W16("t5", 0), W16("pd", 3), W16("hp", 3), A.mult)
-        tt(W16("t5", 1), W16("t5", 0), W16("t5", 2), A.add)
-        ts(R("hmu"), W16("t5", 1), 4095.0, None, A.add)
-        act(R("HM"), IND(R("IO2"), R("hmu")))
-        for k in range(3):
-            for u in range(0, 16, 8):
-                cp(IND(R("WT"), R("wo", 3 * u + 8 * k, 3 * u + 8 * k + 8)),
-                   R("JB", 512 * k + 128 + 16 * u, 512 * k + 256 + 16 * u) if k < 2 else R("HM", 16 * u, 16 * u + 128))
+        act(R("x0s"), IND(R("X0", 0, 257), ix))
+        act(R("e0c", 0, 64), IND(R("E0", 0, 257), ix))
+        scan(R("e0c", 64, 128), R("PX"), R("e0c", 0, 64), 0.0, A.add, A.min)
+        tt(x4(0), R("e0c", 79, 128, 16), R("DX", 4, 8), A.min)
+        ts(R("e0u"), x4(0), FX, None, A.add)
+        ts(x4(5), R("e0u"), -EOFF, None, A.add)
+        tag[0] = "warr"
+        T3 = lambda k, m=1: W16("t3", k, m)
+        for a in range(2):
+            ts(N8("t3", 1, a), R("lof", 32 * a + 16, 32 * a + 24), H - 0.5, 8192.0, A.is_ge, A.mult)
+        tt(T3(0), T3(1), p2, A.subtract)
+        tt(T3(2), T3(0), p1, A.subtract)
+        tt(T3(3, 3), T3(0, 3), R("ef"), A.add)
+        tt(T3(6, 3), T3(3, 3), R("DW"), A.min)
+        ts(R("wo"), T3(6, 3), 2048.0, None, A.add)
+        tag[0] = "hm"
+        tt(T1(3), W16("hp", 1), W16("hp", 2), A.subtract)
+        tt(T1(4), W16("hp", 2), W16("hp", 3), A.subtract)
+        tt(W16("t1", 5, 2), W16("t1", 3, 2), T3(0, 2), A.mult)
+        tt(T1(7), T1(5), T1(6), A.add)
+        ts(W16("val", 2), T1(7), 2.0 ** -13, None, A.mult)
+        o = pb(P1, 256, 512)
+        mm([(o, R("Ib"), W256("JB", 2))] + w2b(P1, 256, 512, W16("val", 2)))
+        act(W256("HM", 2), o, F.Identity, 4096.0)
+        tag[0] = "hj"
+        for k in range(2):
+            o = pb(P0, 256 * k, 256 * k + 256)
+            mm([(o, R("Ib"), W256("JB", k))])
+            act(W256("HM", k), o, F.Identity, 4096.0)
+        tag[0] = "warr"
+        for e, u, v in zip(PAR["WTE"], PAR["WG"], PAR["WG"][1:]):
+            if e == "S":
+                act(IND(R("WT"), R("wo", 8 * u, 8 * v)), R("HM", 128 * u, 128 * v), F.Silu)
+            else:
+                cp(IND(R("WT"), R("wo", 8 * u, 8 * v)), R("HM", 128 * u, 128 * v))
+        tag[0] = "odd"
         if t == RO - 1:
-            dma("S", "dyw", T.yw[:], T.WT[0:128:16, 0:P], [], [WW], 500)
+            dma("Y", "dw2", T.E0[:, 0:256], T.WT[0:128:16, 0:P], [R("E0", 0, 256)], [WW], 800)
+            ts(R("H4", 0, 256), R("E0", 0, 256), RND, -2.0 ** 23, A.add, A.add)
+            dma("Y", "dyw", T.yw[:], T.H4[:, 0:256], [], [R("H4", 0, 256)], 800)
         else:
-            red(R("ps", 0, 1), R("nq", 0, 8))
-            red(R("ps", 1, 2), R("nq", 32, 40))
-            cp(R("psb"), R("ps"))
-            mm([(pb(DBK, 24, 25), R("ONEb"), R("psb", k, k + 1)) for k in range(2)])
-            cp(R("ni", 0, 1), pb(DBK, 24, 25))
+            act(R("junk", 1024, 1040), T3(2), F.Sign, -0.5, 1.0, col(15))
+            mm([(pb(GK, 48, 49), R("ONE"), col(15))])
+            ts(R("ni", 0, 1), pb(GK, 48, 49), -0.5, 1024.0, A.mult, A.add)
             ts(R("ni", 1, 2), R("ni", 0, 1), 1, None, A.bitwise_and)
             ts(R("need", t + 1, t + 2), R("ni", 1, 2), 9.0, None, A.add)
-        b2w(pb(ZB[0], 256, 260), "IN1", o1, o1 + 64)
-        ts(R("xu", 0, 4), pb(ZB[0], 256, 260), 1.0 / 16, None, A.mult)
-        cp(R("xb"), R("IN1", o1 + 64, o1 + 128))
-        cp(pb(XP, 0, 64), R("IN1", o1 + 64, o1 + 128))
-        nearest(0, 0, 64, R("xu", 0, 4), HW, PAR["SPL"])
-        fw, fb = pb(ZB[0], 256, 260), pb(DBK, 256, 320)
-        b2w(fw, "C", 0, 64)
-        mm([(fb, R("BL16"), R("C", 0, 64))])
-        fu = R("xu", 4, 8)
+        tag[0] = "come"
+        xin, din = R("IN1", o1 + 64, o1 + 128), R("IN1", o1 + 128, o1 + 192)
+        ts(R("xu", 0, 4), R("IN1", o1 + 15, o1 + 64, 16), FW, None, A.add)
+        cp(pb(XP, 256, 320), xin)
+        nearest(0, 64, R("xu", 0, 4), HW, 4096.0, 256, 1024, 768, 256, PAR["SPL"], 390)
+        fy, fb, cy, cb = pb(KZ[0], 256, 320), pb(KZ[0], 320, 384), pb(KZ[0], 384, 448), pb(KZ[0], 448, 512)
+        mm([(fy, R("Ib"), R("PP", 0, 64)), (fy, R("BLb"), R("C", 768, 832))])
+        mm([(fb, R("BLb"), R("C", 768, 832))])
+        scan(R("FS", 0, 64), R("RSn", 0, 64), fy, 0.0, A.add, A.max)
+        fu, fw = R("xu", 4, 8), R("FS", 15, 64, 16)
         ts(fu, fw, EOFF, None, A.add)
-        cp(x4(3), fw)
-        tt(R("xg"), IND(XW, fu), R("IN1", o1 + 128, o1 + 192), A.is_ge)
-        tt(R("xd"), IND(XW, fu), R("xb"), A.subtract)
-        b2w(pb(ZB[1], 256, 260), "xg", 0, 64)
+        tt(R("xg"), IND(XW, fu), din, A.is_ge)
+        tt(R("xd"), IND(XW, fu), xin, A.subtract)
         for c in range(4):
-            ts(R("EQ", 256 + 64 * c, 320 + 64 * c), fb, R("e0s", c, c + 1), None, A.is_equal)
-        ts(x4(4), pb(ZB[1], 256, 260), need, None, A.is_ge)
-        tt(x4(5), x4(4), x4(3), A.mult)
-        pairs(4, [(pb(ACC, 0, 64), R("BL4"), R("EQ", 256 + 64 * c, 320 + 64 * c)) for c in range(4)],
-              lambda o, c: ts(o, pb(DBK, 256 + 16 * c, 320), R("xs4", 20 + c, 21 + c), None, A.is_equal))
-        tt(R("xp", 0, 64), pb(ACC, 0, 64), R("THH", 0, 64), A.is_ge)
-        tt(R("xp", 64, 128), pb(ACC, 0, 64), R("THR", 0, 64), A.is_lt)
-        tt(R("xq"), R("xp", 0, 64), R("xp", 64, 128), A.mult)
+            ts(R("EX", 160 + 64 * c, 224 + 64 * c), fb, R("xs4", 20 + c, 21 + c), None, A.is_equal)
+        acc = pb(KZ[1], 0, 64)
+        mm([(acc, R("Ib"), R("THn", 0, 64))] + [(acc, R("BL4"), R("EX", 160 + 64 * c, 224 + 64 * c)) for c in range(4)], sp=False)
+        mm([(cy, R("Ib"), R("NP")), (cy, R("BLb"), R("xg"))])
+        mm([(cb, R("BLb"), R("xg"))])
+        scan(R("FS", 64, 128), R("R01"), cy, 0.0, A.mult, A.max)
+        ts(R("nb"), cb, need, None, A.is_lt)
+        mm([(acc, R("BL4"), R("nb"))], st=False, sp=False)
+        mm(pairs(4, KZ[1], "EX", lambda o, c: ts(o, pb(KZ[0], 320 + 16 * c, 384), R("FS", 15 + 16 * c, 16 + 16 * c), R("FS", 79 + 16 * c, 80 + 16 * c),
+                                                 A.is_equal, A.min)), st=False)
+        ts(R("xq"), acc, 0.0, None, A.is_lt)
         o2 = 64 * t
         tt(R("OUT2", o2, o2 + 64), R("xq"), R("xd"), A.mult)
         swap(R("IN2", o2, o2 + 64), R("OUT2", o2, o2 + 64), src, dst, "a2_%d" % t)
-        b2w(pb(ZB[1], 264, 268), "xq", 0, 64)
-        ts(x4(6), pb(ZB[1], 264, 268), 1.0, None, A.is_lt)
-        tt(x4(7), x4(6), R("DX1"), A.mult)
-        act(x4(8), x4(3), F.Identity, EOFF)
-        tt(x4(9), x4(7), x4(8), A.max)
-        cp(R("xo"), x4(9))
-        cp(IND(R("X"), R("xo")), R("xb"))
+        tag[0] = "take"
+        mm(b2w(pb(DK, 16, 20), "xq", 0, 64))
+        ts(x4(1), pb(DK, 16, 20), -512.0, 8192.0 + EOFF, A.mult, A.add)
+        tt(x4(2), x4(1), fw, A.add)
+        tt(x4(3), x4(2), R("DX", 0, 4), A.min)
+        cp(R("xo"), x4(3))
+        cp(IND(R("X"), R("xo")), xin)
+        tag[0] = "back"
         tt(IND(R("X"), R("e0u")), R("x0s"), R("IN2", o2, o2 + 64), A.add)
-    dma("Y", "dy0", T.yx[:, 0:2048], T.X[:, 0:2048], [], [XW], 4000)
-    dma("S", "dy1", T.yx[:, 2048:P], T.X[:, 2048:P], [], [XW], 4000)
+    dma("Y", "dy0", T.yx[:, 0:2048], T.X[:, 0:2048], [], [XW], 5800)
+    dma("S", "dy1", T.yx[:, 2048:P], T.X[:, 2048:P], [], [XW], 5800)
 
     emit(g, T, ops)
 
 
-def plan(ops, deps, succ, pr, delay, marg, fr):
-    n = len(ops)
+def plan(ops, deps, succ, pr, delay):
+    n, hop = len(ops), PAR["HOP"]
     left = [len(d) for d in deps]
-    pool = {}
-    for k in range(n):
-        if left[k] == 0:
-            pool.setdefault(ops[k]["eng"], []).append(k)
-    rt, fin, free, order, end = [0.0] * n, [0.0] * n, {}, [], 0.0
-    while len(order) < n:
-        t0, e = min((max(free.get(e, 0.0), min(rt[k] for k in p)), e) for e, p in pool.items() if p)
-        p = pool[e]
-        pick = None
-        for k in sorted((k for k in p if rt[k] <= t0), key=lambda k: -pr[k]):
-            if not any(rt[j] > t0 and pr[j] > pr[k] + marg and rt[j] - t0 < fr * ops[k]["cost"] for j in p):
-                pick = k
-                break
-        if pick is None:
-            free[e] = min(rt[j] for j in p if rt[j] > t0)
-            continue
-        p.remove(pick)
-        order.append(pick)
-        fin[pick] = free[e] = t0 + ops[pick]["cost"]
-        end = max(end, free[e] + ops[pick].get("lat", 0))
-        for j in succ[pick]:
-            rt[j] = max(rt[j], free[e] + delay(pick, j))
+    ready = sorted((-pr[k], k) for k in range(n) if left[k] == 0)
+    rt, sta, fin, busy, end = [0.0] * n, [0.0] * n, [0.0] * n, {}, 0.0
+
+    def place(lst, x):
+        lo, hi = 0, len(lst)
+        while lo < hi:
+            m = (lo + hi) // 2
+            if lst[m] < x:
+                lo = m + 1
+            else:
+                hi = m
+        return lo
+
+    while ready:
+        k = ready.pop(0)[1]
+        e, c, t = ops[k]["eng"], ops[k]["cost"], rt[k]
+        moved = c > 0
+        while moved:
+            moved = False
+            for r in [e] + ops[k]["banks"]:
+                lst = busy.setdefault(r, [])
+                i = max(0, place(lst, (t,)) - (1 if r == e else 6))
+                while i < len(lst) and lst[i][0] < t + c + hop:
+                    s, f, e2 = lst[i]
+                    gap = 0.0 if r == e else hop
+                    if (r == e or e2 != e) and s < t + c + gap - 1e-6 and t < f + gap - 1e-6:
+                        t, moved = f + gap, True
+                    i += 1
+        sta[k], fin[k] = t, t + c
+        if c > 0:
+            for r in [e] + ops[k]["banks"]:
+                busy[r].insert(place(busy[r], (t,)), (t, t + c, e))
+        end = max(end, t + c + ops[k].get("lat", 0))
+        for j in succ[k]:
+            rt[j] = max(rt[j], t + c + delay(k, j))
             left[j] -= 1
             if left[j] == 0:
-                pool.setdefault(ops[j]["eng"], []).append(j)
-    return end, order, fin
+                ready.insert(place(ready, (-pr[j], j)), (-pr[j], j))
+    return end, sta, fin
 
 
 def emit(g, T, ops):
     n = len(ops)
-    if "order" not in PLAN:
-        seen, deps = {}, []
+    for o in ops:
+        o["banks"] = sorted(set(name for name, lo, hi in o["rd"] + o["wr"] if name.startswith("pb")))
+    if "graph" not in PLAN:
+        seen, deps, soft = {}, [], []
         for k, o in enumerate(ops):
-            d = set()
+            d, sf = set(), set(o.get("soft", []))
             for w, rgs in ((0, o["rd"]), (1, o["wr"])):
                 for name, lo, hi in rgs:
-                    ps = name.startswith("pb")
                     for k2, w2, lo2, hi2 in seen.get(name, []):
-                        if (ps and ops[k2]["eng"] != o["eng"]) or ((w or w2) and lo < hi2 and lo2 < hi):
-                            d.add(k2)
+                        if (w or w2) and lo < hi2 and lo2 < hi:
+                            inq = w and not w2 and PAR["WQ"] and ops[k2]["eng"] == o["eng"] and o["eng"] in "VS" and "sem" not in o and "sem" not in ops[k2]
+                            (sf if inq else d).add(k2)
             if "after" in o:
                 d.add(o["after"])
             for w, rgs in ((0, o["rd"]), (1, o["wr"])):
                 for name, lo, hi in set(rgs):
                     seen.setdefault(name, []).append((k, w, lo, hi))
             deps.append(sorted(d))
+            soft.append(sf - d)
         anc, red = [], []
         for k in range(n):
             m, keep = 0, []
-            for j in reversed(deps[k]):
+            for j in sorted(deps[k] + list(soft[k]), reverse=True):
                 if not m >> j & 1:
                     keep.append(j)
                 m |= anc[j] | 1 << j
@@ -530,22 +669,29 @@ def emit(g, T, ops):
         for k in range(n):
             for j in red[k]:
                 succ[j].append(k)
-        fwd = lambda k, j: ops[k].get("lat", 0) + (0 if ops[k]["eng"] == ops[j]["eng"] == "PE" else PAR["HOP"])
+        PLAN["graph"] = deps, red, succ, soft
+    if "order" not in PLAN:
+        deps, red, succ, soft = PLAN["graph"]
+        fwd = lambda k, j: ops[k].get("lat", 0) + (0 if ops[k]["eng"] == ops[j]["eng"] == "PE" or k in soft[j] else PAR["HV" if ops[k]["eng"] == "V" else "HOP"])
         bwd = lambda k, j: fwd(j, k)
-        pr0 = [0.0] * n
+        pr0, est = [0.0] * n, [0.0] * n
         for k in range(n - 1, -1, -1):
             pr0[k] = ops[k]["cost"] + max([pr0[j] + fwd(k, j) for j in succ[k]] + [ops[k].get("lat", 0)])
-        best = None
-        for fr in (PAR["FR"], 2 * PAR["FR"]):
-            pr = pr0
+        for k in range(n):
+            est[k] = max([est[j] + ops[j]["cost"] + fwd(j, k) for j in red[k]] + [0.0])
+        best, tot = None, max(pr0)
+        for lam in PAR["LAM"]:
+            pr = [(1 - lam) * pr0[k] + lam * (tot - est[k]) for k in range(n)]
             for it in range(PAR["IT"]):
-                res = plan(ops, red, succ, [max(pr[k], ops[k].get("pri", 0)) for k in range(n)], fwd, PAR["MARG"], fr)
+                res = plan(ops, red, succ, [max(pr[k] + PAR["URG"].get(ops[k]["tag"], 0), ops[k].get("pri", 0)) for k in range(n)], fwd)
                 if best is None or res[0] < best[0]:
                     best = res
-                pr = plan(ops, succ, red, res[2], bwd, PAR["MARG"], fr)[2]
-        PLAN["order"], PLAN["deps"], PLAN["end"] = best[1], deps, best[0]
+                if it + 1 < PAR["IT"]:
+                    back = plan(ops, succ, red, res[2], bwd)
+                    pr = [(1 - PAR["MIX"]) * back[2][k] + PAR["MIX"] * (res[0] - res[1][k]) for k in range(n)]
+        PLAN["order"], PLAN["deps"], PLAN["end"] = sorted(range(n), key=lambda k: (best[1][k], k)), deps, best[0]
     Q = {"V": g.vector, "S": g.scalar, "PE": g.tensor, "G": g, "Y": g.sync}
-    cnt, mark, known, sent = {}, {}, {}, 0
+    cnt, mark, known, sent, bank = {}, {}, {}, 0, {}
     for k in PLAN["order"]:
         o = ops[k]
         e = o["eng"]
@@ -553,7 +699,8 @@ def emit(g, T, ops):
             mark[k] = (o["sem"], o["val"])
             continue
         want = {}
-        for j in PLAN["deps"][k]:
+        others = [j for b in o["banks"] for e2, j in bank.get(b, {}).items() if e2 != e]
+        for j in PLAN["deps"][k] + others:
             if j not in mark or (e == "PE" and ops[j]["eng"] == "PE"):
                 continue
             s, v = mark[j]
@@ -563,6 +710,8 @@ def emit(g, T, ops):
                 Q[e].wait_ge(T.sem[s], v)
                 known[(e, s)] = v
         ins = o["fn"]()
+        for b in o["banks"]:
+            bank.setdefault(b, {})[e] = k
         if "remote" in o:
             sent += o["remote"]
         elif "sem" in o:

@@ -3,37 +3,34 @@ from concourse.mybir import AluOpType as A, AxisListType, ActivationFunctionType
 P, H, S, RO, CAP = 4096, 1536, 256, 3, 64
 F32, BF, F16, I32, U16 = "float32", "bfloat16", "float16", "int32", "uint16"
 SB = {
-    "X": (P + 64, BF), "HLi": (H, I32), "HL": (2 * H + 1024, F32), "DV": (16, F32), "HLo": (H, F32), "WT": (P + 768, F32), "wi": (256, I32), "w16": (256, F16),
-    "hoi": (48, I32), "hou": (48, U16), "DM": (816, BF), "VT": (H + 256, F32),
+    "X": (P + 64, BF), "HLi": (H, I32), "HL": (2 * H + 1024, F32), "WT": (P + 768, F32), "VT": (H + 256, F32), "DM": (1632, BF),
+    "wi": (256, I32), "w16": (256, F16), "hoi": (48, I32), "hou": (48, U16),
     "ONE": (128, F32), "IDf": (128, F32), "BLf": (128, F32), "Ib": (128, BF), "In": (128, BF), "I8": (128, BF), "I8n": (128, BF),
     "BLb": (128, BF), "BL4": (128, BF), "POW": (128, BF), "ONEb": (128, BF), "G2": (16, BF),
     "Z": (144, BF), "Zn": (144, BF), "Zt": (432, BF), "Dt": (384, BF), "BT": (384, BF), "LT": (2048, BF), "THn": (256, BF), "th": (512, BF),
-    "RST": (128, F32), "RSn": (128, F32), "R01": (64, F32), "PW": (128, F16), "PX": (64, F32), "PP": (128, BF), "NP": (64, BF), "NN": (16, BF),
-    "pi": (2, I32), "q16": (128, F32), "dq": (384, F32), "M16": (16, F32), "col": (16, F32), "lasti": (8, I32), "last": (8, U16),
-    "SW": (64, F32), "DL": (64, F32), "DW": (48, F32), "DX": (12, F32), "CODE": (256, F32), "need": (4, F32), "ni": (2, I32),
+    "RST": (128, F32), "R01": (64, F32), "PW": (128, F16), "PX": (64, F32), "PP": (64, BF), "NP": (64, BF), "NN": (16, BF),
+    "pi": (2, I32), "q16": (128, F32), "dq": (384, F32), "M16": (16, F32), "col": (16, F32),
+    "SW": (64, F32), "DL": (64, F32), "DV": (16, F32), "DW": (48, F32), "DX": (12, F32), "CODE": (256, F32), "need": (4, F32), "ni": (2, I32),
     "Aa": (2048, BF), "Ab": (2048, BF), "Ma": (2048, BF), "Mb": (2048, BF), "ma": (128, F32), "mb": (128, F32),
-    "Ua": (520, BF), "Ub": (390, BF), "LSu": (320, U16), "LS": (1088, F16), "C": (832, F16), "PR": (256, F16), "PRf": (256, F32),
-    "ES": (256, F32), "NEW": (1024, F32),
-    "JB": (768, F16), "GE": (768, BF), "SCN": (256, F16), "X0": (272, BF), "H4": (264, F32), "E0": (264, F32),
+    "Ua": (520, BF), "Ub": (390, BF), "LSu": (320, U16), "LS": (1088, F16), "C": (832, F16),
+    "JB": (768, F16), "GE": (768, BF), "SCN": (256, F16), "H4": (256, F32), "E0": (264, F32),
     "eu": (64, U16), "hu": (64, U16), "hp": (64, F32), "ef": (48, F32), "hs": (16, F32), "nup": (32, BF), "dB": (48, F32), "pB": (32, F32),
-    "t1": (128, F32), "t2": (160, F32), "hD": (64, F32), "bs": (64, F32), "lof": (64, F32), "lo": (64, U16),
-    "val": (48, F16), "t3": (144, F32), "wo": (48, U16), "vo": (16, U16), "HM": (768, F32),
-    "EQ": (2176, BF), "EX": (416, BF), "VB": (256, BF), "DB": (256, BF), "FB": (256, BF), "PF": (256, BF), "junk": (1040, BF),
-    "sa": (12, F32), "ixu": (4, U16), "h4c": (64, F16), "e0c": (128, F32), "FS": (128, F32),
-    "OUT1": (576, F16), "IN1": (576, F16), "OUT2": (192, BF), "IN2": (192, BF), "x0s": (64, BF),
-    "e0u": (4, U16), "xs4": (24, F32), "xu": (8, U16), "xg": (64, BF), "xd": (64, BF), "nb": (64, BF), "xq": (64, BF), "xo": (4, U16),
+    "EQ": (2176, BF), "VB": (256, BF), "DB": (256, BF), "vo": (16, U16),
+    "PR": (1024, F32), "NEW": (1024, F32), "HM": (768, F32), "t1": (128, F32), "t2": (144, F32), "t3": (144, F32),
+    "hD": (64, F32), "bs": (64, F32), "lof": (64, F32), "lo": (64, U16), "val": (48, F16), "wo": (48, U16),
+    "FB": (256, BF), "PF": (256, BF), "junk": (1040, BF), "sa": (12, F32), "ixu": (72, U16), "e0c": (128, F32), "FS": (128, F32),
+    "IN0": (1632, BF), "INI": (72, U16), "LA": (264, F32), "xin": (128, BF), "OUT2": (192, BF), "IN2": (192, BF), "x0s": (64, BF),
+    "EX": (416, BF), "e0u": (4, U16), "xs4": (24, F32), "fu": (4, U16), "xg": (64, BF), "xd": (64, BF), "nb": (64, BF), "xq": (64, BF), "xo": (4, U16),
 }
 SCRATCH = {k: ("sbuf", [128, w], d) for k, (w, d) in SB.items()}
 for _b in range(8):
     SCRATCH["pb%d" % _b] = ("psum", [128, 512], F32)
-SCRATCH["pb6"] = ("psum", [128, 1024], BF)
-DMAS = ["dho", "dhl", "dwr", "ddm0", "ddm1", "ddm2", "dx0", "dx1", "dyl", "dyw", "dw2", "dy0", "dy1"]
-SEMAPHORES = ["V", "S", "PE", "G", "sent"] + DMAS + ["a1_%d" % t for t in range(RO)] + ["a2_%d" % t for t in range(RO)]
+DMAS = ["dho", "dhl", "dwr", "ddm0", "ddm1", "ddm2", "dx", "dyl", "dyw", "dw2", "dyx"]
+SEMAPHORES = ["V", "S", "PE", "G", "sent"] + DMAS + ["a%d_%d" % (k, t) for k in range(3) for t in range(RO)]
 
-PAR = dict(GA=1.56, SC=3.8, HOP=100.0, PEC=0.5, NET=3000.0, DMAL=2400.0,
-           SPL=24, SPS=(40, 0, 0, 0, 0, 0), GS=(0, 64), NQ=2, IT=3, MIX=0.3, LAM=(0.2, 0.4, 0.6), NE=8, WQ=0, UM="R",
-           HLE="SS", HG=((0, 2, 4), (0, 4)), WTE="SSSSSS", WG=(0, 2, 4, 6), HV=300.0, PRE="VVVV", FBE="V", EB="PPPPSS",
-           URG={})
+PAR = dict(GA=1.4, SC=3.0, HOP=200.0, HV=270.0, FS=90.0, PEC=0.42, NET=3600.0, DMAL=2400.0, KB=4.0, IT=4, MIX=0.0, LAM=(0.4,),
+           SPL=32, SPS=32, HG=((0, 4), (0, 4)),
+           URG={'faila': -750, 'x0a': 3400, 'own': 3250, 'hj': 2850, 'first': 1900, 'lists': -600, 'lista': -3150, 'die1': -950, 'die3': 450, 'x0b': -2300, 'up1': -250, 'climb1a': -250, 'die2': -150, 'take': 800, 'new0': -2050, 'mark1': 1350, 'come': -2100, 'mark2': -550, 'warr': 650, 'up2': 150, 'set': 150, 'climb2b': -150, 'new1': 1200, 'hm': -3850, 'odd': -800, 'mark0': -400, 'climb3a': 300, 'where': -1350, 'yl': -1650, 'send': 300, 'payb': -700, 'climb2a': 300, 'climb3b': 150, 'mark00': -400, 'paya': -600})
 PLAN = {}
 
 
@@ -49,7 +46,7 @@ def rank_program(g, core, T, topo):
         hi = T[name].shape[1] if hi is None else hi
         ap = T[name][:, lo:hi:step] if step > 1 else T[name][:, lo:hi]
         return dict(ap=ap, rg=[(name, lo, hi)], n=len(range(lo, hi, step)), ps=name.startswith("pb"),
-                    b2=name == "pb6" or SB.get(name, (0, F32))[1] in (BF, F16, U16), ind=False)
+                    b2=SB.get(name, (0, F32))[1] in (BF, F16, U16), ind=False)
 
     def REV(x):
         name, lo, hi = x["rg"][0]
@@ -99,7 +96,7 @@ def rank_program(g, core, T, topo):
         add("V", lambda: g.vector.tensor_reduce(out["ap"], a["ap"], AxisListType.X, A.add), [out], [a], max(64, a["n"]))
 
     def act(out, a, f=F.Copy, bias=0.0, scale=1.0, acc=None):
-        c = 80 + SC * a["n"] if out["ind"] else 80 + GA * a["n"] if a["ind"] else max(64, a["n"]) + (24 if acc else 0)
+        c = PAR["FS"] + (80 + SC * a["n"] if out["ind"] else 80 + GA * a["n"] if a["ind"] else max(64, a["n"]) + (24 if acc else 0))
         if out["ind"]:
             add("S", lambda: g.scalar.activation(out["ap"], a["ap"], f), [out], [a], c)
         elif acc:
@@ -114,7 +111,7 @@ def rank_program(g, core, T, topo):
                 ins = g.tensor.matmul(o["ap"], l["ap"], r["ap"], each or (st and k == 0), each or (sp and k == len(lst) - 1))
             return ins
         add("PE", fn, [o for o, l, r in lst], [x for o, l, r in lst for x in (l, r)],
-            sum(PEC * max(64, r["n"]) * (1 if r["b2"] else 4) for o, l, r in lst))
+            sum(PEC * max(min(64, l["n"]), r["n"]) * (1 if r["b2"] else 4) for o, l, r in lst))
 
     def b2w(out, name, lo, hi, Z="Z", z0=0):
         return [(out, R(Z, z0 + 15 - r, z0 + 143 - r), R(name, lo + r, hi, 16)) for r in range(16)]
@@ -133,39 +130,48 @@ def rank_program(g, core, T, topo):
 
     def dma(q, sem, out, in_, outs, ins, kb, first=False):
         e = g.sync if q == "Y" else g.scalar
-        add(q, lambda: e.dma_start(out, in_), outs, ins, 60, sem=sem, lat=PAR["DMAL"] + kb, pri=(1e9 - len(ops) if first else 0))
+        add(q, lambda: e.dma_start(out, in_), outs, ins, 60, sem=sem, lat=PAR["DMAL"] + PAR["KB"] * kb, pri=(1e9 - len(ops) if first else 0))
 
     def swap(land, out, dst, src, sem):
         rid, pid, _ = topo.addr(dst)
-        eng = topo.engines(core, dst)[:PAR["NE"]]
-        m = sum(1 << e for e in eng)
-        add("G", lambda: g.remote_dma(land["ap"], out["ap"], T.sem[sem], T.sem.sent, pid, rid, m), [], [out], 300, remote=len(eng))
-        add("N", None, [land], [], 0, sem=sem, val=len(topo.engines(src, core)[:PAR["NE"]]), lat=PAR["NET"] - PAR["HOP"], after=len(ops) - 1)
+        add("G", lambda: g.remote_dma(land["ap"], out["ap"], T.sem[sem], T.sem.sent, pid, rid, topo.mask(core, dst)), [], [out], 300,
+            remote=len(topo.engines(core, dst)))
+        add("N", None, [land], [], 0, sem=sem, val=len(topo.engines(src, core)), lat=PAR["NET"] - PAR["HOP"], after=len(ops) - 1)
 
     pb = lambda b, lo=0, hi=512, st=1: R("pb%d" % b, lo, hi, st)
     KZ, ACC, DK, GK, P0, XP, P1 = (0, 1), 2, 3, 4, 5, 6, 7
 
-    dma("Y", "dho", T.hoi[:], T.ho[:], [R("hoi")], [], 140, True)
-    dma("S", "dwr", T.wi[:], T.wr[:], [R("wi")], [], 860, True)
-    dma("Y", "dhl", T.HLi[:], T.hl[:], [R("HLi")], [], 5170, True)
-    dma("Y", "dx0", T.X[:, 0:2048], T.xs[:, 0:2048], [R("X", 0, 2048)], [], 8000, True)
-    dma("Y", "dx1", T.X[:, 2048:P], T.xs[:, 2048:P], [R("X", 2048, P)], [], 10880, True)
+    dma("Y", "dho", T.hoi[:], T.ho[:], [R("hoi")], [], 24, True)
+    dma("S", "dwr", T.wi[:], T.wr[:], [R("wi")], [], 152, True)
+    dma("Y", "dhl", T.HLi[:], T.hl[:], [R("HLi")], [], 920, True)
+    dma("Y", "dx", T.X[:, 0:P], T.xs[:], [R("X", 0, P)], [], 1944, True)
     for t in range(RO):
-        dma("Y", "ddm%d" % t, T.DM[:, 272 * t:272 * t + 256], T.dm[:, 256 * t:256 * t + 256], [R("DM", 272 * t, 272 * t + 256)], [],
-            11200 + 300 * t, True)
+        d0 = 544 * t + 272
+        dma("Y", "ddm%d" % t, T.DM[:, d0:d0 + 256], T.dm[:, 256 * t:256 * t + 256], [R("DM", d0, d0 + 256)],
+            [R("X", 0, P)] if t else [], 64 if t else 2008, True)
 
     col = lambda k: R("col", k, k + 1)
-    QC, PWc, SCL, FW, FX = col(0), col(1), col(2), col(3), col(4)
+    QC, PWc, SCL, FW, FX, SC2, N4 = col(0), col(1), col(2), col(3), col(4), col(6), col(7)
+    fill = lambda out, v: iota(out, [[0, out["n"]]], v, 0)
     ms(R("ONE"), 1.0)
     iota(R("pi", 0, 1), [[0, 1]], 0, 1, False)
+    iota(R("q16"), [[0, 8], [1, 16]], 0, 0)
     asel(R("dq", 0, 128), R("ONE"), [[-16, 8], [0, 16]], A.is_ge, 0, 1)
     asel(R("BLf"), R("dq", 0, 128), [[16, 8], [0, 16]], A.is_ge, 15, -1)
-    iota(R("q16"), [[0, 8], [1, 16]], 0, 0)
     asel(R("IDf"), R("ONE"), [[-1, 128]], A.is_equal, 0, 1)
-    iota(R("lasti"), [[16, 8]], 15, 0, False)
     iota(R("SW"), [[16, 64]], 0, 0)
-    iota(R("CODE"), [[0, 256]], 1, 0)
-    iota(R("VT"), [[0, H + 256]], 0, 0)
+    tag[0] = "fill"
+    fill(R("CODE"), 1)
+    fill(R("VT"), 0)
+    fill(R("BT"), 0)
+    for t in range(RO):
+        fill(R("DM", 544 * t + 256, 544 * t + 272), 0)
+        fill(R("DM", 544 * t + 528, 544 * t + 544), 256)
+    fill(R("LA", 256, 264), 0)
+    for a in range(2):
+        fill(R("PR", 512 * a, 512 * a + 128), 0)
+    fill(R("E0", 256, 264), 8192)
+    tag[0] = "set"
     ts(R("pi", 1, 2), R("pi", 0, 1), 15, None, A.bitwise_and)
     cp(QC, R("pi", 1, 2))
     ts(R("M16"), R("q16", 0, 16), QC, None, A.is_equal)
@@ -184,26 +190,29 @@ def rank_program(g, core, T, topo):
         else:
             act(R("WT", 512 * b, 512 * b + 512), pb(k0), F.Identity, 4096.0)
     cp(R("hou"), R("hoi"))
-    for k in range(4):
-        ts(R("HL", 384 * k, 384 * k + 384), R("HLi", 384 * k, 384 * k + 384), 4096.0, None, A.add)
+    tag[0] = "lists"
+    for k in range(8):
+        cp(R("HL", 192 * k, 192 * k + 192), R("HLi", 192 * k, 192 * k + 192))
+    tag[0] = "set"
+    aff = lambda out, x, m, c=0.0: ts(out, x, m, c, A.mult, A.add)
     ms(R("Z"), 0.0)
     cp(R("Z", 15, 143, 16), R("BLf", 0, 128, 16))
-    act(R("Zn"), R("Z"), scale=-4096.0)
-    ms(R("BT"), 0.0)
-    for t in range(RO):
-        MT = R("M16", t, t + 1)
-        act(R("Zt", 144 * t, 144 * t + 144), R("Z"), F.Identity, 0.0, MT)
-        ts(col(8 + t), MT, -1.0, 1.0, A.mult, A.add)
-        act(R("Dt", 128 * t, 128 * t + 128), R("IDf"), F.Identity, 0.0, col(8 + t))
-        act(R("BT", 128 * t + t, 128 * t + 128, 16), R("BLf", 0, 128, 16))
-        ts(col(12 + t), MT, 30720.0, 6144.0, A.mult, A.add)
-    for k, v in ((0, 2.0), (8, -1.0)):
-        act(R("G2", k, k + 8), R("BLf", 0, 128, 16), scale=v)
+    aff(R("Zn"), R("Z"), -4096.0)
+    aff(R("col", 8, 11), R("M16", 0, 3), -1.0, 1.0)
+    aff(R("col", 12, 15), R("M16", 0, 3), 30720.0, 2048.0)
     for nm, v in (("I8", 8192.0), ("I8n", -8192.0), ("Ib", 1.0), ("In", -1.0)):
         act(R(nm), R("IDf"), scale=v)
+    for t in range(RO):
+        aff(R("Zt", 144 * t, 144 * t + 144), R("Z"), R("M16", t, t + 1))
+        aff(R("Dt", 128 * t, 128 * t + 128), R("Ib"), col(8 + t))
+        cp(R("BT", 128 * t + t, 128 * t + 128, 16), R("BLf", 0, 128, 16))
+    for k, v in ((0, 2.0), (8, -1.0)):
+        aff(R("G2", k, k + 8), R("BLf", 0, 128, 16), v)
     act(R("BLb"), R("BLf"))
-    act(R("BL4"), R("BLf"), scale=4.0)
-    act(R("ONEb"), R("ONE"))
+    aff(R("BL4"), R("BLb"), 4.0)
+    ms(R("ONEb"), 1.0)
+    ts(R("RST"), R("q16"), 0.5, 1e6, A.is_lt, A.mult)
+    ts(R("R01"), R("q16", 0, 64), 0.5, None, A.is_gt)
     ms(R("th", 0, 256), 0.25)
     ms(R("th", 256, 512), 0.0)
     ms(R("th", 256, 512, 16), -2.0)
@@ -211,71 +220,60 @@ def rank_program(g, core, T, topo):
     ms(R("th", 0, 256), 0.0)
     tt(R("t1", 0, 16), R("THn", 0, 16), R("M16"), A.mult)
     red(col(5), R("t1", 0, 16))
-    ts(PWc, col(5), -0.5, None, A.mult)
-    act(R("POW"), R("BLf"), F.Identity, 0.0, PWc)
-    ts(SCL, QC, 0.5, -8192.0, A.is_gt, A.mult)
-    ts(FW, QC, 14.5, 1536.0, A.is_lt, A.mult)
-    ts(FX, QC, 14.5, 16384.0, A.is_lt, A.mult)
-    ms(R("RST"), 0.0)
-    ms(R("RST", 0, 128, 16), 1e6)
-    act(R("RSn"), R("RST"), scale=-1.0)
-    act(R("R01"), R("RST", 0, 64), F.Relu, 1.0, -1.0)
+    ts(R("POW"), R("BLb"), col(5), -0.5, A.mult, A.mult)
+    aff(SCL, R("M16", 0, 1), 8192.0, -8192.0)
+    aff(SC2, R("M16", 0, 1), 8192.0, -6144.0)
+    aff(FW, R("M16", 15, 16), -1536.0, 1536.0)
+    aff(FX, R("M16", 15, 16), -16384.0, 16384.0)
     ts(R("dq", 0, 128), R("q16"), QC, None, A.subtract)
     ts(R("dq", 128, 256), R("dq", 0, 128), 0.5, 4096.0, A.is_lt, A.mult)
     ts(R("dq", 256, 384), R("dq", 0, 128), 1.0, -1536.0, A.is_equal, A.mult)
     tt(R("PW"), R("dq", 128, 256), R("dq", 256, 384), A.add)
-    ts(R("PP"), R("dq", 0, 128), 0.0, -65536.0, A.not_equal, A.mult)
-    ts(R("dq", 128, 192), R("dq", 0, 64), 0.5, 32768.0, A.is_lt, A.mult)
-    ts(R("dq", 256, 320), R("dq", 0, 64), 1.0, -16384.0, A.is_equal, A.mult)
-    tt(R("PX"), R("dq", 128, 192), R("dq", 256, 320), A.add)
-    cp(R("last"), R("lasti"))
+    ts(R("PP"), R("dq", 0, 64), 0.0, -65536.0, A.not_equal, A.mult)
+    ts(R("PX"), R("PW", 0, 64), 16384.0 / 1536, None, A.mult)
     ts(R("SW"), R("SW"), QC, None, A.add)
-    act(R("DL"), R("SW"), F.Identity, 2.0 * H)
-    act(R("DV"), R("SW", 0, 16), F.Identity, float(H))
-    ts(col(6), SCL, 2048.0, None, A.add)
-    act(R("DW"), R("SW", 0, 48), F.Identity, P - 2048.0)
-    act(R("DX", 0, 4), R("SW", 0, 4), F.Identity, float(P))
+    aff(R("DL"), R("SW"), 1.0, 2.0 * H)
+    aff(R("DV"), R("SW", 0, 16), 1.0, float(H))
+    aff(R("DW"), R("SW", 0, 48), 1.0, P - 2048.0)
+    aff(R("DX", 0, 4), R("SW", 0, 4), 1.0, float(P))
     ts(R("DX", 4, 8), R("DX", 0, 4), FX, None, A.subtract)
-    act(R("DX", 8, 12), R("SW", 0, 4), F.Identity, 1.0, 2.0)
-    ms(R("Ua"), 1.0)
-    ms(R("Ub"), 1.0)
+    aff(R("DX", 8, 12), R("SW", 0, 4), 2.0, 1.0)
+    ms(R("Ua", 1, 520, 130), 1.0)
+    ms(R("Ub", 1, 390, 130), 1.0)
     ms(R("need", 0, 1), 9.0)
-    for t in range(RO):
-        ms(R("DM", 272 * t + 256, 272 * t + 272), 256.0)
-    ms(R("X0", 256, 272), 0.0)
-    ms(R("H4", 256, 264), 0.0)
-    ms(R("E0", 256, 264), 8192.0)
+    ms(R("ixu"), 0.0)
 
     XW, HW, WW = R("X", 0, P), R("HL", 0, H), R("WT", 0, P)
     EOFF, RND = 32768.0, 2.0 ** 23 - 4096
     gat = []
 
-    def nearest(a, n, hoff, hw, sub, lu, ls, cc, xp, split, uo):
+    def nearest(a, n, hoff, hw, lu, ls, cc, xp, split, uo):
         An, Mn, mn, Un = ("Aa", "Ma", "ma", "Ua") if a == 0 else ("Ab", "Mb", "mb", "Ub")
-        ts(R("LSu", lu, lu + n), IND(hw, hoff), -sub, None, A.add)
+        cp(R("LSu", lu, lu + n), IND(hw, hoff))
         ts(R("LS", ls, ls + n), R("LSu", lu, lu + n), -2048.0, None, A.add)
         ns = n - split
-        cuts = [u for u in PAR["GS"] if u < ns] + [ns] if n == 128 else [0, ns]
+        cuts = [u for u in (0, 64, 96) if u < ns] + [ns]
         for u, v in zip(cuts, cuts[1:]):
             act(R(An, 16 * u, 16 * v), IND(XW, R("LSu", lu + u, lu + v)))
             ops[-1]["soft"] = gat[-1:]
             gat.append(len(ops) - 1)
         if split:
             cp(R(An, 16 * ns, 16 * n), IND(XW, R("LSu", lu + ns, lu + n)))
-        nq = n // PAR["NQ"] if n == 128 else n
-        for u in range(0, n, nq):
-            for j in range(16):
-                o = pb(KZ[a], j, 128, 16)
-                tt(R(Mn, 128 * j + u, 128 * j + u + nq), R(An, 16 * u + j, 16 * (u + nq), 16), pb(XP, xp + u, xp + u + nq), A.max)
-                if u + nq == n:
-                    mm([(o, R(An, j, 2048, 16), R("G2", 8, 16)), (o, R(Mn, 128 * j, 128 * j + 128), R("G2", 0, 8))])
+        mm([(pb(KZ[a], 0, 128), R("Ib"), R("th", 0, 128))], sp=False)
+        ops[-1]["wr"].append(("pb%d" % KZ[a], 0, 512))
+        mm([(pb(KZ[a], j, 128, 16), R(An, j, 2048, 16), R("G2", 8, 16)) for j in range(16)], st=False, sp=False)
+        for u, v, d in ((0, 64, 1), (64, 96, 2), (96, 128, 2))[:1 if n == 64 else 3]:
+            w = 16 // d
+            x = pb(XP, xp + u, xp + v) if d == 1 else pb(XP, 192 + 128 * a + 2 * (u - 64), 192 + 128 * a + 2 * (v - 64))
+            for j in range(w):
+                tt(R(Mn, 16 * u + j, 16 * v, w), R(An, 16 * u + j, 16 * v, w), x, A.max)
+                ops[-1]["wr"] = [(Mn + str(j % 8), u, v)]
+                if v == n:
+                    mm([(pb(KZ[a], k, 128, 16), R(Mn, k, 2048, 16), R("G2", 0, 8)) for k in range(j, 16, w)], st=False, sp=(j == w - 1))
+                    ops[-1]["rd"] = [(Mn + str(j % 8), 0, 128), ("G2", 0, 8)]
         scan(R(mn), R("RST"), pb(KZ[a], 0, 128), 0.0, A.add, A.min)
-        if PAR["UM"] == "R":
-            scan(REV(pb(KZ[a], 128, 256)), R("RST"), REV(pb(KZ[a], 0, 128)), 0.0, A.add, A.min)
-            tt(R(Un, uo + 2, uo + 130), R(mn), pb(KZ[a], 128, 256), A.is_le)
-        else:
-            scan(R(mn + "2"), R("RST"), pb(KZ[a], 0, 128), 0.0, A.add, A.min)
-            tt(R(Un, uo + 2, uo + 130), IND(R(mn), R("last")), R(mn + "2"), A.is_equal)
+        scan(REV(pb(KZ[a], 128, 256)), R("RST"), REV(pb(KZ[a], 0, 128)), 0.0, A.add, A.min)
+        tt(R(Un, uo + 2, uo + 130), R(mn), pb(KZ[a], 128, 256), A.is_le)
         z = pb(KZ[a], 128, 128 + n)
         mm([(z, R("Ib"), R("LS", ls, ls + n)), (z, R(Un, uo + 2, uo + 130), R("I8", 0, n)), (z, R(Un, uo + 1, uo + 129), R("I8n", 0, n))])
         ts(R("C", cc, cc + n), z, SCL, -2048.0, A.add, A.max)
@@ -299,37 +297,27 @@ def rank_program(g, core, T, topo):
     N8 = lambda name, i, a: R(name, 16 * i + 8 * a, 16 * i + 8 * a + 8)
     EP = {1: 0, 2: 1, 0: 2}
     LP = {0: 0, 1: 1, 3: 2, 2: 3}
-    NEW = lambda i, a: R("NEW", 512 * a + 128 * LP[i], 512 * a + 128 * LP[i] + 128)
+    NEW = lambda name, i, a: R(name, 512 * a + 128 * LP[i], 512 * a + 128 * LP[i] + 128)
     U = lambda a, i, k: R("Ub" if a else "Ua", 130 * (i - 1) + k, 130 * (i - 1) + k + 128)
     W256 = lambda name, i: R(name, 256 * i, 256 * i + 256)
     HB = lambda name, i, a: R(name, 256 * i + 128 * a, 256 * i + 128 * a + 128)
 
     def unwrap(i, a):
-        sc = HB("SCN", 0, a)
-        scan(sc, R("PW"), HB("JB", i - 1, a), 0.0, A.add, A.min)
-        e = R("SCN", 128 * a + 15, 128 * a + 128, 16)
-        ts(N8("hu", i, a), e, FW, None, A.add)
+        scan(HB("SCN", 0, a), R("PW"), HB("JB", i - 1, a), 0.0, A.add, A.min)
+        ts(N8("hu", i, a), R("SCN", 128 * a + 15, 128 * a + 128, 16), FW, None, A.add)
         if a:
             ts(W16("hp", i), R("SCN", 15, 256, 16), FW, None, A.add)
 
-    def relist(q, o, i, lo, hi):
-        if PAR["PRE"][i] == "V":
-            ts(R("PR", lo, hi), q, SCL, -2048.0, A.add, A.max)
-            pr, bias = (o, R("Ib"), R("PR", lo, hi)), 6144.0
-        else:
-            act(R("PRf", lo, hi), q, F.Relu, col(6))
-            pr, bias = (o, R("IDf"), R("PRf", lo, hi)), 4096.0
-        mm([(o, R("Ib"), R("LS", 256 * i + lo, 256 * i + hi)), (o, R("In"), R("C", 256 * i - 256 + lo, 256 * i - 256 + hi)), pr])
-        o0 = o["rg"][0][1]
-        for u in range(lo, hi, 128):
-            act(NEW(i, u // 128), pb(P1, o0 + u - lo, o0 + u - lo + 128), F.Identity, bias)
-
-    def newlist(t, i, a):
+    def keep(t, i, a):
         o = pb(P1, 128 * a, 128 * a + 128)
         if i == 0:
             mm([(o, R("Dt", 128 * t, 128 * t + 128), HB("LS", 0, a)), (o, R("BT", 128 * t, 128 * t + 128), HB("C", 0, a))])
-            act(NEW(0, a), o, F.Identity, col(12 + t))
-            return
+            act(NEW("NEW", 0, a), o, F.Identity, col(12 + t))
+        else:
+            mm([(o, R("Ib"), HB("LS", i, a)), (o, R("In"), HB("C", i - 1, a))])
+            act(NEW("NEW", i, a), o)
+
+    def comes(t, i, a):
         q = pb(P0, 128 * a, 128 * a + 128)
         lst = [(q, U(a, i, 2), R("I8")), (q, U(a, i, 1), R("I8n"))]
         if i == 3:
@@ -337,36 +325,40 @@ def rank_program(g, core, T, topo):
         else:
             lst += w2b(P0, 128 * a, 128 * a + 128, N8("val", 1, a))
         mm(lst)
-        relist(q, o, i, 128 * a, 128 * a + 128)
+        act(NEW("PR", i, a), q, F.Relu, SC2)
 
-    sent = []
+    sent, granted = [], []
     for t in range(RO):
         need = R("need", t, t + 1)
         h0 = W16("hou", t)
-        hw1, sub1 = (R("HLi"), 0.0) if t == 0 else (HW, 4096.0)
-        dmt = lambda lo, hi: R("DM", 272 * t + lo, 272 * t + hi)
-        T1, T2 = (lambda k: W16("t1", k)), (lambda k: W16("t2", k))
+        hw1 = R("HLi") if t == 0 else HW
+        x0t = lambda lo, hi: R("DM", 544 * t + lo, 544 * t + hi)
+        dmt = lambda lo, hi: x0t(272 + lo, 272 + hi)
+        dst, src = T.cores[(rank + 1 + t % (N - 1)) % N], T.cores[(rank - 1 - t % (N - 1)) % N]
+        T1, T2, T3 = (lambda k, m=1: W16("t1", k, m)), (lambda k: W16("t2", k)), (lambda k, m=1: W16("t3", k, m))
         p1, p2 = W16("pB", 0), W16("pB", 1)
         tag[0] = "first"
-        ts(R("LS", 0, 256), IND(hw1, h0), -2048.0 - sub1, None, A.add)
+        ts(R("LS", 0, 256), IND(hw1, h0), -2048.0, None, A.add)
         mm(b2w(pb(GK, 32, 48), "LS", 0, 256, "Zt", 144 * t))
         ts(W16("eu", 0), pb(GK, 32, 48), 2048.0, None, A.add)
         for a in range(2):
             ts(HB("JB", 0, a), IND(WW, N8("eu", 0, a)), RND, -2.0 ** 23, A.add, A.add)
+            ops[-1]["soft"] = granted[-1:]
             unwrap(1, a)
         for a in range(2):
-            cp(HB("X0", 0, a), IND(XW, N8("eu", 0, a)))
-            cp(pb(XP, 128 * a, 128 * a + 128), HB("X0", 0, a))
+            tag[0] = "x0" + "ab"[a]
+            cp(x0t(128 * a, 128 * a + 128), IND(XW, N8("eu", 0, a)))
+            mm([(pb(XP, 64 * a, 64 * a + 64), R("Ib"), x0t(128 * a, 128 * a + 64))] +
+               [(pb(XP, 192 + 128 * a + q, 320 + 128 * a, 2), R("Ib"), x0t(128 * a + 64, 128 * a + 128)) for q in range(2)], each=True)
         tag[0] = "misc"
+        swap(R("IN0", 544 * t, 544 * t + 544), x0t(0, 544), dst, src, "a0_%d" % t)
         ts(W16("ef", EP[0]), W16("eu", 0), -2048.0, None, A.add)
         cp(W16("hp", 0), W16("hoi", t))
         mm([(pb(P1, 256, 512), R("LT", 128 * t, 128 * t + 128), R("LS", 0, 256))])
         act(R("E0", 0, 256), pb(P1, 256, 512), F.Identity, 2048.0)
-        ts(R("NP"), R("PP", 0, 64), need, 1.0, A.subtract, A.add)
-        ts(col(7), need, 4096.0, None, A.mult)
-        if PAR["FBE"] == "S":
-            ts(col(11), need, -0.5, None, A.add)
-        tag[0] = "mark0"
+        ts(R("NP"), R("PP"), need, 1.0, A.subtract, A.add)
+        ts(N4, need, 4096.0, None, A.mult)
+        tag[0] = "mark0" if t else "mark00"
         if t:
             act(R("CODE"), R("CODE"), scale=2.0 ** 40)
             ops[-1]["soft"] = sent[-1:]
@@ -396,7 +388,7 @@ def rank_program(g, core, T, topo):
             else:
                 d3 = W16("dB", 2)
                 ts(d3, dW, 1.0, 8192.0, A.is_ge, A.mult)
-                ts(R("NN"), d3, -8.0, col(7), A.mult, A.add)
+                ts(R("NN"), d3, -8.0, N4, A.mult, A.add)
                 tag[0] = "where"
                 tt(T2(3), d3, p2, A.subtract)
                 tt(T2(4), T2(3), p1, A.subtract)
@@ -406,65 +398,54 @@ def rank_program(g, core, T, topo):
             for a in range(2):
                 lo = 128 * a
                 tag[0] = "climb%d%s" % (i, "ab"[a])
-                nearest(a, 128, N8("hu", i, a), hw1 if i == 1 else HW, sub1 if i == 1 else 4096.0, lo, 256 * i + lo, 256 * i - 256 + lo, lo,
-                        PAR["SPS"][2 * i - 2 + a], 130 * (i - 1))
-                eu = N8("eu", i, a)
-                if PAR["EB"][2 * i - 2 + a] == "P":
-                    ew = pb(KZ[a], 256, 264)
-                    mm(b2w(ew, "C", 256 * i - 256 + lo, 256 * i - 128 + lo))
-                else:
-                    y = pb(KZ[a], 256, 384)
-                    mm([(y, R("Ib"), R("PP")), (y, R("BLb"), HB("C", i - 1, a))])
-                    scan(HB("ES", 0, a), R("RSn"), y, 0.0, A.add, A.max)
-                    ew = R("ES", lo + 15, lo + 128, 16)
+                nearest(a, 128, N8("hu", i, a), hw1 if i == 1 else HW, lo, 256 * i + lo, 256 * i - 256 + lo, 64 * a,
+                        PAR["SPS"] if (i, a) == (1, 0) else 0, 130 * (i - 1))
+                eu, ew = N8("eu", i, a), pb(KZ[a], 256, 264)
+                mm(b2w(ew, "C", 256 * i - 256 + lo, 256 * i - 128 + lo))
                 ts(eu, ew, EOFF, None, A.add)
-                ge = HB("GE", i - 1, a)
                 if i < 3:
                     ts(HB("JB", i, a), IND(WW, eu), RND, -2.0 ** 23, A.add, A.add)
                     unwrap(i + 1, a)
+                    tag[0] = "new0"
                     if i == 1:
-                        tag[0] = "new0"
-                        newlist(t, 0, a)
+                        keep(t, 0, a)
+                    keep(t, i, a)
                     continue
                 tag[0] = "fail" + "ab"[a]
+                ge = HB("GE", 2, a)
                 tt(ge, IND(XW, eu), dmt(lo, lo + 128), A.is_ge)
                 act(HB("H4", 0, a), IND(WW, eu), F.Identity, -4096.0)
+                scan(HB("SCN", 0, a), R("PW"), HB("H4", 0, a), 0.0, A.add, A.min)
+                ts(R("ixu", 24 * t + 8 + 8 * a, 24 * t + 16 + 8 * a), R("SCN", lo + 15, lo + 128, 16), FW, None, A.add)
                 sc = pb(DK, 256 + lo, 384 + lo)
                 mm([(sc, R("BL4"), HB("DB", 0, a)), (sc, R("BLb"), ge)])
-                if PAR["FBE"] == "S":
-                    act(HB("FB", 0, a), sc, F.Sign, col(11), -1.0)
-                    scan(HB("PF", 0, a), R("ONEb"), HB("FB", 0, a), R("PF", 127, 128) if a else 0.0, A.add, A.add)
-                else:
-                    ts(HB("FB", 0, a), sc, need, 2.0, A.is_lt, A.mult)
-                    scan(HB("PF", 0, a), R("ONEb"), HB("FB", 0, a), R("PF", 127, 128) if a else 0.0, A.mult, A.add)
+                ts(HB("FB", 0, a), sc, need, 2.0, A.is_lt, A.mult)
+                scan(HB("PF", 0, a), R("ONEb"), HB("FB", 0, a), R("PF", 127, 128) if a else 0.0, A.mult, A.add)
                 for c in range(4):
                     act(R("junk", 512 * a + 128 * c, 512 * a + 128 * c + 128), HB("PF", 0, a), F.Sign,
                         R("DX", 8 + c, 9 + c), -1.0, R("sa", 4 * a + c, 4 * a + c + 1))
                     if a:
-                        ts(R("ixu", c, c + 1), R("sa", 4 + c, 5 + c), R("sa", 8 + c, 9 + c), 0.5, A.add, A.mult)
+                        ts(R("ixu", 24 * t + c, 24 * t + c + 1), R("sa", 4 + c, 5 + c), R("sa", 8 + c, 9 + c), 0.5, A.add, A.mult)
                 if a == 0:
                     ts(R("sa", 8, 12), R("sa", 0, 4), 256.0, None, A.add)
                 tag[0] = "pay" + "ab"[a]
                 cn = pb(GK, 16 + 8 * a, 24 + 8 * a)
                 mm([(cn, R("Ib"), N8("NN", 0, a))] + b2w(cn, "GE", 512 + lo, 640 + lo, "Zn"))
-                q8 = lambda name, k, m=1: R(name, 32 * a + 8 * k, 32 * a + 8 * (k + m))
                 tt(N8("t2", 8, a), ew, N8("t2", 6, a), A.subtract)
                 tt(N8("val", 1, a), N8("t2", 8, a), N8("t2", 5, a), A.max)
-                newlist(t, 3, a)
-                newlist(t, 2, a)
+                keep(t, 3, a)
+                comes(t, 3, a)
+                comes(t, 2, a)
                 ts(N8("t2", 7, a), cn, 0.0, float(H), A.max, A.min)
                 for k in range(4):
-                    tt(q8("lof", LP[k]), N8("t2", 7, a), N8("hD", k, a), A.add)
-                cp(q8("lo", 0, 4), q8("lof", 0, 4))
+                    tt(R("lof", 32 * a + 8 * LP[k], 32 * a + 8 * LP[k] + 8), N8("t2", 7, a), N8("hD", k, a), A.add)
+                cp(R("lo", 32 * a, 32 * a + 32), R("lof", 32 * a, 32 * a + 32))
             if i == 3:
                 for a in range(2):
                     tag[0] = "list" + "ab"[a]
                     for u, v in zip(PAR["HG"][a], PAR["HG"][a][1:]):
-                        off, new = R("lo", 32 * a + 8 * u, 32 * a + 8 * v), R("NEW", 512 * a + 128 * u, 512 * a + 128 * v)
-                        if PAR["HLE"][a] == "S":
-                            act(IND(R("HL"), off), new, F.Silu)
-                        else:
-                            cp(IND(R("HL"), off), new)
+                        tt(IND(R("HL"), R("lo", 32 * a + 8 * u, 32 * a + 8 * v)), R("NEW", 512 * a + 128 * u, 512 * a + 128 * v),
+                           R("PR", 512 * a + 128 * u, 512 * a + 128 * v), A.add)
                 break
             tag[0] = "up%d" % i
             tt(W256("GE", i - 1), IND(XW, W16("eu", i)), dmt(0, 256), A.is_ge)
@@ -479,37 +460,28 @@ def rank_program(g, core, T, topo):
                 tt(T2(1), T2(0), p1, A.add)
                 tt(T2(2), W16("ef", EP[2]), p1, A.subtract)
                 tt(W16("val", 0), T2(1), T2(2), A.max)
-                q, o = pb(P0, 256, 512), pb(P1, 256, 512)
-                mm([(q, R("Ib"), R("th", 0, 256))] + w2b(P0, 256, 512, W16("val", 0)) +
+                mm([(pb(P0, 256, 512), R("Ib"), R("th", 0, 256))] + w2b(P0, 256, 512, W16("val", 0)) +
                    [(pb(P0, 256 + 128 * a, 384 + 128 * a), U(a, 1, k), R(w)) for a in range(2) for k, w in ((2, "I8"), (1, "I8n"))])
-                relist(q, o, 1, 0, 256)
+                for a in range(2):
+                    act(NEW("PR", 1, a), pb(P0, 256 + 128 * a, 384 + 128 * a), F.Relu, SC2)
                 tt(T2(5), T2(0), p2, A.add)
                 ts(T2(6), p2, 2048.0 - EOFF, None, A.add)
         tag[0] = "send"
-        dst, src = T.cores[(rank + 1 + t % (N - 1)) % N], T.cores[(rank - 1 - t % (N - 1)) % N]
-        o1 = 192 * t
-        ix = R("ixu")
-        cp(R("h4c"), IND(R("H4", 0, 257), ix))
-        cp(R("OUT1", o1 + 64, o1 + 128), IND(R("X0", 0, 257), ix))
-        scan(R("OUT1", o1, o1 + 64), R("PW", 0, 64), R("h4c"), 0.0, A.add, A.min)
-        cp(R("OUT1", o1 + 128, o1 + 192), IND(dmt(0, 257), ix))
-        swap(R("IN1", o1, o1 + 192), R("OUT1", o1, o1 + 192), dst, src, "a1_%d" % t)
+        ix = R("ixu", 24 * t, 24 * t + 4)
+        swap(R("INI", 24 * t, 24 * t + 24), R("ixu", 24 * t, 24 * t + 24), dst, src, "a1_%d" % t)
         sent.append(len(ops) - 2)
         tag[0] = "yl"
         if t == RO - 1:
-            for k in range(4):
-                ts(R("HLo", 384 * k, 384 * k + 384), R("HL", 384 * k, 384 * k + 384), RND, -2.0 ** 23, A.add, A.add)
-            dma("Y", "dyl", T.yl[:], T.HLo[:], [], [R("HLo")], 4400)
+            dma("Y", "dyl", T.yl[:], T.HL[:, 0:H], [], [HW], 768)
         tag[0] = "own"
         x4 = lambda k: R("xs4", 4 * k, 4 * k + 4)
-        act(R("x0s"), IND(R("X0", 0, 257), ix))
-        act(R("e0c", 0, 64), IND(R("E0", 0, 257), ix))
+        cp(R("x0s"), IND(x0t(0, 257), ix))
+        cp(R("e0c", 0, 64), IND(R("E0", 0, 257), ix))
         scan(R("e0c", 64, 128), R("PX"), R("e0c", 0, 64), 0.0, A.add, A.min)
         tt(x4(0), R("e0c", 79, 128, 16), R("DX", 4, 8), A.min)
         ts(R("e0u"), x4(0), FX, None, A.add)
         ts(x4(5), R("e0u"), -EOFF, None, A.add)
         tag[0] = "warr"
-        T3 = lambda k, m=1: W16("t3", k, m)
         for a in range(2):
             ts(N8("t3", 1, a), R("lof", 32 * a + 16, 32 * a + 24), H - 0.5, 8192.0, A.is_ge, A.mult)
         tt(T3(0), T3(1), p2, A.subtract)
@@ -520,7 +492,7 @@ def rank_program(g, core, T, topo):
         tag[0] = "hm"
         tt(T1(3), W16("hp", 1), W16("hp", 2), A.subtract)
         tt(T1(4), W16("hp", 2), W16("hp", 3), A.subtract)
-        tt(W16("t1", 5, 2), W16("t1", 3, 2), T3(0, 2), A.mult)
+        tt(T1(5, 2), T1(3, 2), T3(0, 2), A.mult)
         tt(T1(7), T1(5), T1(6), A.add)
         ts(W16("val", 2), T1(7), 2.0 ** -13, None, A.mult)
         o = pb(P1, 256, 512)
@@ -532,16 +504,12 @@ def rank_program(g, core, T, topo):
             mm([(o, R("Ib"), W256("JB", k))])
             act(W256("HM", k), o, F.Identity, 4096.0)
         tag[0] = "warr"
-        for e, u, v in zip(PAR["WTE"], PAR["WG"], PAR["WG"][1:]):
-            if e == "S":
-                act(IND(R("WT"), R("wo", 8 * u, 8 * v)), R("HM", 128 * u, 128 * v), F.Silu)
-            else:
-                cp(IND(R("WT"), R("wo", 8 * u, 8 * v)), R("HM", 128 * u, 128 * v))
+        act(IND(R("WT"), R("wo")), R("HM"), F.Silu)
         tag[0] = "odd"
         if t == RO - 1:
-            dma("Y", "dw2", T.E0[:, 0:256], T.WT[0:128:16, 0:P], [R("E0", 0, 256)], [WW], 800)
-            ts(R("H4", 0, 256), R("E0", 0, 256), RND, -2.0 ** 23, A.add, A.add)
-            dma("Y", "dyw", T.yw[:], T.H4[:, 0:256], [], [R("H4", 0, 256)], 800)
+            dma("Y", "dw2", T.E0[:, 0:256], T.WT[0:128:16, 0:P], [R("E0", 0, 256)], [WW], 256)
+            ts(R("H4"), R("E0", 0, 256), RND, -2.0 ** 23, A.add, A.add)
+            dma("Y", "dyw", T.yw[:], T.H4[:], [], [R("H4")], 256)
         else:
             act(R("junk", 1024, 1040), T3(2), F.Sign, -0.5, 1.0, col(15))
             mm([(pb(GK, 48, 49), R("ONE"), col(15))])
@@ -549,16 +517,20 @@ def rank_program(g, core, T, topo):
             ts(R("ni", 1, 2), R("ni", 0, 1), 1, None, A.bitwise_and)
             ts(R("need", t + 1, t + 2), R("ni", 1, 2), 9.0, None, A.add)
         tag[0] = "come"
-        xin, din = R("IN1", o1 + 64, o1 + 128), R("IN1", o1 + 128, o1 + 192)
-        ts(R("xu", 0, 4), R("IN1", o1 + 15, o1 + 64, 16), FW, None, A.add)
-        cp(pb(XP, 256, 320), xin)
-        nearest(0, 64, R("xu", 0, 4), HW, 4096.0, 256, 1024, 768, 256, PAR["SPL"], 390)
-        fy, fb, cy, cb = pb(KZ[0], 256, 320), pb(KZ[0], 320, 384), pb(KZ[0], 384, 448), pb(KZ[0], 448, 512)
-        mm([(fy, R("Ib"), R("PP", 0, 64)), (fy, R("BLb"), R("C", 768, 832))])
+        cp(R("LA", 0, 128), IND(HW, R("INI", 24 * t + 8, 24 * t + 16)))
+        act(R("LA", 128, 256), IND(HW, R("INI", 24 * t + 16, 24 * t + 24)))
+        xin, din, ii = R("xin", 0, 64), R("xin", 64, 128), R("INI", 24 * t, 24 * t + 4)
+        act(xin, IND(R("IN0", 544 * t, 544 * t + 257), ii))
+        mm([(pb(XP, 128, 192), R("Ib"), xin)])
+        nearest(0, 64, ii, R("LA", 0, 257), 256, 1024, 768, 128, PAR["SPL"], 390)
+        act(din, IND(R("IN0", 544 * t + 272, 544 * t + 529), ii))
+        ops[-1]["soft"] = gat[-1:]
+        fy, fb, cy, cb = pb(KZ[0], 256, 260), pb(KZ[0], 320, 384), pb(KZ[0], 384, 448), pb(KZ[0], 448, 512)
+        mm(b2w(fy, "C", 768, 832))
         mm([(fb, R("BLb"), R("C", 768, 832))])
-        scan(R("FS", 0, 64), R("RSn", 0, 64), fy, 0.0, A.add, A.max)
-        fu, fw = R("xu", 4, 8), R("FS", 15, 64, 16)
-        ts(fu, fw, EOFF, None, A.add)
+        fu, fw = R("fu"), R("FS", 0, 4)
+        ts(fu, fy, EOFF, None, A.add)
+        cp(fw, fy)
         tt(R("xg"), IND(XW, fu), din, A.is_ge)
         tt(R("xd"), IND(XW, fu), xin, A.subtract)
         for c in range(4):
@@ -570,11 +542,13 @@ def rank_program(g, core, T, topo):
         scan(R("FS", 64, 128), R("R01"), cy, 0.0, A.mult, A.max)
         ts(R("nb"), cb, need, None, A.is_lt)
         mm([(acc, R("BL4"), R("nb"))], st=False, sp=False)
-        mm(pairs(4, KZ[1], "EX", lambda o, c: ts(o, pb(KZ[0], 320 + 16 * c, 384), R("FS", 15 + 16 * c, 16 + 16 * c), R("FS", 79 + 16 * c, 80 + 16 * c),
+        mm(pairs(4, KZ[1], "EX", lambda o, c: ts(o, pb(KZ[0], 320 + 16 * c, 384), R("FS", c, c + 1), R("FS", 79 + 16 * c, 80 + 16 * c),
                                                  A.is_equal, A.min)), st=False)
-        ts(R("xq"), acc, 0.0, None, A.is_lt)
+        ts(pb(KZ[1], 64, 128), acc, 0.0, None, A.is_lt)
+        granted.append(len(ops) - 1)
         o2 = 64 * t
-        tt(R("OUT2", o2, o2 + 64), R("xq"), R("xd"), A.mult)
+        tt(R("OUT2", o2, o2 + 64), R("xd"), pb(KZ[1], 64, 128), A.mult)
+        ts(R("xq"), acc, 0.0, None, A.is_lt)
         swap(R("IN2", o2, o2 + 64), R("OUT2", o2, o2 + 64), src, dst, "a2_%d" % t)
         tag[0] = "take"
         mm(b2w(pb(DK, 16, 20), "xq", 0, 64))
@@ -585,8 +559,7 @@ def rank_program(g, core, T, topo):
         cp(IND(R("X"), R("xo")), xin)
         tag[0] = "back"
         tt(IND(R("X"), R("e0u")), R("x0s"), R("IN2", o2, o2 + 64), A.add)
-    dma("Y", "dy0", T.yx[:, 0:2048], T.X[:, 0:2048], [], [XW], 5800)
-    dma("S", "dy1", T.yx[:, 2048:P], T.X[:, 2048:P], [], [XW], 5800)
+    dma("S", "dyx", T.yx[:], T.X[:, 0:P], [], [XW], 1024)
 
     emit(g, T, ops)
 
@@ -642,20 +615,19 @@ def emit(g, T, ops):
     if "graph" not in PLAN:
         seen, deps, soft = {}, [], []
         for k, o in enumerate(ops):
-            d, sf = set(), set(o.get("soft", []))
+            d = set()
             for w, rgs in ((0, o["rd"]), (1, o["wr"])):
                 for name, lo, hi in rgs:
                     for k2, w2, lo2, hi2 in seen.get(name, []):
                         if (w or w2) and lo < hi2 and lo2 < hi:
-                            inq = w and not w2 and PAR["WQ"] and ops[k2]["eng"] == o["eng"] and o["eng"] in "VS" and "sem" not in o and "sem" not in ops[k2]
-                            (sf if inq else d).add(k2)
+                            d.add(k2)
             if "after" in o:
                 d.add(o["after"])
             for w, rgs in ((0, o["rd"]), (1, o["wr"])):
                 for name, lo, hi in set(rgs):
                     seen.setdefault(name, []).append((k, w, lo, hi))
             deps.append(sorted(d))
-            soft.append(sf - d)
+            soft.append(set(o.get("soft", [])) - d)
         anc, red = [], []
         for k in range(n):
             m, keep = 0, []
@@ -672,7 +644,8 @@ def emit(g, T, ops):
         PLAN["graph"] = deps, red, succ, soft
     if "order" not in PLAN:
         deps, red, succ, soft = PLAN["graph"]
-        fwd = lambda k, j: ops[k].get("lat", 0) + (0 if ops[k]["eng"] == ops[j]["eng"] == "PE" or k in soft[j] else PAR["HV" if ops[k]["eng"] == "V" else "HOP"])
+        fwd = lambda k, j: ops[k].get("lat", 0) + (0 if ops[k]["eng"] == ops[j]["eng"] == "PE" or k in soft[j]
+                                                   else PAR["HV" if ops[k]["eng"] == "V" else "HOP"])
         bwd = lambda k, j: fwd(j, k)
         pr0, est = [0.0] * n, [0.0] * n
         for k in range(n - 1, -1, -1):

from concourse.mybir import AluOpType as A, AxisListType, ActivationFunctionType as F

P, H, S, RO, CAP = 4096, 1536, 256, 3, 64
F32, BF, F16, I32, U16 = "float32", "bfloat16", "float16", "int32", "uint16"
SB = {
    "X": (P + 64, BF), "HLi": (H, I32), "HL": (2 * H + 1024, F32), "WT": (P + 768, F32), "VT": (H + 256, F32), "DM": (1632, BF),
    "wi": (256, I32), "w16": (256, F16), "hoi": (48, I32), "hou": (48, U16),
    "ONE": (128, F32), "IDf": (128, F32), "BLf": (128, F32), "Ib": (128, BF), "In": (128, BF), "I8": (128, BF), "I8n": (128, BF),
    "BLb": (128, BF), "BL4": (128, BF), "POW": (128, BF), "ONEb": (128, BF), "G2": (16, BF),
    "Z": (144, BF), "Zn": (144, BF), "Zt": (432, BF), "Dt": (384, BF), "BT": (384, BF), "LT": (2048, BF), "THn": (256, BF), "th": (512, BF),
    "RST": (128, F32), "R01": (64, F32), "PW": (128, F16), "PX": (64, F32), "PP": (64, BF), "NP": (64, BF), "NN": (16, BF),
    "pi": (2, I32), "q16": (128, F32), "dq": (384, F32), "M16": (16, F32), "col": (16, F32),
    "SW": (64, F32), "DL": (64, F32), "DV": (16, F32), "DW": (48, F32), "DX": (12, F32), "CODE": (256, F32), "need": (4, F32), "ni": (2, I32),
    "Aa": (2048, BF), "Ab": (2048, BF), "Ma": (2048, BF), "Mb": (2048, BF), "ma": (128, F32), "mb": (128, F32),
    "Ua": (520, BF), "Ub": (390, BF), "LSu": (320, U16), "LS": (1088, F16), "C": (832, F16),
    "JB": (768, F16), "GE": (768, BF), "SCN": (256, F16), "H4": (256, F32), "E0": (264, F32),
    "eu": (64, U16), "hu": (64, U16), "hp": (64, F32), "ef": (48, F32), "hs": (16, F32), "nup": (32, BF), "dB": (48, F32), "pB": (32, F32),
    "EQ": (2176, BF), "VB": (256, BF), "DB": (256, BF), "vo": (16, U16),
    "PR": (1024, F32), "NEW": (1024, F32), "HM": (768, F32), "t1": (128, F32), "t2": (144, F32), "t3": (144, F32),
    "hD": (64, F32), "bs": (64, F32), "lof": (64, F32), "lo": (64, U16), "val": (48, F16), "wo": (48, U16),
    "FB": (256, BF), "PF": (256, BF), "junk": (1040, BF), "sa": (12, F32), "ixu": (72, U16), "e0c": (128, F32), "FS": (128, F32),
    "IN0": (1632, BF), "INI": (72, U16), "LA": (264, F32), "xin": (128, BF), "OUT2": (192, BF), "IN2": (192, BF), "x0s": (64, BF),
    "EX": (416, BF), "e0u": (4, U16), "xs4": (24, F32), "fu": (4, U16), "xg": (64, BF), "xd": (64, BF), "nb": (64, BF), "xq": (64, BF), "xo": (4, U16),
}
SCRATCH = {k: ("sbuf", [128, w], d) for k, (w, d) in SB.items()}
for _b in range(8):
    SCRATCH["pb%d" % _b] = ("psum", [128, 512], F32)
DMAS = ["dho", "dhl", "dwr", "ddm0", "ddm1", "ddm2", "dx", "dyl", "dyw", "dw2", "dyx"]
SEMAPHORES = ["V", "S", "PE", "G", "sent"] + DMAS + ["a%d_%d" % (k, t) for k in range(3) for t in range(RO)]

PAR = dict(GA=1.4, SC=3.0, HOP=200.0, HV=270.0, FS=90.0, PEC=0.42, NET=3600.0, DMAL=2400.0, KB=4.0, IT=4, MIX=0.0, LAM=(0.4,),
           SPL=32, SPS=32, HG=((0, 4), (0, 4)),
           URG={'faila': -750, 'x0a': 3400, 'own': 3250, 'hj': 2850, 'first': 1900, 'lists': -600, 'lista': -3150, 'die1': -950, 'die3': 450, 'x0b': -2300, 'up1': -250, 'climb1a': -250, 'die2': -150, 'take': 800, 'new0': -2050, 'mark1': 1350, 'come': -2100, 'mark2': -550, 'warr': 650, 'up2': 150, 'set': 150, 'climb2b': -150, 'new1': 1200, 'hm': -3850, 'odd': -800, 'mark0': -400, 'climb3a': 300, 'where': -1350, 'yl': -1650, 'send': 300, 'payb': -700, 'climb2a': 300, 'climb3b': 150, 'mark00': -400, 'paya': -600})
PLAN = {}


def rank_program(g, core, T, topo):
    rank = T.rank_of(core)
    if rank is None:
        return
    N = len(T.cores)
    ops, tag = [], ["set"]
    GA, SC, PEC = PAR["GA"], PAR["SC"], PAR["PEC"]

    def R(name, lo=0, hi=None, step=1):
        hi = T[name].shape[1] if hi is None else hi
        ap = T[name][:, lo:hi:step] if step > 1 else T[name][:, lo:hi]
        return dict(ap=ap, rg=[(name, lo, hi)], n=len(range(lo, hi, step)), ps=name.startswith("pb"),
                    b2=SB.get(name, (0, F32))[1] in (BF, F16, U16), ind=False)

    def REV(x):
        name, lo, hi = x["rg"][0]
        return dict(x, ap=T[name][:, hi - 1:(lo - 1 if lo else None):-1])

    def IND(win, off):
        return dict(ap=win["ap"].indirect(off["ap"]), rg=win["rg"], off=off["rg"], n=16 * off["n"], ps=False, b2=win["b2"], ind=True)

    def add(eng, fn, outs, ins, cost, **kw):
        rd, wr = [], []
        for o in outs:
            wr += o["rg"]
            rd += o.get("off", [])
        for i in ins:
            if isinstance(i, dict):
                rd += i["rg"] + i.get("off", [])
        ops.append(dict(eng=eng, fn=fn, rd=rd, wr=wr, cost=cost, tag=tag[0], **kw))

    def ap(x):
        return x["ap"] if isinstance(x, dict) else x

    def vcost(out, in0, base):
        return 60 + SC * out["n"] if out["ind"] else 60 + GA * in0["n"] if in0["ind"] else max(64, base)

    def tt(out, a, b, op):
        add("V", lambda: g.vector.tensor_tensor(out["ap"], a["ap"], b["ap"], op), [out], [a, b],
            vcost(out, a, b["n"] * (1 if a["ps"] or b["ps"] else 2)))

    def ts(out, a, s1, s2, op0, op1=None):
        c = vcost(out, a, a["n"] * (0.5 if a["b2"] and out["b2"] else 1))
        if op1 is None:
            add("V", lambda: g.vector.tensor_scalar(out["ap"], a["ap"], ap(s1), None, op0), [out], [a, s1], c)
        else:
            add("V", lambda: g.vector.tensor_scalar(out["ap"], a["ap"], ap(s1), ap(s2), op0, op1), [out], [a, s1, s2], c)

    def cp(out, a):
        add("V", lambda: g.vector.tensor_copy(out["ap"], a["ap"]), [out], [a], vcost(out, a, a["n"] * (0.5 if a["b2"] and out["b2"] else 1)))

    def ms(out, v):
        add("V", lambda: g.vector.memset(out["ap"], v), [out], [], max(64, out["n"] * (0.5 if out["b2"] else 1)))

    def scan(out, d0, d1, init, op0, op1):
        add("V", lambda: g.vector.tensor_tensor_scan(out["ap"], d0["ap"], d1["ap"], ap(init), op0, op1), [out], [d0, d1, init],
            max(64, out["n"] * (0.5 if out["b2"] and d0["b2"] and d1["b2"] else 1)))

    def red(out, a):
        add("V", lambda: g.vector.tensor_reduce(out["ap"], a["ap"], AxisListType.X, A.add), [out], [a], max(64, a["n"]))

    def act(out, a, f=F.Copy, bias=0.0, scale=1.0, acc=None):
        c = PAR["FS"] + (80 + SC * a["n"] if out["ind"] else 80 + GA * a["n"] if a["ind"] else max(64, a["n"]) + (24 if acc else 0))
        if out["ind"]:
            add("S", lambda: g.scalar.activation(out["ap"], a["ap"], f), [out], [a], c)
        elif acc:
            add("S", lambda: g.scalar.activation(out["ap"], a["ap"], f, ap(bias), scale, accum_out=acc["ap"]), [out, acc], [a, bias], c)
        else:
            add("S", lambda: g.scalar.activation(out["ap"], a["ap"], f, ap(bias), ap(scale)), [out], [a, bias, scale], c)

    def mm(lst, each=False, st=True, sp=True):
        def fn():
            ins = None
            for k, (o, l, r) in enumerate(lst):
                ins = g.tensor.matmul(o["ap"], l["ap"], r["ap"], each or (st and k == 0), each or (sp and k == len(lst) - 1))
            return ins
        add("PE", fn, [o for o, l, r in lst], [x for o, l, r in lst for x in (l, r)],
            sum(PEC * max(min(64, l["n"]), r["n"]) * (1 if r["b2"] else 4) for o, l, r in lst))

    def b2w(out, name, lo, hi, Z="Z", z0=0):
        return [(out, R(Z, z0 + 15 - r, z0 + 143 - r), R(name, lo + r, hi, 16)) for r in range(16)]

    def w2b(b, lo, hi, w):
        return [(pb(b, lo + r, hi, 16), R("LT", 128 * r, 128 * r + 128), w) for r in range(16)]

    def iota(out, pat, base, cm, flt=True):
        if flt:
            add("G", lambda: g.iota(out["ap"], pat, base, cm, allow_small_or_imprecise_dtypes=True), [out], [], 160 + 2 * out["n"])
        else:
            add("G", lambda: g.iota(out["ap"], pat, base, cm), [out], [], 160 + 2 * out["n"])

    def asel(out, a, pat, op, base, cm):
        add("G", lambda: g.affine_select(out["ap"], a["ap"], pat, op, 0.0, base, cm), [out], [a], 200 + 2 * out["n"])

    def dma(q, sem, out, in_, outs, ins, kb, first=False):
        e = g.sync if q == "Y" else g.scalar
        add(q, lambda: e.dma_start(out, in_), outs, ins, 60, sem=sem, lat=PAR["DMAL"] + PAR["KB"] * kb, pri=(1e9 - len(ops) if first else 0))

    def swap(land, out, dst, src, sem):
        rid, pid, _ = topo.addr(dst)
        add("G", lambda: g.remote_dma(land["ap"], out["ap"], T.sem[sem], T.sem.sent, pid, rid, topo.mask(core, dst)), [], [out], 300,
            remote=len(topo.engines(core, dst)))
        add("N", None, [land], [], 0, sem=sem, val=len(topo.engines(src, core)), lat=PAR["NET"] - PAR["HOP"], after=len(ops) - 1)

    pb = lambda b, lo=0, hi=512, st=1: R("pb%d" % b, lo, hi, st)
    KZ, ACC, DK, GK, P0, XP, P1 = (0, 1), 2, 3, 4, 5, 6, 7

    dma("Y", "dho", T.hoi[:], T.ho[:], [R("hoi")], [], 24, True)
    dma("S", "dwr", T.wi[:], T.wr[:], [R("wi")], [], 152, True)
    dma("Y", "dhl", T.HLi[:], T.hl[:], [R("HLi")], [], 920, True)
    dma("Y", "dx", T.X[:, 0:P], T.xs[:], [R("X", 0, P)], [], 1944, True)
    for t in range(RO):
        d0 = 544 * t + 272
        dma("Y", "ddm%d" % t, T.DM[:, d0:d0 + 256], T.dm[:, 256 * t:256 * t + 256], [R("DM", d0, d0 + 256)],
            [R("X", 0, P)] if t else [], 64 if t else 2008, True)

    col = lambda k: R("col", k, k + 1)
    QC, PWc, SCL, FW, FX, SC2, N4 = col(0), col(1), col(2), col(3), col(4), col(6), col(7)
    fill = lambda out, v: iota(out, [[0, out["n"]]], v, 0)
    ms(R("ONE"), 1.0)
    iota(R("pi", 0, 1), [[0, 1]], 0, 1, False)
    iota(R("q16"), [[0, 8], [1, 16]], 0, 0)
    asel(R("dq", 0, 128), R("ONE"), [[-16, 8], [0, 16]], A.is_ge, 0, 1)
    asel(R("BLf"), R("dq", 0, 128), [[16, 8], [0, 16]], A.is_ge, 15, -1)
    asel(R("IDf"), R("ONE"), [[-1, 128]], A.is_equal, 0, 1)
    iota(R("SW"), [[16, 64]], 0, 0)
    tag[0] = "fill"
    fill(R("CODE"), 1)
    fill(R("VT"), 0)
    fill(R("BT"), 0)
    for t in range(RO):
        fill(R("DM", 544 * t + 256, 544 * t + 272), 0)
        fill(R("DM", 544 * t + 528, 544 * t + 544), 256)
    fill(R("LA", 256, 264), 0)
    for a in range(2):
        fill(R("PR", 512 * a, 512 * a + 128), 0)
    fill(R("E0", 256, 264), 8192)
    tag[0] = "set"
    ts(R("pi", 1, 2), R("pi", 0, 1), 15, None, A.bitwise_and)
    cp(QC, R("pi", 1, 2))
    ts(R("M16"), R("q16", 0, 16), QC, None, A.is_equal)
    for i in range(16):
        o = R("LT", 128 * i, 128 * i + 128)
        if i % 2:
            act(o, R("BLf"), F.Identity, 0.0, R("M16", i, i + 1))
        else:
            ts(o, R("BLf"), R("M16", i, i + 1), None, A.mult)
    cp(R("w16"), R("wi"))
    for b in range(8):
        k0 = (0, 1, 2, 3, 4, 5, 7, 0)[b]
        mm([(pb(k0, 256 * k, 256 * k + 256), R("LT", 128 * (2 * b + k), 128 * (2 * b + k) + 128), R("w16")) for k in range(2)], each=True)
        if b in (1, 4, 6):
            ts(R("WT", 512 * b, 512 * b + 512), pb(k0), 4096.0, None, A.add)
        else:
            act(R("WT", 512 * b, 512 * b + 512), pb(k0), F.Identity, 4096.0)
    cp(R("hou"), R("hoi"))
    tag[0] = "lists"
    for k in range(8):
        cp(R("HL", 192 * k, 192 * k + 192), R("HLi", 192 * k, 192 * k + 192))
    tag[0] = "set"
    aff = lambda out, x, m, c=0.0: ts(out, x, m, c, A.mult, A.add)
    ms(R("Z"), 0.0)
    cp(R("Z", 15, 143, 16), R("BLf", 0, 128, 16))
    aff(R("Zn"), R("Z"), -4096.0)
    aff(R("col", 8, 11), R("M16", 0, 3), -1.0, 1.0)
    aff(R("col", 12, 15), R("M16", 0, 3), 30720.0, 2048.0)
    for nm, v in (("I8", 8192.0), ("I8n", -8192.0), ("Ib", 1.0), ("In", -1.0)):
        act(R(nm), R("IDf"), scale=v)
    for t in range(RO):
        aff(R("Zt", 144 * t, 144 * t + 144), R("Z"), R("M16", t, t + 1))
        aff(R("Dt", 128 * t, 128 * t + 128), R("Ib"), col(8 + t))
        cp(R("BT", 128 * t + t, 128 * t + 128, 16), R("BLf", 0, 128, 16))
    for k, v in ((0, 2.0), (8, -1.0)):
        aff(R("G2", k, k + 8), R("BLf", 0, 128, 16), v)
    act(R("BLb"), R("BLf"))
    aff(R("BL4"), R("BLb"), 4.0)
    ms(R("ONEb"), 1.0)
    ts(R("RST"), R("q16"), 0.5, 1e6, A.is_lt, A.mult)
    ts(R("R01"), R("q16", 0, 64), 0.5, None, A.is_gt)
    ms(R("th", 0, 256), 0.25)
    ms(R("th", 256, 512), 0.0)
    ms(R("th", 256, 512, 16), -2.0)
    scan(R("THn"), R("th", 0, 256), R("th", 256, 512), 0.0, A.mult, A.min)
    ms(R("th", 0, 256), 0.0)
    tt(R("t1", 0, 16), R("THn", 0, 16), R("M16"), A.mult)
    red(col(5), R("t1", 0, 16))
    ts(R("POW"), R("BLb"), col(5), -0.5, A.mult, A.mult)
    aff(SCL, R("M16", 0, 1), 8192.0, -8192.0)
    aff(SC2, R("M16", 0, 1), 8192.0, -6144.0)
    aff(FW, R("M16", 15, 16), -1536.0, 1536.0)
    aff(FX, R("M16", 15, 16), -16384.0, 16384.0)
    ts(R("dq", 0, 128), R("q16"), QC, None, A.subtract)
    ts(R("dq", 128, 256), R("dq", 0, 128), 0.5, 4096.0, A.is_lt, A.mult)
    ts(R("dq", 256, 384), R("dq", 0, 128), 1.0, -1536.0, A.is_equal, A.mult)
    tt(R("PW"), R("dq", 128, 256), R("dq", 256, 384), A.add)
    ts(R("PP"), R("dq", 0, 64), 0.0, -65536.0, A.not_equal, A.mult)
    ts(R("PX"), R("PW", 0, 64), 16384.0 / 1536, None, A.mult)
    ts(R("SW"), R("SW"), QC, None, A.add)
    aff(R("DL"), R("SW"), 1.0, 2.0 * H)
    aff(R("DV"), R("SW", 0, 16), 1.0, float(H))
    aff(R("DW"), R("SW", 0, 48), 1.0, P - 2048.0)
    aff(R("DX", 0, 4), R("SW", 0, 4), 1.0, float(P))
    ts(R("DX", 4, 8), R("DX", 0, 4), FX, None, A.subtract)
    aff(R("DX", 8, 12), R("SW", 0, 4), 2.0, 1.0)
    ms(R("Ua", 1, 520, 130), 1.0)
    ms(R("Ub", 1, 390, 130), 1.0)
    ms(R("need", 0, 1), 9.0)
    ms(R("ixu"), 0.0)

    XW, HW, WW = R("X", 0, P), R("HL", 0, H), R("WT", 0, P)
    EOFF, RND = 32768.0, 2.0 ** 23 - 4096
    gat = []

    def nearest(a, n, hoff, hw, lu, ls, cc, xp, split, uo):
        An, Mn, mn, Un = ("Aa", "Ma", "ma", "Ua") if a == 0 else ("Ab", "Mb", "mb", "Ub")
        cp(R("LSu", lu, lu + n), IND(hw, hoff))
        ts(R("LS", ls, ls + n), R("LSu", lu, lu + n), -2048.0, None, A.add)
        ns = n - split
        cuts = [u for u in (0, 64, 96) if u < ns] + [ns]
        for u, v in zip(cuts, cuts[1:]):
            act(R(An, 16 * u, 16 * v), IND(XW, R("LSu", lu + u, lu + v)))
            ops[-1]["soft"] = gat[-1:]
            gat.append(len(ops) - 1)
        if split:
            cp(R(An, 16 * ns, 16 * n), IND(XW, R("LSu", lu + ns, lu + n)))
        mm([(pb(KZ[a], 0, 128), R("Ib"), R("th", 0, 128))], sp=False)
        ops[-1]["wr"].append(("pb%d" % KZ[a], 0, 512))
        mm([(pb(KZ[a], j, 128, 16), R(An, j, 2048, 16), R("G2", 8, 16)) for j in range(16)], st=False, sp=False)
        for u, v, d in ((0, 64, 1), (64, 96, 2), (96, 128, 2))[:1 if n == 64 else 3]:
            w = 16 // d
            x = pb(XP, xp + u, xp + v) if d == 1 else pb(XP, 192 + 128 * a + 2 * (u - 64), 192 + 128 * a + 2 * (v - 64))
            for j in range(w):
                tt(R(Mn, 16 * u + j, 16 * v, w), R(An, 16 * u + j, 16 * v, w), x, A.max)
                ops[-1]["wr"] = [(Mn + str(j % 8), u, v)]
                if v == n:
                    mm([(pb(KZ[a], k, 128, 16), R(Mn, k, 2048, 16), R("G2", 0, 8)) for k in range(j, 16, w)], st=False, sp=(j == w - 1))
                    ops[-1]["rd"] = [(Mn + str(j % 8), 0, 128), ("G2", 0, 8)]
        scan(R(mn), R("RST"), pb(KZ[a], 0, 128), 0.0, A.add, A.min)
        scan(REV(pb(KZ[a], 128, 256)), R("RST"), REV(pb(KZ[a], 0, 128)), 0.0, A.add, A.min)
        tt(R(Un, uo + 2, uo + 130), R(mn), pb(KZ[a], 128, 256), A.is_le)
        z = pb(KZ[a], 128, 128 + n)
        mm([(z, R("Ib"), R("LS", ls, ls + n)), (z, R(Un, uo + 2, uo + 130), R("I8", 0, n)), (z, R(Un, uo + 1, uo + 129), R("I8n", 0, n))])
        ts(R("C", cc, cc + n), z, SCL, -2048.0, A.add, A.max)

    def pairs(nb, bank, EQ, eqop):
        res, o = [], 0
        for c in range(nb):
            w = 16 * (nb - c)
            eqop(R(EQ, o, o + w), c)
            lst = [(pb(bank, 16 * c, 16 * c + 16), R("POW"), R(EQ, o, o + 16))]
            if w > 16:
                lst.append((pb(bank, 16 * c + 16, 16 * nb), R("BL4"), R(EQ, o + 16, o + w)))
            o += w
            if nb == 16:
                mm(lst, st=False, sp=False)
            else:
                res += lst
        return res

    W16 = lambda name, i, m=1: R(name, 16 * i, 16 * (i + m))
    N8 = lambda name, i, a: R(name, 16 * i + 8 * a, 16 * i + 8 * a + 8)
    EP = {1: 0, 2: 1, 0: 2}
    LP = {0: 0, 1: 1, 3: 2, 2: 3}
    NEW = lambda name, i, a: R(name, 512 * a + 128 * LP[i], 512 * a + 128 * LP[i] + 128)
    U = lambda a, i, k: R("Ub" if a else "Ua", 130 * (i - 1) + k, 130 * (i - 1) + k + 128)
    W256 = lambda name, i: R(name, 256 * i, 256 * i + 256)
    HB = lambda name, i, a: R(name, 256 * i + 128 * a, 256 * i + 128 * a + 128)

    def unwrap(i, a):
        scan(HB("SCN", 0, a), R("PW"), HB("JB", i - 1, a), 0.0, A.add, A.min)
        ts(N8("hu", i, a), R("SCN", 128 * a + 15, 128 * a + 128, 16), FW, None, A.add)
        if a:
            ts(W16("hp", i), R("SCN", 15, 256, 16), FW, None, A.add)

    def keep(t, i, a):
        o = pb(P1, 128 * a, 128 * a + 128)
        if i == 0:
            mm([(o, R("Dt", 128 * t, 128 * t + 128), HB("LS", 0, a)), (o, R("BT", 128 * t, 128 * t + 128), HB("C", 0, a))])
            act(NEW("NEW", 0, a), o, F.Identity, col(12 + t))
        else:
            mm([(o, R("Ib"), HB("LS", i, a)), (o, R("In"), HB("C", i - 1, a))])
            act(NEW("NEW", i, a), o)

    def comes(t, i, a):
        q = pb(P0, 128 * a, 128 * a + 128)
        lst = [(q, U(a, i, 2), R("I8")), (q, U(a, i, 1), R("I8n"))]
        if i == 3:
            lst.append((q, R("LT", 128 * t, 128 * t + 128), HB("LS", 0, a)))
        else:
            lst += w2b(P0, 128 * a, 128 * a + 128, N8("val", 1, a))
        mm(lst)
        act(NEW("PR", i, a), q, F.Relu, SC2)

    sent, granted = [], []
    for t in range(RO):
        need = R("need", t, t + 1)
        h0 = W16("hou", t)
        hw1 = R("HLi") if t == 0 else HW
        x0t = lambda lo, hi: R("DM", 544 * t + lo, 544 * t + hi)
        dmt = lambda lo, hi: x0t(272 + lo, 272 + hi)
        dst, src = T.cores[(rank + 1 + t % (N - 1)) % N], T.cores[(rank - 1 - t % (N - 1)) % N]
        T1, T2, T3 = (lambda k, m=1: W16("t1", k, m)), (lambda k: W16("t2", k)), (lambda k, m=1: W16("t3", k, m))
        p1, p2 = W16("pB", 0), W16("pB", 1)
        tag[0] = "first"
        ts(R("LS", 0, 256), IND(hw1, h0), -2048.0, None, A.add)
        mm(b2w(pb(GK, 32, 48), "LS", 0, 256, "Zt", 144 * t))
        ts(W16("eu", 0), pb(GK, 32, 48), 2048.0, None, A.add)
        for a in range(2):
            ts(HB("JB", 0, a), IND(WW, N8("eu", 0, a)), RND, -2.0 ** 23, A.add, A.add)
            ops[-1]["soft"] = granted[-1:]
            unwrap(1, a)
        for a in range(2):
            tag[0] = "x0" + "ab"[a]
            cp(x0t(128 * a, 128 * a + 128), IND(XW, N8("eu", 0, a)))
            mm([(pb(XP, 64 * a, 64 * a + 64), R("Ib"), x0t(128 * a, 128 * a + 64))] +
               [(pb(XP, 192 + 128 * a + q, 320 + 128 * a, 2), R("Ib"), x0t(128 * a + 64, 128 * a + 128)) for q in range(2)], each=True)
        tag[0] = "misc"
        swap(R("IN0", 544 * t, 544 * t + 544), x0t(0, 544), dst, src, "a0_%d" % t)
        ts(W16("ef", EP[0]), W16("eu", 0), -2048.0, None, A.add)
        cp(W16("hp", 0), W16("hoi", t))
        mm([(pb(P1, 256, 512), R("LT", 128 * t, 128 * t + 128), R("LS", 0, 256))])
        act(R("E0", 0, 256), pb(P1, 256, 512), F.Identity, 2048.0)
        ts(R("NP"), R("PP"), need, 1.0, A.subtract, A.add)
        ts(N4, need, 4096.0, None, A.mult)
        tag[0] = "mark0" if t else "mark00"
        if t:
            act(R("CODE"), R("CODE"), scale=2.0 ** 40)
            ops[-1]["soft"] = sent[-1:]
        act(IND(R("VT"), h0), R("CODE"), F.Silu)
        ops[-1]["cost"] += 0 if t else 1560
        for i in range(1, 4):
            tag[0] = "die%d" % i
            act(R("VB"), IND(R("VT", 0, H), W16("hu", i)), scale=2.0 ** (-40 * t - 11))
            hs, hc = ("hp", 16) if i == 1 else ("hs", 0)
            if i > 1:
                tt(R("hs"), W16("hp", i), W16("nup", i - 2), A.add)
            mm([(pb(ACC, 0, 256), R("Ib"), R("THn"))] + (w2b(ACC, 0, 256, W16("nup", 1)) if i == 3 else []), sp=False)
            pairs(16, ACC, "EQ", lambda o, c, i=i, hs=hs, hc=hc: ts(
                o, R("JB", 256 * i - 256 + 16 * c, 256 * i), R(hs, hc + c, hc + c + 1), None, A.is_equal))
            mm([(pb(ACC, 0, 256), R("I8"), R("VB"))], st=False)
            act(R("DB"), pb(ACC, 0, 256), F.Relu, 0.0, 2.0 ** 38)
            dW = pb(DK, 0, 16)
            mm(b2w(dW, "DB", 0, 256))
            if i < 3:
                tt(T1(0), R(hs, hc, hc + 16), dW, A.add)
                tag[0] = "mark%d" % i
                tt(T1(1), T1(0), R("DV"), A.min)
                cp(R("vo"), T1(1))
                act(IND(R("VT"), R("vo")), R("CODE"), F.Silu)
                tag[0] = "up%d" % i
                ts(W16("dB", i - 1), T1(0), 2000.0, 8192.0, A.is_ge, A.mult)
            else:
                d3 = W16("dB", 2)
                ts(d3, dW, 1.0, 8192.0, A.is_ge, A.mult)
                ts(R("NN"), d3, -8.0, N4, A.mult, A.add)
                tag[0] = "where"
                tt(T2(3), d3, p2, A.subtract)
                tt(T2(4), T2(3), p1, A.subtract)
                for k, nq in ((0, T2(4)), (1, T2(4)), (2, T2(3)), (3, d3)):
                    tt(W16("bs", k), W16("hp", k), nq, A.add)
                tt(R("hD"), R("bs"), R("DL"), A.min)
            for a in range(2):
                lo = 128 * a
                tag[0] = "climb%d%s" % (i, "ab"[a])
                nearest(a, 128, N8("hu", i, a), hw1 if i == 1 else HW, lo, 256 * i + lo, 256 * i - 256 + lo, 64 * a,
                        PAR["SPS"] if (i, a) == (1, 0) else 0, 130 * (i - 1))
                eu, ew = N8("eu", i, a), pb(KZ[a], 256, 264)
                mm(b2w(ew, "C", 256 * i - 256 + lo, 256 * i - 128 + lo))
                ts(eu, ew, EOFF, None, A.add)
                if i < 3:
                    ts(HB("JB", i, a), IND(WW, eu), RND, -2.0 ** 23, A.add, A.add)
                    unwrap(i + 1, a)
                    tag[0] = "new0"
                    if i == 1:
                        keep(t, 0, a)
                    keep(t, i, a)
                    continue
                tag[0] = "fail" + "ab"[a]
                ge = HB("GE", 2, a)
                tt(ge, IND(XW, eu), dmt(lo, lo + 128), A.is_ge)
                act(HB("H4", 0, a), IND(WW, eu), F.Identity, -4096.0)
                scan(HB("SCN", 0, a), R("PW"), HB("H4", 0, a), 0.0, A.add, A.min)
                ts(R("ixu", 24 * t + 8 + 8 * a, 24 * t + 16 + 8 * a), R("SCN", lo + 15, lo + 128, 16), FW, None, A.add)
                sc = pb(DK, 256 + lo, 384 + lo)
                mm([(sc, R("BL4"), HB("DB", 0, a)), (sc, R("BLb"), ge)])
                ts(HB("FB", 0, a), sc, need, 2.0, A.is_lt, A.mult)
                scan(HB("PF", 0, a), R("ONEb"), HB("FB", 0, a), R("PF", 127, 128) if a else 0.0, A.mult, A.add)
                for c in range(4):
                    act(R("junk", 512 * a + 128 * c, 512 * a + 128 * c + 128), HB("PF", 0, a), F.Sign,
                        R("DX", 8 + c, 9 + c), -1.0, R("sa", 4 * a + c, 4 * a + c + 1))
                    if a:
                        ts(R("ixu", 24 * t + c, 24 * t + c + 1), R("sa", 4 + c, 5 + c), R("sa", 8 + c, 9 + c), 0.5, A.add, A.mult)
                if a == 0:
                    ts(R("sa", 8, 12), R("sa", 0, 4), 256.0, None, A.add)
                tag[0] = "pay" + "ab"[a]
                cn = pb(GK, 16 + 8 * a, 24 + 8 * a)
                mm([(cn, R("Ib"), N8("NN", 0, a))] + b2w(cn, "GE", 512 + lo, 640 + lo, "Zn"))
                tt(N8("t2", 8, a), ew, N8("t2", 6, a), A.subtract)
                tt(N8("val", 1, a), N8("t2", 8, a), N8("t2", 5, a), A.max)
                keep(t, 3, a)
                comes(t, 3, a)
                comes(t, 2, a)
                ts(N8("t2", 7, a), cn, 0.0, float(H), A.max, A.min)
                for k in range(4):
                    tt(R("lof", 32 * a + 8 * LP[k], 32 * a + 8 * LP[k] + 8), N8("t2", 7, a), N8("hD", k, a), A.add)
                cp(R("lo", 32 * a, 32 * a + 32), R("lof", 32 * a, 32 * a + 32))
            if i == 3:
                for a in range(2):
                    tag[0] = "list" + "ab"[a]
                    for u, v in zip(PAR["HG"][a], PAR["HG"][a][1:]):
                        tt(IND(R("HL"), R("lo", 32 * a + 8 * u, 32 * a + 8 * v)), R("NEW", 512 * a + 128 * u, 512 * a + 128 * v),
                           R("PR", 512 * a + 128 * u, 512 * a + 128 * v), A.add)
                break
            tag[0] = "up%d" % i
            tt(W256("GE", i - 1), IND(XW, W16("eu", i)), dmt(0, 256), A.is_ge)
            mm(b2w(pb(GK, 0, 16), "GE", 256 * i - 256, 256 * i))
            ts(T1(2), pb(GK, 0, 16), need, 8192.0, A.is_ge, A.mult)
            tt(W16("nup", i - 1), T1(2), W16("dB", i - 1), A.max)
            tt(W16("pB", i - 1), W16("nup", i - 1), W16("dB", i - 1), A.subtract)
            tag[0] = "new1"
            ts(W16("ef", EP[i]), W16("eu", i), -2048.0, None, A.add)
            if i == 2:
                ts(T2(0), W16("ef", EP[0]), -8192.0, None, A.add)
                tt(T2(1), T2(0), p1, A.add)
                tt(T2(2), W16("ef", EP[2]), p1, A.subtract)
                tt(W16("val", 0), T2(1), T2(2), A.max)
                mm([(pb(P0, 256, 512), R("Ib"), R("th", 0, 256))] + w2b(P0, 256, 512, W16("val", 0)) +
                   [(pb(P0, 256 + 128 * a, 384 + 128 * a), U(a, 1, k), R(w)) for a in range(2) for k, w in ((2, "I8"), (1, "I8n"))])
                for a in range(2):
                    act(NEW("PR", 1, a), pb(P0, 256 + 128 * a, 384 + 128 * a), F.Relu, SC2)
                tt(T2(5), T2(0), p2, A.add)
                ts(T2(6), p2, 2048.0 - EOFF, None, A.add)
        tag[0] = "send"
        ix = R("ixu", 24 * t, 24 * t + 4)
        swap(R("INI", 24 * t, 24 * t + 24), R("ixu", 24 * t, 24 * t + 24), dst, src, "a1_%d" % t)
        sent.append(len(ops) - 2)
        tag[0] = "yl"
        if t == RO - 1:
            dma("Y", "dyl", T.yl[:], T.HL[:, 0:H], [], [HW], 768)
        tag[0] = "own"
        x4 = lambda k: R("xs4", 4 * k, 4 * k + 4)
        cp(R("x0s"), IND(x0t(0, 257), ix))
        cp(R("e0c", 0, 64), IND(R("E0", 0, 257), ix))
        scan(R("e0c", 64, 128), R("PX"), R("e0c", 0, 64), 0.0, A.add, A.min)
        tt(x4(0), R("e0c", 79, 128, 16), R("DX", 4, 8), A.min)
        ts(R("e0u"), x4(0), FX, None, A.add)
        ts(x4(5), R("e0u"), -EOFF, None, A.add)
        tag[0] = "warr"
        for a in range(2):
            ts(N8("t3", 1, a), R("lof", 32 * a + 16, 32 * a + 24), H - 0.5, 8192.0, A.is_ge, A.mult)
        tt(T3(0), T3(1), p2, A.subtract)
        tt(T3(2), T3(0), p1, A.subtract)
        tt(T3(3, 3), T3(0, 3), R("ef"), A.add)
        tt(T3(6, 3), T3(3, 3), R("DW"), A.min)
        ts(R("wo"), T3(6, 3), 2048.0, None, A.add)
        tag[0] = "hm"
        tt(T1(3), W16("hp", 1), W16("hp", 2), A.subtract)
        tt(T1(4), W16("hp", 2), W16("hp", 3), A.subtract)
        tt(T1(5, 2), T1(3, 2), T3(0, 2), A.mult)
        tt(T1(7), T1(5), T1(6), A.add)
        ts(W16("val", 2), T1(7), 2.0 ** -13, None, A.mult)
        o = pb(P1, 256, 512)
        mm([(o, R("Ib"), W256("JB", 2))] + w2b(P1, 256, 512, W16("val", 2)))
        act(W256("HM", 2), o, F.Identity, 4096.0)
        tag[0] = "hj"
        for k in range(2):
            o = pb(P0, 256 * k, 256 * k + 256)
            mm([(o, R("Ib"), W256("JB", k))])
            act(W256("HM", k), o, F.Identity, 4096.0)
        tag[0] = "warr"
        act(IND(R("WT"), R("wo")), R("HM"), F.Silu)
        tag[0] = "odd"
        if t == RO - 1:
            dma("Y", "dw2", T.E0[:, 0:256], T.WT[0:128:16, 0:P], [R("E0", 0, 256)], [WW], 256)
            ts(R("H4"), R("E0", 0, 256), RND, -2.0 ** 23, A.add, A.add)
            dma("Y", "dyw", T.yw[:], T.H4[:], [], [R("H4")], 256)
        else:
            act(R("junk", 1024, 1040), T3(2), F.Sign, -0.5, 1.0, col(15))
            mm([(pb(GK, 48, 49), R("ONE"), col(15))])
            ts(R("ni", 0, 1), pb(GK, 48, 49), -0.5, 1024.0, A.mult, A.add)
            ts(R("ni", 1, 2), R("ni", 0, 1), 1, None, A.bitwise_and)
            ts(R("need", t + 1, t + 2), R("ni", 1, 2), 9.0, None, A.add)
        tag[0] = "come"
        cp(R("LA", 0, 128), IND(HW, R("INI", 24 * t + 8, 24 * t + 16)))
        act(R("LA", 128, 256), IND(HW, R("INI", 24 * t + 16, 24 * t + 24)))
        xin, din, ii = R("xin", 0, 64), R("xin", 64, 128), R("INI", 24 * t, 24 * t + 4)
        act(xin, IND(R("IN0", 544 * t, 544 * t + 257), ii))
        mm([(pb(XP, 128, 192), R("Ib"), xin)])
        nearest(0, 64, ii, R("LA", 0, 257), 256, 1024, 768, 128, PAR["SPL"], 390)
        act(din, IND(R("IN0", 544 * t + 272, 544 * t + 529), ii))
        ops[-1]["soft"] = gat[-1:]
        fy, fb, cy, cb = pb(KZ[0], 256, 260), pb(KZ[0], 320, 384), pb(KZ[0], 384, 448), pb(KZ[0], 448, 512)
        mm(b2w(fy, "C", 768, 832))
        mm([(fb, R("BLb"), R("C", 768, 832))])
        fu, fw = R("fu"), R("FS", 0, 4)
        ts(fu, fy, EOFF, None, A.add)
        cp(fw, fy)
        tt(R("xg"), IND(XW, fu), din, A.is_ge)
        tt(R("xd"), IND(XW, fu), xin, A.subtract)
        for c in range(4):
            ts(R("EX", 160 + 64 * c, 224 + 64 * c), fb, R("xs4", 20 + c, 21 + c), None, A.is_equal)
        acc = pb(KZ[1], 0, 64)
        mm([(acc, R("Ib"), R("THn", 0, 64))] + [(acc, R("BL4"), R("EX", 160 + 64 * c, 224 + 64 * c)) for c in range(4)], sp=False)
        mm([(cy, R("Ib"), R("NP")), (cy, R("BLb"), R("xg"))])
        mm([(cb, R("BLb"), R("xg"))])
        scan(R("FS", 64, 128), R("R01"), cy, 0.0, A.mult, A.max)
        ts(R("nb"), cb, need, None, A.is_lt)
        mm([(acc, R("BL4"), R("nb"))], st=False, sp=False)
        mm(pairs(4, KZ[1], "EX", lambda o, c: ts(o, pb(KZ[0], 320 + 16 * c, 384), R("FS", c, c + 1), R("FS", 79 + 16 * c, 80 + 16 * c),
                                                 A.is_equal, A.min)), st=False)
        ts(pb(KZ[1], 64, 128), acc, 0.0, None, A.is_lt)
        granted.append(len(ops) - 1)
        o2 = 64 * t
        tt(R("OUT2", o2, o2 + 64), R("xd"), pb(KZ[1], 64, 128), A.mult)
        ts(R("xq"), acc, 0.0, None, A.is_lt)
        swap(R("IN2", o2, o2 + 64), R("OUT2", o2, o2 + 64), src, dst, "a2_%d" % t)
        tag[0] = "take"
        mm(b2w(pb(DK, 16, 20), "xq", 0, 64))
        ts(x4(1), pb(DK, 16, 20), -512.0, 8192.0 + EOFF, A.mult, A.add)
        tt(x4(2), x4(1), fw, A.add)
        tt(x4(3), x4(2), R("DX", 0, 4), A.min)
        cp(R("xo"), x4(3))
        cp(IND(R("X"), R("xo")), xin)
        tag[0] = "back"
        tt(IND(R("X"), R("e0u")), R("x0s"), R("IN2", o2, o2 + 64), A.add)
    dma("S", "dyx", T.yx[:], T.X[:, 0:P], [], [XW], 1024)

    emit(g, T, ops)


def plan(ops, deps, succ, pr, delay):
    n, hop = len(ops), PAR["HOP"]
    left = [len(d) for d in deps]
    ready = sorted((-pr[k], k) for k in range(n) if left[k] == 0)
    rt, sta, fin, busy, end = [0.0] * n, [0.0] * n, [0.0] * n, {}, 0.0

    def place(lst, x):
        lo, hi = 0, len(lst)
        while lo < hi:
            m = (lo + hi) // 2
            if lst[m] < x:
                lo = m + 1
            else:
                hi = m
        return lo

    while ready:
        k = ready.pop(0)[1]
        e, c, t = ops[k]["eng"], ops[k]["cost"], rt[k]
        moved = c > 0
        while moved:
            moved = False
            for r in [e] + ops[k]["banks"]:
                lst = busy.setdefault(r, [])
                i = max(0, place(lst, (t,)) - (1 if r == e else 6))
                while i < len(lst) and lst[i][0] < t + c + hop:
                    s, f, e2 = lst[i]
                    gap = 0.0 if r == e else hop
                    if (r == e or e2 != e) and s < t + c + gap - 1e-6 and t < f + gap - 1e-6:
                        t, moved = f + gap, True
                    i += 1
        sta[k], fin[k] = t, t + c
        if c > 0:
            for r in [e] + ops[k]["banks"]:
                busy[r].insert(place(busy[r], (t,)), (t, t + c, e))
        end = max(end, t + c + ops[k].get("lat", 0))
        for j in succ[k]:
            rt[j] = max(rt[j], t + c + delay(k, j))
            left[j] -= 1
            if left[j] == 0:
                ready.insert(place(ready, (-pr[j], j)), (-pr[j], j))
    return end, sta, fin


def emit(g, T, ops):
    n = len(ops)
    for o in ops:
        o["banks"] = sorted(set(name for name, lo, hi in o["rd"] + o["wr"] if name.startswith("pb")))
    if "graph" not in PLAN:
        seen, deps, soft = {}, [], []
        for k, o in enumerate(ops):
            d = set()
            for w, rgs in ((0, o["rd"]), (1, o["wr"])):
                for name, lo, hi in rgs:
                    for k2, w2, lo2, hi2 in seen.get(name, []):
                        if (w or w2) and lo < hi2 and lo2 < hi:
                            d.add(k2)
            if "after" in o:
                d.add(o["after"])
            for w, rgs in ((0, o["rd"]), (1, o["wr"])):
                for name, lo, hi in set(rgs):
                    seen.setdefault(name, []).append((k, w, lo, hi))
            deps.append(sorted(d))
            soft.append(set(o.get("soft", [])) - d)
        anc, red = [], []
        for k in range(n):
            m, keep = 0, []
            for j in sorted(deps[k] + list(soft[k]), reverse=True):
                if not m >> j & 1:
                    keep.append(j)
                m |= anc[j] | 1 << j
            anc.append(m)
            red.append(keep)
        succ = [[] for _ in ops]
        for k in range(n):
            for j in red[k]:
                succ[j].append(k)
        PLAN["graph"] = deps, red, succ, soft
    if "order" not in PLAN:
        deps, red, succ, soft = PLAN["graph"]
        fwd = lambda k, j: ops[k].get("lat", 0) + (0 if ops[k]["eng"] == ops[j]["eng"] == "PE" or k in soft[j]
                                                   else PAR["HV" if ops[k]["eng"] == "V" else "HOP"])
        bwd = lambda k, j: fwd(j, k)
        pr0, est = [0.0] * n, [0.0] * n
        for k in range(n - 1, -1, -1):
            pr0[k] = ops[k]["cost"] + max([pr0[j] + fwd(k, j) for j in succ[k]] + [ops[k].get("lat", 0)])
        for k in range(n):
            est[k] = max([est[j] + ops[j]["cost"] + fwd(j, k) for j in red[k]] + [0.0])
        best, tot = None, max(pr0)
        for lam in PAR["LAM"]:
            pr = [(1 - lam) * pr0[k] + lam * (tot - est[k]) for k in range(n)]
            for it in range(PAR["IT"]):
                res = plan(ops, red, succ, [max(pr[k] + PAR["URG"].get(ops[k]["tag"], 0), ops[k].get("pri", 0)) for k in range(n)], fwd)
                if best is None or res[0] < best[0]:
                    best = res
                if it + 1 < PAR["IT"]:
                    back = plan(ops, succ, red, res[2], bwd)
                    pr = [(1 - PAR["MIX"]) * back[2][k] + PAR["MIX"] * (res[0] - res[1][k]) for k in range(n)]
        PLAN["order"], PLAN["deps"], PLAN["end"] = sorted(range(n), key=lambda k: (best[1][k], k)), deps, best[0]
    Q = {"V": g.vector, "S": g.scalar, "PE": g.tensor, "G": g, "Y": g.sync}
    cnt, mark, known, sent, bank = {}, {}, {}, 0, {}
    for k in PLAN["order"]:
        o = ops[k]
        e = o["eng"]
        if e == "N":
            mark[k] = (o["sem"], o["val"])
            continue
        want = {}
        others = [j for b in o["banks"] for e2, j in bank.get(b, {}).items() if e2 != e]
        for j in PLAN["deps"][k] + others:
            if j not in mark or (e == "PE" and ops[j]["eng"] == "PE"):
                continue
            s, v = mark[j]
            want[s] = max(want.get(s, 0), v)
        for s, v in want.items():
            if known.get((e, s), 0) < v:
                Q[e].wait_ge(T.sem[s], v)
                known[(e, s)] = v
        ins = o["fn"]()
        for b in o["banks"]:
            bank.setdefault(b, {})[e] = k
        if "remote" in o:
            sent += o["remote"]
        elif "sem" in o:
            ins.then_inc(T.sem[o["sem"]], 16)
            mark[k] = (o["sem"], 16)
        else:
            cnt[e] = cnt.get(e, 0) + 1
            ins.then_inc(T.sem[e], 1)
            mark[k] = (e, cnt[e])
    for e in ("V", "S", "PE", "G"):
        g.sync.wait_ge(T.sem[e], cnt[e])
    g.sync.wait_ge(T.sem.sent, sent)
    for s in DMAS:
        g.sync.wait_ge(T.sem[s], 16)
